import numpy as np, ml_dtypes
CORES = [5,29,101,125,133,157,229,253]
N = 8
BF = ml_dtypes.bfloat16
V, L, RO, HP, S, ST = 1760, 256, 3, 2, 4, 97
def parts(rng):
    cen = rng.integers(0, 255, (1, 8, 16, 24)); k = rng.integers(0, 24, (N, 8, 1, V)); size = rng.choice(np.array([3, 12, 40, 90]), (N, 8, 1, V))
    x = np.take_along_axis(cen, k, 3) + np.floor((2 * size + 1) * rng.random((N, 8, 16, V))).astype(np.int64) - size
    x = np.minimum(np.maximum(x, 0), 254)
    hub = np.argsort(rng.random((N, 8, 1, V)), axis=3); u = rng.random((N, 8, 16, V))
    c = np.take_along_axis(hub, np.minimum((V * u * u).astype(np.int64), V - 1), 3)
    c = np.where(rng.random((N, 8, 1, V)) < 0.06, c[:, :, :1], c)
    w = rng.integers(0, V, (N, 8, 16, L)); u = rng.random((N, 8, L)); n = 2 * np.minimum((8 * u * u).astype(np.int64), 7) + 1
    t = rng.integers(0, 1600, (N, 8, L))
    return x, c, w, n, t
def trap(rng, d, T, f):
    x, c, w, n, t = d
    o = np.argsort(rng.random((N, 8, V)), axis=2); z = np.argsort(rng.random((N, 8, L)), axis=2)
    if len(f):
        for r in range(N):
            for g in range(8):
                u = o[r, g].copy(); o[r, g] = np.concatenate([np.array(f), u[~np.isin(u, np.array(f))]])
    for r in range(N):
        q = (r + S) % N; b = (r - S) % N
        for g in range(8):
            tv = o[r, g, :T]; tw = o[q, g, T:2 * T]; h = o[b, g, 2 * T:3 * T]; la = z[r, g, :T]; lb = z[b, g, T:2 * T]
            c[r, g][:, tv] = tw; c[q, g][:, tw] = tv
            w[r, g][0, la] = tv; n[r, g][la] = 1
            x[b, g][:, h] = x[r, g][:, tv]
            w[b, g][0, lb] = h; w[b, g][1, lb] = tv; n[b, g][lb] = 3; t[b, g][lb] = np.maximum(t[b, g][lb], 1)
def pack(d):
    x, c, w, n, t = d
    return {"pts": np.ascontiguousarray(x.reshape(N, 128, V)).astype(np.float32).astype(BF), "cand": np.ascontiguousarray(c.reshape(N, 128, V)).astype(np.int32),
            "way": np.ascontiguousarray(w.reshape(N, 128, L)).astype(np.int32), "cnt": np.ascontiguousarray(n).astype(np.int32), "th": np.ascontiguousarray(t).astype(np.int32)}
def setup_inputs(rng):
    d = parts(rng); trap(rng, d, 12, [])
    return pack(d)
def setup_inputs_spread(rng):
    x, c, w, n, t = parts(rng)
    x = np.minimum((np.exp2(8 * rng.random((N, 8, 1, V))) * rng.random((N, 8, 16, V))).astype(np.int64), 254)
    hub = np.argsort(rng.random((N, 8, 1, V)), axis=3)
    c = np.take_along_axis(hub, np.minimum((V * rng.random((N, 8, 16, V)) ** 6).astype(np.int64), V - 1), 3)
    hub = np.argsort(rng.random((N, 8, 1, V)), axis=3)
    w = np.take_along_axis(hub, np.minimum((V * rng.random((N, 8, 16, L)) ** 3).astype(np.int64), V - 1), 3)
    n = 2 * rng.integers(0, 8, (N, 8, L)) + 1; t = np.minimum(np.exp2(12 * rng.random((N, 8, L))).astype(np.int64) - 1, 4095)
    d = (x, c, w, n, t); trap(rng, d, 12, [])
    return pack(d)
def setup_inputs_ends(rng):
    cls = rng.integers(0, 5, (N, 8, 1, V)); cls[..., 0] = 0; cls[..., V - 1] = 1
    x = 254 * np.where(cls == 0, 0, np.where(cls == 1, 1, rng.integers(0, 2, (N, 8, 16, V))))
    c = np.where(rng.random((N, 8, 16, V)) < 0.7, (V - 1) * rng.integers(0, 2, (N, 8, 16, V)), rng.integers(0, V, (N, 8, 16, V)))
    w = np.where(rng.random((N, 8, 1, L)) < 0.25, rng.integers(0, V, (N, 8, 16, L)), (V - 1) * rng.integers(0, 2, (N, 8, 16, L)))
    n = 1 + 14 * rng.integers(0, 2, (N, 8, L)); t = 4095 * rng.integers(0, 2, (N, 8, L))
    for r in range(N):
        q = (r + S) % N
        for g in range(8):
            lo = rng.permutation(np.flatnonzero(cls[r, g, 0, 1:] == 0) + 1); up = rng.permutation(np.flatnonzero(cls[q, g, 0, :V - 1] == 1)); lq = rng.permutation(np.flatnonzero(cls[q, g, 0, 1:] == 0) + 1)
            uh = rng.permutation(np.flatnonzero(cls[r, g, 0, :V - 1] == 1))
            for m, l in enumerate((3, 8, L - 2, L - 1)):
                w[r, g][0::2, l] = lo[8 * m:8 * m + 8]; w[r, g][1::2, l] = up[8 * m:8 * m + 8]; n[r, g, l] = 15; t[r, g, l] = 4095
            for m, l in enumerate((5, L - 4, L - 3)):
                e = lo[32 + m]; col = np.concatenate([up[32:40], up[32:40]])
                if m > 0: col[15] = lq[0]
                if m > 1: col[6] = lq[1]
                c[r, g][:, e] = col; w[r, g][0, l] = e; n[r, g, l] = 1; t[r, g, l] = 4095
            for m, l in enumerate((6, L - 6, 11, L - 5)):
                e = lo[36 + m]; h = lo[40 + m]; f = up[44 + m]; z = lq[24 + m]
                w[r, g][0, l] = uh[m]; w[r, g][1, l] = z; w[r, g][2, l] = e; n[r, g, l] = 3; t[r, g, l] = 0
                if m < 2:
                    c[r, g][:15, e] = z; c[r, g][15, e] = f; c[q, g][:, f] = h
                else:
                    c[r, g][:, e] = f; c[q, g][:15, f] = uh[m]; c[q, g][15, f] = h
            if g % 2 == 0: c[r, g][:, V - 1] = lq[4:20]
            else:
                c[r, g][:15, V - 1] = V - 1; c[r, g][15, V - 1] = lq[4]
    return pack((x, c, w, n, t))
def setup_inputs_corners(rng):
    d = parts(rng); x, c, w, n, t = d
    for r in range(N):
        for g in range(8):
            k = (g + r) % 8
            if k == 0: w[r, g] = w[r, g][:1].copy(); n[r, g] = 15
            if k == 1: w[r, g] = (V - 1) * rng.integers(0, 2, (16, L)); n[r, g] = 1
            if k == 2: n[r, g] = 13 + 2 * rng.integers(0, 2, L)
            if k == 3: c[r, g] = np.arange(V)[None, :]
            if k == 4: c[r, g] = c[r, g][:1].copy()
            if k == 5: w[r, g] = rng.choice(np.array([0, V // 2, V - 1]), (16, L))
            if k == 6: n[r, g] = 1 + 14 * rng.integers(0, 2, L); t[r, g] = 0
            if k < 6: t[r, g] = 4095 * rng.integers(0, 2, L)
    trap(rng, d, 12, [V - 1, V - ST, V - ST - 1, 0])
    o = np.argsort(rng.random((N, 8, V)), axis=2)
    for r in (0, 1):
        q = (r + S) % N
        for g in range(8):
            w[r, g][0] = o[r, g, :L]; w[r, g][1] = o[q, g, L:2 * L]; w[r, g][2] = o[r, g, 2 * L:3 * L]; n[r, g] = 3; t[r, g] = 4095
    q = S % N
    for g in range(8):
        x[0, g][:, o[0, g, :L]] = x[q, g][:, o[q, g, L:2 * L]]
        e = o[0, g, 2 * L:3 * L:2]; f = o[q, g, 2 * L:3 * L:2]; v = x[q, g][:, f].copy(); s = rng.integers(6, 41, len(e))
        v[0] = np.where(v[0] < 200, v[0] + s, v[0] - s)
        x[0, g][:, e] = v; c[0, g][:, e] = f[None, :]
    t[0] = rng.choice(np.array([1, 2, 5, 4095]), (8, L))
    M = int(rng.choice(np.array([31, 63, 95]))); pk = rng.permutation(8 * L)[:M]; pick = np.zeros(8 * L, np.int64); pick[pk] = 4095
    t[1] = pick.reshape(8, L); q = (1 + S) % N
    for u in pk[:16]:
        g = int(u) // L; l = int(u) % L
        c[1, g][:, o[1, g, 2 * L + l]] = o[q, g, L + l]
    return pack(d)
def setup_inputs_crowd(rng):
    d = parts(rng); x, c, w, n, t = d
    n[...] = np.maximum(n, 3); t[...] = np.maximum(t, 1); o = np.argsort(rng.random((N, 8, V)), axis=2)
    far = rng.permutation(V); rest = far[(RO + 1) * L:]; z = int(rng.integers(0, N))
    c[:, 7] = rest[c[:, 7] % len(rest)]; w[:, 7] = rest[w[:, 7] % len(rest)]
    for r in range(N): o[r, 7, :len(rest)] = rng.permutation(rest)
    for g in range(8):
        s = rng.integers(0, 255, (16, 1))
        for r in range(N):
            q = (r + S) % N; a = o[r, g, :L]; b = o[q, g, L:2 * L]
            if g == 6:
                c[r, g] = rng.permutation(V)[:16][:, None]; continue
            x[r, g][:, a] = s; x[q, g][:, b] = s
            aa = a.copy(); bb = b.copy()
            if g in (0, 1, 2, 5): aa[:] = a[0]
            if g in (0, 1, 3, 5): bb[:] = b[0]
            if g == 1:
                u = int(rng.integers(0, L)); aa[u] = a[1]; bb[u] = b[1]
            if g == 4: aa = a[rng.integers(0, 3, L)]; bb = b[rng.integers(0, 3, L)]
            if g == 5: t[r, g, 0] = 0
            if g == 7: aa[L - 1] = a[0]
            w[r, g][0] = aa; w[r, g][1] = bb
    q = (z + S) % N; hs = far[:(RO + 1) * L].reshape(RO + 1, L); bs = rng.permutation(far[:RO * L]).reshape(RO, L)
    for m in range(RO):
        x[z, 7][:, hs[m]] = x[q, 7][:, bs[m]]; w[z, 7][2 * m] = hs[m]; w[z, 7][2 * m + 1] = bs[m]
    w[z, 7][2 * RO] = hs[RO]; n[z, 7] = 2 * RO + 1
    return pack(d)
def setup_inputs_ties(rng):
    d = parts(rng); x, c, w, n, t = d
    pat = 64 * rng.integers(0, 2, (1, 8, 16, 10)); x[...] = np.take_along_axis(pat, rng.integers(0, 10, (N, 8, 1, V)), 3)
    c[:, :, 8:] = c[:, :, :8].copy()
    t[...] = np.maximum(64 * rng.integers(0, 11, (N, 8, L)) + rng.integers(-1, 2, (N, 8, L)), 0)
    K = 24; o = np.argsort(rng.random((N, 8, V)), axis=2); z = np.argsort(rng.random((N, 8, L)), axis=2)
    for r in range(N):
        q = (r + S) % N
        for g in range(8):
            la = z[r, g, :K]; a = o[r, g, :K]; e = o[r, g, K:2 * K]; b = o[q, g, 2 * K:3 * K]
            s = rng.integers(1, 64, (1, K)); near = rng.integers(1, 8, K)
            v = np.floor(s * rng.random((16, K))).astype(np.int64); hi = 254 - np.floor(s * rng.random((16, K))).astype(np.int64)
            u = v.copy(); u[3] = u[3] + near
            x[r, g][:, a] = v; x[r, g][:, e] = u; x[q, g][:, b] = hi
            turn = rng.random(K) < 0.5
            w[r, g][0, la] = np.where(turn, e, a); w[r, g][1, la] = b; w[r, g][2, la] = np.where(turn, a, e); n[r, g][la] = 3
            t[r, g][la] = np.add.reduce(hi - v, axis=0) - near + rng.integers(-1, 2, K)
    trap(rng, d, 12, [])
    return pack(d)
def check_inputs(d):
    bad = []
    for k, lo, hi in (("pts", 0, 254), ("cand", 0, V - 1), ("way", 0, V - 1), ("cnt", 1, 15), ("th", 0, 4095)):
        a = np.asarray(d[k]).astype(np.float64)
        if not (np.min(a) >= lo and np.max(a) <= hi): bad.append("range of " + k)
    a = np.asarray(d["pts"]).astype(np.float64)
    if not np.all(a == np.floor(a)): bad.append("pts not whole")
    if np.any((np.asarray(d["cnt"]).astype(np.int64) & 1) != 1): bad.append("cnt not odd")
    return bad
def hop(e, xa, ca, xb, old, use):
    c = np.take_along_axis(ca, e[:, None, :], 2); xe = np.take_along_axis(xa, e[:, None, :], 2)
    xc = np.take_along_axis(xb, c.reshape(8, 1, 16 * L), 2).reshape(8, 16, 16, L)
    s = np.add.reduce(np.abs(xc - xe[:, :, None, :]), axis=1)
    on = np.any((c[:, :, None, :] == old[:, None]) & use[:, None], axis=2)
    ok = (xc[:, 0] != 255) & ~on
    i = np.argmin(np.where(ok, s, 9999), axis=1)
    return np.any(ok, axis=1), np.take_along_axis(c, i[:, None, :], 1)[:, 0]
def reference(pts, cand, way, cnt, th):
    x = pts.astype(np.float32).astype(np.int32).reshape(N, 8, 16, V); c = cand.astype(np.int64).reshape(N, 8, 16, V)
    w = way.astype(np.int64).reshape(N, 8, 16, L); n = cnt.astype(np.int64); t = th.astype(np.int64)
    rows = np.arange(16)[None, :, None]; low = np.arange(L)[:, None] > np.arange(L)[None, :]; A = [0] * N
    for rnd in range(RO):
        wins = []
        for r in range(N):
            q = (r + S) % N; p = w[r]; k = n[r]
            v = np.zeros((8, 16, 16, L), np.int32)
            v[:, :, 0::2] = np.take_along_axis(x[r], p[:, 0::2].reshape(8, 1, 8 * L), 2).reshape(8, 16, 8, L)
            v[:, :, 1::2] = np.take_along_axis(x[q], p[:, 1::2].reshape(8, 1, 8 * L), 2).reshape(8, 16, 8, L)
            dead = (v[:, 0] == 255) & (rows < k[:, None, :]); cut = np.any(dead, axis=1); j = np.argmax(dead, axis=1)
            pre = np.where((j & 1) == 1, j, np.maximum(j - 1, 0)); s = j + 2 - (j & 1); post = np.maximum(k - s, 0); first = pre >= post
            start = np.where(cut & ~first, s, 0); m = np.where(cut, np.where(first, pre, post), k); none = m == 0
            ix = np.minimum(rows + start[:, None, :], 15)
            p2 = np.take_along_axis(p, ix, 1); v = np.take_along_axis(v, ix[:, None], 2)
            new = p[:, 0] + ST; new = np.where(new >= V, new - V, new)
            p2[:, 0] = np.where(none, new, p2[:, 0]); m = np.where(none, 1, m)
            live = (v[:, 0] != 255) & (rows < m[:, None, :])
            d = np.add.reduce(np.abs(v[:, :, :15] - v[:, :, 1:]), axis=1)
            d = np.where(live[:, :15] & live[:, 1:], d, 9999)
            i = np.argmin(d, axis=1); least = np.min(d, axis=1); prop = least < t[r] + 8 * (A[r] & 31)
            a = np.take_along_axis(p2, (i + (i & 1))[:, None, :], 1)[:, 0]; b = np.take_along_axis(p2, (i + 1 - (i & 1))[:, None, :], 1)[:, 0]
            same = (a[:, :, None] == a[:, None, :]) | (b[:, :, None] == b[:, None, :])
            win = prop & ~np.any(same & low[None] & prop[:, None, :], axis=2)
            mid = (np.take_along_axis(x[r], a[:, None, :], 2) + np.take_along_axis(x[q], b[:, None, :], 2)) >> 1
            wins.append((win, a, b, mid)); w[r] = p2; n[r] = m
        for r in range(N):
            win, a, b, mid = wins[r]; A[r] = int(np.count_nonzero(win))
            for g in range(8): x[r, g][:, a[g][win[g]]] = mid[g][:, win[g]]
        for r in range(N):
            win, a, b, mid = wins[r]; q = (r + S) % N
            for g in range(8): x[q, g][:, b[g][win[g]]] = 255
        for r in range(N):
            q = (r + S) % N
            for h in range(HP):
                p = w[r]; k = n[r]; use = rows < k[:, None, :]
                e = np.take_along_axis(p, k[:, None, :] - 1, 1)[:, 0]
                f1, u1 = hop(e, x[r], c[r], x[q], p[:, 1::2], use[:, 1::2])
                f2, u2 = hop(u1, x[q], c[q], x[r], p[:, 0::2], use[:, 0::2])
                go = f1 & f2 & (k <= 13)
                p = np.where(go[:, None, :] & (rows == k[:, None, :]), u1[:, None, :], p)
                p = np.where(go[:, None, :] & (rows == k[:, None, :] + 1), u2[:, None, :], p)
                w[r] = p; n[r] = np.where(go, k + 2, k)
    w = np.where(np.arange(16)[None, None, :, None] < n[:, :, None, :], w, 0)
    return {"yx": x.reshape(N, 128, V).astype(np.float32).astype(BF), "yw": w.reshape(N, 128, L).astype(np.float32), "yn": n.astype(np.float32)}

@@ -1,0 +1,693 @@
+import numpy as np
+from concourse.mybir import AluOpType, AxisListType, ActivationFunctionType
+
+NV, NL, ROUNDS = 1760, 256, 3
+B17 = 131072.0
+BIGH, BIGP = 8192.0, -4096.0
+MAGIC = 12582912.0
+TURN_AT, BESIDE_AT, PATH_AT = 2, 2, 7
+CF_FROM_CU = True
+Y_FIRST = True
+RLAT = 2500.0
+PLAN_HOP, PLAN_APP, PLAN_FIRST, PLAN_CUT = "SSSVVVVV", "SSSSVVVV", "SSSVVVVV", "SSSSVVVV"
+EDGE_S = (0, 2, 5)
+SAMEQ = False
+GA, SC, PEC, LAT, SLACK = 1.5, 3.5, 0.42, 60.0, 120.0
+
+SLOTS = ["n", "nm1", "th16", "bound", "SB", "NE", "j", "nd0", "jp", "t1", "back", "mx", "H2", "S2", "C2", "mB", "none",
+         "dl", "dm", "as1", "bs1", "prop", "z1", "z2", "w1", "win", "e1", "g1", "fd", "fd2", "go", "go2", "de", "df", "hv", "fv", "f1", "h1",
+         "lt14", "TRL", "LT", "CF0", "CF1", "col", "OH0", "OH1", "OH2", "OH3", "OH4", "SC0", "SC1", "SC2", "SC3", "SC4",
+         "D0", "D1", "D2", "D3", "TD0", "TD1", "TD2", "TD3", "TR0", "TR1", "TR2", "TR3", "L0", "L1", "L2", "L3", "G8"]
+SL = {k: 16 * i for i, k in enumerate(SLOTS)}
+COLS = {"PM": 0, "PAR0": 1, "PAR1": 2, "GRP": 3, "NZ": 4, "PN0": 5, "PN1": 6, "ODD": 7, "ACT": 8, "A128": 9}
+
+F32, BF, F16, I32, U16 = "float32", "bfloat16", "float16", "int32", "uint16"
+SB = {
+    "X": ([4032], BF), "CH": ([NV], I32), "CP": ([NV], I32), "XO": ([NV], BF), "IOT": ([NV], F32),
+    "SM": ([16 * len(SLOTS)], F32), "SI": ([64], I32), "WI": ([512], I32), "WF": ([16, 2, 16], F32), "WL": ([512], F32),
+    "KM": ([128], F32), "KIO": ([256], F32), "TM1": ([512], F16), "P3": ([16, 16], F32), "CF": ([256], F16),
+    "ID": ([128], BF), "NI": ([128], BF), "BI": ([128], BF), "IH": ([128], F16), "ONES": ([128], BF),
+    "W16": ([144], BF), "W1": ([144], BF), "TRI": ([2048], BF), "ZM": ([512], F16), "DM": ([512], F16), "ZF": ([512], F32),
+    "KB": ([256], BF), "RSTB": ([256], F32), "K1": ([256], F32), "IO2": ([512], F32), "KC": ([256], F32),
+    "BCL": ([32], U16), "REP": ([8], U16), "APL": ([16], U16),
+    "P1": ([272], F32), "PU": ([256], U16), "VAL": ([256], F32), "INV": ([256], F32), "PEN": ([512], F32),
+    "RUN": ([256], F32), "NE1": ([256], F32), "DA": ([256], F32), "DB": ([256], F32), "UAB": ([512], F32),
+    "ABU": ([32], U16), "ROW": ([512], F16), "EQ": ([8704], BF), "ACCS": ([256], BF), "WINB": ([16], BF),
+    "XA": ([256], F32), "XS": ([256], F32), "XR": ([256], F32), "NEG": ([256], BF), "YS": ([1280], F16),
+    "VG": ([4096], BF), "A1": ([4096], BF), "A2": ([16, 16, 16], BF), "XB": ([4096], BF), "VW": ([1536], F32), "Y2": ([512], BF),
+    "EU": ([16], U16), "FU": ([16], U16), "CU": ([256], U16), "C16": ([8, 2, 16], F16), "N16": ([8, 2, 16], F16),
+    "DC": ([256], F32), "PO": ([16, 24], F32), "PEV": ([16, 28], F32), "EQH": ([1792], BF),
+    "UF": ([256], F32), "UE": ([256], F32), "MK": ([256], F32), "UP": ([256], F32),
+}
+for _r in range(ROUNDS):
+    SB["MID%d" % _r] = ([256], BF)
+    SB["RM%d" % _r] = ([512], BF)
+    SB["LU%d" % _r] = ([64], U16)
+    SB["RL%d" % _r] = ([32], U16)
+SCRATCH = {k: ("sbuf", [128] + v[0], v[1]) for k, v in SB.items()}
+SCRATCH["pZ"] = ("psum", [128, 16, 2, 16], F32)
+SCRATCH["pE"] = ("psum", [128, 512], F32)
+SCRATCH["pC"] = ("psum", [128, 512], F32)
+for _r in range(5):
+    SCRATCH["pD%d" % _r] = ("psum", [128, 32, 16], F32)
+SEMAPHORES = ["sV", "sS", "sP", "sG"] + ["d%d" % i for i in range(24)] + ["r%d" % i for i in range(12)]
+OP = AluOpType
+AF = ActivationFunctionType
+ALL = slice(None)
+ESEM = {"V": "sV", "S": "sS", "P": "sP", "G": "sG"}
+EXT = {}
+PLAN = {}
+
+
+def order_calls(ops):
+    n = len(ops)
+    acc = {}
+    hard = [set() for _ in ops]
+    soft = [set() for _ in ops]
+    for i, o in enumerate(ops):
+        hard[i] |= set(o["after"])
+        mine = [(nm, "rd", m) for nm, m in o["rd"]] + [(nm, o["wk"], m) for nm, m in o["wr"]]
+        for (nm, kind, m) in mine:
+            psum = nm[0] == "p"
+            for (j, k2, m2) in acc.get(nm, []):
+                oj = ops[j]
+                same = oj["q"] == o["q"] and oj["sem"] is None and o["sem"] is None
+                if psum and not same:
+                    hard[i].add(j)
+                elif psum and o["q"] == "P":
+                    if kind != "acc" or k2 != "acc":
+                        soft[i].add(j)
+                elif (m & m2) and (kind != "rd" or k2 != "rd"):
+                    if same and k2 == "rd" and not SAMEQ:
+                        soft[i].add(j)
+                    else:
+                        hard[i].add(j)
+        for (nm, kind, m) in mine:
+            lst = acc.setdefault(nm, [])
+            if kind == "wr" and nm[0] != "p":
+                lst[:] = [e for e in lst if e[2] & ~m]
+            lst.append((i, kind, m))
+    succ = [[] for _ in ops]
+    left = [0] * n
+    for i in range(n):
+        for j in hard[i] | soft[i]:
+            succ[j].append(i)
+            left[i] += 1
+    prio = [0.0] * n
+    for i in range(n - 1, -1, -1):
+        if ops[i]["inorder"]:
+            prio[i] = -10.0 * i
+        else:
+            prio[i] = max([prio[k] for k in succ[i]] + [-10.0 * n]) + 1.0e-4 * (ops[i]["cost"] + ops[i]["lat"])
+    rdy = [0.0] * n
+    ready = {}
+    for i in range(n):
+        if not left[i]:
+            ready.setdefault(ops[i]["q"], []).append(i)
+    free = {}
+    order = []
+    while len(order) < n:
+        best = None
+        for q in sorted(ready):
+            if ready[q]:
+                f = free.get(q, 0.0)
+                s0 = max(f, min(rdy[i] for i in ready[q]))
+                i = max((i for i in ready[q] if rdy[i] <= s0 + SLACK), key=lambda k: (prio[k], -k))
+                st = max(f, rdy[i])
+                if best is None or st < best[0]:
+                    best = (st, i)
+        st, i = best
+        o = ops[i]
+        ready[o["q"]].remove(i)
+        free[o["q"]] = st + o["cost"]
+        order.append(i)
+        for k in succ[i]:
+            rdy[k] = max(rdy[k], st + o["cost"] + (o["lat"] + LAT if i in hard[k] else 0.0))
+            left[k] -= 1
+            if not left[k]:
+                ready.setdefault(ops[k]["q"], []).append(k)
+    pos = {i: t for t, i in enumerate(order)}
+    seen = {}
+    waits = {}
+    sig = set()
+    for i in order:
+        o = ops[i]
+        waits[i] = []
+        if o["q"] == "R":
+            continue
+        need = {}
+        for j in hard[i]:
+            key = ops[j]["sem"][0] if ops[j]["sem"] else ESEM[ops[j]["q"]]
+            if key not in need or pos[j] > pos[need[key]]:
+                need[key] = j
+        sq = seen.setdefault(o["q"], {})
+        for key in sorted(need):
+            if sq.get(key, -1) < pos[need[key]]:
+                sq[key] = pos[need[key]]
+                waits[i].append((key, need[key]))
+                sig.add(need[key])
+    return order, waits, sig
+
+
+def rank_program(g, core, T, topo):
+    rank = T.rank_of(core)
+    if rank is None:
+        return
+    mate = T.cores[(rank + len(T.cores) // 2) % len(T.cores)]
+    rid, pid = topo.addr(mate, core)
+    engs = topo.engines(core, mate)
+    ops = []
+    cnts = {"d": 0, "r": 0, "main": False}
+
+    def A(name, *idx):
+        key = (name, str(idx))
+        if key not in EXT:
+            shp = SCRATCH[name][1][1:]
+            ext = np.arange(int(np.prod(shp))).reshape(shp)[tuple(idx)].reshape(-1)
+            m = 0
+            for e in ext.tolist():
+                m |= 1 << e
+            EXT[key] = (m, len(ext))
+        ap = T[name][(ALL,) + tuple(idx)] if idx else T[name][:]
+        return (ap, [(name, EXT[key][0])], EXT[key][1], 4 if SCRATCH[name][2] in (F32, I32) else 2, False)
+
+    def c(name, lo=0, hi=None, st=None):
+        if hi is None:
+            hi = SCRATCH[name][1][1]
+        return A(name, slice(lo, hi, st))
+
+    def s(k, n=1):
+        return c("SM", SL[k], SL[k] + 16 * n)
+
+    def col(k):
+        return c("SM", SL["col"] + COLS[k], SL["col"] + COLS[k] + 1)
+
+    def ind(win, off):
+        return (win[0].indirect(off[0]), win[1] + off[1], 16 * off[2], win[3], True)
+
+    def add(q, fn, outs, ins, cost, sem=None, lat=0.0, wk="wr", after=()):
+        rd = []
+        for a in ins:
+            if isinstance(a, tuple):
+                rd += a[1]
+        wr = []
+        for a in outs:
+            wr += a[1]
+        ops.append({"q": q, "fn": fn, "rd": rd, "wr": wr, "sem": sem, "cost": cost, "lat": lat, "wk": wk, "after": list(after),
+                    "inorder": cnts["main"]})
+
+    def p(a):
+        return a[0] if isinstance(a, tuple) else a
+
+    def vc(o, a, k=1.0):
+        if a[4]:
+            return 50 + 0.83 * GA * o[2]
+        return 30 + 0.83 * max(64, o[2] * k * (0.5 if o[3] == 2 and a[3] == 2 else 1.0))
+
+    def cp(o, i):
+        add("V", lambda: g.vector.tensor_copy(o[0], i[0]), [o], [i], vc(o, i))
+
+    def scat(win, off, i):
+        add("V", lambda: g.vector.tensor_copy(win[0].indirect(off[0]), i[0]), [win], [off, i], 50 + 0.83 * SC * i[2])
+
+    def tt(o, a, b, op):
+        k = 1.0 if "p" in (a[1][0][0][0], b[1][0][0][0]) else 2.0
+        add("V", lambda: g.vector.tensor_tensor(o[0], a[0], b[0], op), [o], [a, b], vc(o, a, k))
+
+    def ts(o, a, s1, op0, s2=None, op1=None):
+        if op1 is None:
+            add("V", lambda: g.vector.tensor_scalar(o[0], a[0], p(s1), None, op0), [o], [a, s1], vc(o, a))
+        else:
+            add("V", lambda: g.vector.tensor_scalar(o[0], a[0], p(s1), p(s2), op0, op1), [o], [a, s1, s2], vc(o, a))
+
+    def scan(o, d0, d1, op0, op1):
+        add("V", lambda: g.vector.tensor_tensor_scan(o[0], d0[0], d1[0], 0.0, op0, op1), [o], [d0, d1], vc(o, d0))
+
+    def tr(o, i):
+        add("V", lambda: g.vector.transpose(o[0], i[0]), [o], [i], vc(o, i))
+
+    def ms(o, v):
+        add("V", lambda: g.vector.memset(o[0], v), [o], [], vc(o, o))
+
+    def act(o, i, f=AF.Identity, bias=0.0, scale=1.0):
+        add("S", lambda: g.scalar.activation(o[0], i[0], f, bias=p(bias), scale=p(scale)), [o], [i, bias, scale],
+            65 + 0.83 * GA * o[2] if i[4] else 40 + 0.83 * max(64, o[2]))
+
+    def sfill(o, v):
+        act(o, c("KIO", 0, o[2]) if o[2] <= 256 else c("X", 0, o[2]), AF.Identity, v, 0.0)
+
+    def mm(o, l, r, st, sp):
+        add("P", lambda: g.tensor.matmul(o[0], l[0], r[0], st, sp), [o], [l, r], PEC * max(64, o[2]) * (4 if l[3] == 4 else 1),
+            wk="wr" if st or sp else "acc")
+
+    def iota(o, pat, base, cm, fl=True):
+        if fl:
+            add("G", lambda: g.iota(o[0], pat, base, cm, allow_small_or_imprecise_dtypes=True), [o], [], 130 + 1.66 * o[2])
+        else:
+            add("G", lambda: g.iota(o[0], pat, base, cm), [o], [], 130 + 1.66 * o[2])
+
+    def gcp(o, i):
+        add("G", lambda: g.affine_select(o[0], i[0], [[0, o[2]]], OP.is_ge, 0.0, 0, 0), [o], [i], 170 + 1.66 * o[2])
+
+    def dma(o, i, nbytes, after=()):
+        k = "d%d" % cnts["d"]
+        cnts["d"] += 1
+        add("Y", lambda: g.sync.dma_start(p(o), p(i)).then_inc(T.sem[k], 16), [o] if isinstance(o, tuple) else [], [i], 60.0,
+            (k, 16), 2000 + nbytes / 200.0, after=after)
+
+    def send(dst, src, use=engs[:len(engs) // 2]):
+        neng = len(use)
+        emask = sum(1 << e for e in use)
+        k = "d%d" % cnts["d"]
+        r = "r%d" % cnts["r"]
+        cnts["d"] += 1
+        cnts["r"] += 1
+        t = 128 * src[2] * src[3] / 80.0
+        add("G", lambda: g.remote_dma(dst[0], src[0], T.sem[r], T.sem[k], pid, rid, emask), [], [src], 300.0, (k, neng), RLAT)
+        add("R", None, [dst], [], t, (r, neng), 0.0, after=[len(ops) - 1])
+
+    def bc(k, n=1):
+        return ind(s(k, n), c("BCL", 0, 16 * n))
+
+    def turn(src, b0, mat, zh):
+        for h in range(2):
+            for rh in range(2):
+                mm(A("pZ", slice(8 * zh, 8 * zh + 8), h), c(mat, (2 * h + rh) * 128, (2 * h + rh + 1) * 128),
+                   c(src, 128 * rh, 128 * rh + 128) if src == "CF" else A(src, slice(b0, b0 + 8), rh), rh == 0, rh == 1)
+
+    def zhalf(zh):
+        return A("pZ", slice(8 * zh, 8 * zh + 8))
+
+    HOME, PART = c("X", 0, NV), c("X", NV, 2 * NV)
+    K256 = c("KIO")
+    E = c("pE", 0, 256)
+    CL = c("pC", 0, 256)
+    P1 = c("P1", 0, 256)
+    G8 = c("SM", SL["G8"], SL["G8"] + 8)
+    CF8 = c("SM", SL["CF0"], SL["CF0"] + 8)
+
+    H = NV // 2
+    for k in range(2):
+        dma(c("X", k * H, k * H + H), T.pts[:, k * H:k * H + H], 256 * H)
+    ms(c("WI", 256, 512), 0)
+    zero = len(ops) - 1
+    dma(c("WI", 0, 256), T.way[:], 131072)
+    dma((T.WI[0:128:16, 256:512], [("WI1", 1)]), T.cnt[:], 8192, [zero])
+    dma((T.WI[1:128:16, 256:512], [("WI2", 1)]), T.th[:], 8192, [zero])
+    dma(c("CH"), T.cand[:], 512 * NV)
+    iota(c("KM"), [[-1, 128]], 0, 1)
+    iota(c("SI", 0, 2), [[0, 2]], 0, 1, False)
+    iota(s("CF0", 2), [[1, 32]], 0, 0)
+    iota(K256, [[0, 16], [1, 16]], 0, 0)
+    for k in range(2):
+        send(c("X", NV + k * H, NV + k * H + H), c("X", k * H, k * H + H), engs)
+    send(c("CP"), c("CH"), engs[len(engs) // 2:])
+    iota(c("IOT"), [[1, NV]], 1, 0)
+    ops[-1]["after"] = [len(ops) - 5]
+
+    PI = c("SI", 0, 1)
+    ts(c("SI", 2, 3), PI, 15, OP.bitwise_and)
+    ts(c("SI", 3, 4), PI, 4, OP.logical_shift_right, 1, OP.bitwise_and)
+    ts(c("SI", 4, 5), PI, 4, OP.logical_shift_right)
+    ts(c("SI", 5, 6), PI, 1, OP.bitwise_and)
+    cp(col("PM"), c("SI", 2, 3))
+    cp(col("PAR1"), c("SI", 3, 4))
+    cp(col("GRP"), c("SI", 4, 5))
+    ts(col("ODD"), c("SI", 5, 6), 16.0, OP.mult)
+    ts(col("PAR0"), col("PAR1"), -1.0, OP.mult, 1.0, OP.add)
+    ts(col("NZ"), col("PM"), 0.0, OP.is_gt)
+    cp(c("BCL"), s("CF0", 2))
+    act(col("PN0"), col("PAR0"), AF.Identity, 0.0, col("NZ"))
+    act(col("PN1"), col("PAR1"), AF.Identity, 0.0, col("NZ"))
+    for h in range(2):
+        for rh in range(2):
+            k = 2 * h + rh
+            ts(c("ZF", 128 * k, 128 * k + 128), c("KM"), 16.0 * (h - rh), OP.is_equal, col("PAR%d" % h), OP.mult)
+            ts(c("TM1", 128 * k, 128 * k + 128), c("KM"), 16.0 * (h - rh) + 1.0, OP.is_equal, col("PN%d" % h), OP.mult)
+    cp(A("WF"), (T.WI[:], c("WI")[1] + [("WI1", 1), ("WI2", 1)], 512, 4, False))
+    turn("WF", 0, "ZF", 0)
+    turn("WF", 8, "ZF", 1)
+    tr(c("WL"), A("pZ"))
+    ts(c("ID"), c("KM"), 0.0, OP.is_equal)
+    ts(c("IH"), c("KM"), 0.0, OP.is_equal)
+    act(c("NI"), c("ID"), AF.Identity, 0.0, -1.0)
+    act(c("BI"), c("ID"), AF.Identity, 0.0, B17)
+    sfill(c("W16"), 0.0)
+    sfill(c("W1"), 0.0)
+    sfill(c("P1", 256, 272), 0.0)
+    ts(G8, CF8, col("GRP"), OP.is_equal)
+    act(c("KB"), K256)
+    act(c("W16", 15, 128, 16), G8, AF.Identity, 0.0, 16.0)
+    act(c("W1", 15, 128, 16), G8)
+    cp(s("n"), c("WL", 256, 512, 16))
+    act(s("bound"), c("WL", 257, 512, 16), AF.Identity, 0.0, 16.0)
+    act(s("th16"), c("WL", 257, 512, 16), AF.Identity, 0.0, 16.0)
+    act(c("UP"), c("WL", 0, 256), AF.Identity, 1.0)
+    tt(c("VAL"), bc("n"), K256, OP.is_gt)
+    act(s("NE"), s("n"), AF.Identity, 0.0, -B17)
+    sfill(s("SB"), 0.0)
+    tt(P1, c("UP"), c("VAL"), OP.mult)
+    act(c("IO2", 0, 256), K256, AF.Identity, 0.0, B17)
+    act(c("IO2", 256, 512), K256, AF.Identity, -2.0 * B17, -B17)
+    for k in range(4):
+        sfill(c("TRI", 512 * k, 512 * k + 512), 0.0)
+    for k in range(8):
+        sfill(c("A1", 512 * k + 496, 512 * k + 512), 0.0)
+    sfill(c("DA"), 0.0)
+    sfill(c("DB"), 0.0)
+    sfill(c("ACCS", 0, 16), 0.0)
+    sfill(c("NEG"), BIGP)
+    sfill(c("ONES"), 1.0)
+    sfill(c("X", 2 * NV, 4032), 0.0)
+    for r in range(ROUNDS):
+        sfill(c("RM%d" % r, 256, 512), BIGH)
+    for k in range(5):
+        sfill(s("SC%d" % k), 2.0 * k * B17)
+    ts(c("RSTB"), K256, 0.0, OP.is_equal, 1.0e9, OP.mult)
+    cp(c("ZM"), c("ZF"))
+    tt(c("DM"), c("ZM"), c("TM1"), OP.subtract)
+    ts(s("LT"), s("CF0"), col("PM"), OP.is_gt)
+    act(s("TRL"), s("CF0"), AF.Identity, col("PM"), 16.0)
+    ts(c("REP"), CF8, 0.0, OP.mult, col("PM"), OP.add)
+    ts(c("APL"), s("CF0"), col("ODD"), OP.add)
+    for ll in range(16):
+        act(c("TRI", 129 * ll, 128 * ll + 128, 16), G8, AF.Identity, 0.0, c("SM", SL["LT"] + ll, SL["LT"] + ll + 1))
+    t1, t2 = 2.0 * NV, 2.0 * NV + 256
+    for k, (trash, off) in enumerate(((t1, NV), (t2, 0), (t1, 0), (t1, NV))):
+        act(s("TR%d" % k), s("TRL"), AF.Identity, trash)
+        act(s("TD%d" % k), s("TRL"), AF.Identity, trash - off + 1.0)
+    act(c("K1"), K256, AF.Identity, 1.0)
+    act(c("KC", 0, 256, 2), c("KIO", 0, 256, 2), AF.Identity, -1.0)
+    act(c("KC", 1, 256, 2), c("KIO", 1, 256, 2))
+    ms(A("N16"), 0.0)
+
+    def sel(w, ll):
+        return c(w, 15 - ll, 143 - ll)
+
+    def to_list(lst, name, lo, st):
+        for rh in range(2):
+            ts(c(lst, 8 * rh, 8 * rh + 8), c(name, lo + st * rh, lo + st * rh + 14 * st + 1, 2 * st), -1.0, OP.add)
+
+    def penalty():
+        tt(c("PEN"), bc("SB", 2), c("IO2"), OP.subtract)
+
+    def last_point():
+        act(c("INV"), c("VAL"), AF.Identity, 1.0, -1.0)
+        scan(c("UE", 0, 256), c("INV"), P1, OP.mult, OP.add)
+        to_list("EU", "UE", 15, 16)
+        act(s("e1"), c("UE", 15, 256, 16))
+
+    def edges():
+        ts(c("PU", 0, 256, 2), c("P1", 0, 256, 2), -1.0, OP.add)
+        ts(c("PU", 1, 256, 2), c("P1", 1, 256, 2), 1.0, OP.max, NV - 1.0, OP.add)
+        tt(c("DA", 0, 256, 2), c("P1", 0, 256, 2), c("P1", 2, 258, 2), OP.subtract)
+        tt(c("DB", 1, 256, 2), c("P1", 1, 256, 2), c("P1", 3, 258, 2), OP.subtract)
+        act(c("DA", 13, 256, 16), c("P1", 14, 256, 16))
+        mm(E, c("ID"), c("KB"), True, False)
+        for k in range(8):
+            src = ind(c("X", 0, 2 * NV), c("PU", 32 * k, 32 * k + 32))
+            if k in EDGE_S:
+                act(c("VG", 512 * k, 512 * k + 512), src, AF.Copy)
+            else:
+                cp(c("VG", 512 * k, 512 * k + 512), src)
+            d = A("pD%d" % (k % 5), slice(0, 31))
+            mm(d, c("ID"), c("VG", 512 * k, 512 * k + 496), True, False)
+            mm(d, c("NI"), c("VG", 512 * k + 16, 512 * k + 512), False, True)
+            act(c("A1", 512 * k, 512 * k + 496), d, AF.Abs)
+            if k % 2:
+                q = k // 2
+                for ll in range(16):
+                    mm(c("pE", 64 * q, 64 * q + 64), sel("W16", ll), c("A1", 1024 * q + ll, 1024 * q + 1024, 16), False, q == 3 and ll == 15)
+
+    def cut():
+        act(s("nm1"), s("n"), AF.Identity, -1.0)
+        ts(c("UP"), E, 500000.0, OP.is_lt, 99.0, OP.mult)
+        ts(s("nd0"), c("pE", 0, 256, 16), 1500000.0, OP.is_lt)
+        tt(CL, c("UP"), c("K1"), OP.max)
+        scan(c("RUN"), c("RSTB"), CL, OP.add, OP.min)
+        tt(s("j"), c("RUN", 15, 256, 16), s("nd0"), OP.mult)
+        tt(s("jp"), s("j"), s("n"), OP.min)
+        ts(c("SI", 16, 32), s("jp"), 0.5, OP.mult, -0.25, OP.add)
+        ts(s("t1"), s("jp"), 2.0, OP.mult)
+        ts(s("H2"), c("SI", 16, 32), 2.0, OP.mult)
+        ts(s("S2"), c("SI", 16, 32), 2.0 * B17, OP.mult, 2.0 * B17, OP.add)
+        tt(s("mx"), s("t1"), s("nm1"), OP.max)
+        tt(s("back"), s("nm1"), s("t1"), OP.is_gt)
+        tt(s("C2"), s("mx"), s("H2"), OP.subtract)
+        tt(s("SB"), s("back"), s("S2"), OP.mult)
+        ts(s("mB"), s("C2"), -B17, OP.mult, B17, OP.add)
+        tt(s("NE"), s("mB"), s("SB"), OP.subtract)
+        penalty()
+
+    def new_end():
+        act(s("none"), s("C2"), AF.Relu, 1.0, -1.0)
+        ts(s("dl"), c("P1", 0, 256, 16), NV - 96.0, OP.is_lt, float(NV), OP.mult)
+        act(s("dm"), s("dl"), AF.Identity, 97.0 - NV)
+        ts(s("n"), s("C2"), -1.0, OP.add, 1.0, OP.max)
+        ts(c("INV"), c("PEN", 256, 512), B17, OP.is_gt)
+        tt(c("UP"), P1, c("P1", 1, 257), OP.subtract)
+        act(c("INV", 0, 256, 16), s("CF0"), AF.Identity, 0.0, 0.0)
+        tt(s("dl"), s("dm"), s("none"), OP.mult)
+        scan(c("UE"), c("INV"), c("UP"), OP.mult, OP.add)
+        tt(s("e1"), c("UE", 14, 256, 16), s("dl"), OP.add)
+        to_list("EU", "SM", SL["e1"], 1)
+
+    def shift():
+        tt(s("OH0", 5), ind(s("SB"), c("REP", 0, 5)), s("SC0", 5), OP.is_equal)
+        for k in range(5):
+            y = c("YS", 256 * k, 256 * k + 256)
+            tt(y, bc("OH%d" % k), c("P1", 2 * k, 2 * k + 256), OP.mult)
+            mm(c("pC", 256, 512), c("IH"), y, k == 0, k == 4)
+        tt(c("VAL"), bc("n"), K256, OP.is_gt)
+        tt(P1, c("pC", 256, 512), c("VAL"), OP.mult)
+        tt(c("P1", 0, 256, 16), c("P1", 0, 256, 16), s("dl"), OP.add)
+
+    def propose(r):
+        tt(E, E, c("PEN", 0, 256), OP.max)
+        tt(E, E, c("PEN", 256, 512), OP.max)
+        scan(c("RUN"), c("RSTB"), E, OP.add, OP.min)
+        tt(c("NE1"), E, c("RUN"), OP.not_equal)
+        tt(s("prop"), c("RUN", 15, 256, 16), s("bound"), OP.is_lt)
+        scan(c("UAB", 0, 256), c("NE1"), c("DA"), OP.mult, OP.add)
+        scan(c("UAB", 256, 512), c("NE1"), c("DB"), OP.mult, OP.add)
+        AB = c("UAB", 13, 512, 16)
+        ts(c("ABU"), AB, -1.0, OP.add)
+        tt(s("as1"), c("UAB", 13, 256, 16), s("prop"), OP.mult)
+        tt(s("bs1"), c("UAB", 269, 512, 16), s("prop"), OP.mult)
+        act(c("XA"), ind(HOME, c("ABU", 0, 16)), AF.Identity, -0.5)
+        cp(c("ROW"), ind(c("IOT"), c("ABU")))
+        tt(c("XS"), ind(PART, c("ABU", 16, 32)), c("XA"), OP.add)
+        act(c("XR"), c("XS"), AF.Identity, MAGIC, 0.5)
+        act(c("MID%d" % r), c("XR"), AF.Identity, -MAGIC)
+        send(c("RM%d" % r, 0, 256), c("MID%d" % r))
+        for lh in range(16):
+            for e, k in enumerate(("as1", "bs1")):
+                o = 4352 * e + 256 * lh
+                ts(c("EQ", o + 16 * lh, o + 256), c("ROW", 256 * e + 16 * lh, 256 * e + 256),
+                   c("SM", SL[k] + lh, SL[k] + lh + 1), OP.is_equal)
+                if lh < 15:
+                    mm(A("pD3", slice(lh + 1, 16)), c("ID"), c("EQ", o + 16 * lh + 16, o + 256), lh == 0 and e == 0, lh == 14 and e == 1)
+        act(c("ACCS", 16, 256), A("pD3", slice(1, 16)), AF.Copy)
+        tt(s("D0", 2), AB, s("TD0", 2), OP.subtract)
+        tt(s("D2", 2), AB, s("TD2", 2), OP.subtract)
+        for ll in range(16):
+            mm(A("pD4", slice(0, 2)), c("TRI", 128 * ll, 128 * ll + 128), c("EQ", ll, 8704, 272), ll == 0, False)
+        for ll in range(16):
+            mm(A("pD4", 0), sel("W1", ll), c("ACCS", ll, 256, 16), False, ll == 15)
+        ts(s("z1", 2), A("pD4", slice(0, 2)), 0.5, OP.is_lt)
+        tt(s("w1"), s("z1"), s("prop"), OP.mult)
+        tt(s("win"), s("w1"), s("z2"), OP.mult)
+        tt(s("L0", 4), ind(s("win"), c("REP", 0, 4)), s("D0", 4), OP.mult)
+        tt(s("D0", 4), s("L0", 4), s("TR0", 4), OP.add)
+        cp(c("LU%d" % r), s("D0", 4))
+        send(c("RL%d" % r), c("LU%d" % r, 0, 32))
+        if r:
+            new_end()
+        scat(c("X"), c("LU%d" % r, 32, 48), c("MID%d" % r))
+
+    def apply_merges(r):
+        scat(c("X"), c("RL%d" % r), c("RM%d" % r))
+        scat(c("X"), c("LU%d" % r, 48, 64), c("NEG"))
+
+    def count():
+        act(c("WINB"), s("win"))
+        mm(c("pC", 256, 272), c("ONES"), c("WINB"), True, True)
+        add("V", lambda: g.vector.tensor_reduce(col("ACT")[0], T.pC[:, 256:272], AxisListType.X, OP.add), [col("ACT")], [c("pC", 256, 272)], 90.0)
+        cp(c("SI", 8, 9), col("ACT"))
+        ts(c("SI", 9, 10), c("SI", 8, 9), 31, OP.bitwise_and)
+        ts(col("A128"), c("SI", 9, 10), 128.0, OP.mult)
+        act(s("bound"), s("th16"), AF.Identity, col("A128"))
+
+    def rows():
+        gcp(A("P3"), P1)
+        for t in range(4):
+            n = min(6, 21 - 6 * t)
+            gcp(A("PO", ALL, slice(6 * t, 6 * t + n)), A("P3", ALL, slice(1, 2 * n + 1, 2)))
+        for t in range(4):
+            n = min(7, 22 - 7 * t)
+            gcp(A("PEV", ALL, slice(7 * t, 7 * t + n)), A("P3", ALL, slice(0, 2 * n, 2)))
+
+    def hop(first, plan, merges=None, beside=None):
+        tab, mine, other, lst = (c("CH"), HOME, PART, c("EU")) if first else (c("CP"), PART, HOME, c("FU"))
+
+        def turned():
+            ts(c("CF"), c("CU") if CF_FROM_CU else ind(tab, lst), 1.0, OP.add)
+            turn("CF", 0, "ZM", 0)
+            turn("CF", 0, "DM", 1)
+
+        def on_path():
+            tr(CL, zhalf(0))
+            for k in range(6 if first else 7):
+                o = c("EQH", 256 * k, 256 * k + 256)
+                tt(o, CL, A("PO" if first else "PEV", ALL, slice(k, k + 16)), OP.is_equal)
+                mm(E, c("BI"), o, False, False)
+            tr(c("DC"), zhalf(1))
+        cp(c("CU"), ind(tab, lst))
+        mm(E, c("ID"), c("KB"), True, False)
+        if merges is not None:
+            apply_merges(merges)
+        pe = [k for k in range(8) if plan[k] in "SV"]
+        va = [k for k in range(8) if plan[k] == "A"]
+        ga = [k for k in range(8) if plan[k] == "G"]
+        act(c("Y2", 0, 512, 2), ind(mine, lst), AF.Relu, 255.0, -1.0)
+        if pe:
+            lo, hi = 64 * min(pe), 64 * max(pe) + 64
+            cp(c("Y2", lo + 1, hi, 2), c("Y2", lo, hi, 2))
+        if va:
+            a0, a1 = 32 * min(va), 32 * max(va) + 32
+            for i in range(16):
+                ts(c("XB", 16 * a0 + i, 16 * a1, 16), c("Y2", 2 * a0, 2 * a1, 2), -1.0, OP.mult, 255.0, OP.add)
+        if ga:
+            a0, a1 = 32 * min(ga), 32 * max(ga) + 32
+            for i in range(16):
+                gcp(c("XB", 16 * a0 + i, 16 * a1, 16), c("Y2", 2 * a0, 2 * a1, 2))
+        order = (0, 4, 1, 5, 2, 3, 6, 7) if ga else (0, 4, 1, 5, 2, 6, 3, 7)
+        for t0, k in enumerate(order):
+            if t0 == TURN_AT:
+                turned()
+            if t0 == BESIDE_AT and beside is not None:
+                beside()
+            src = ind(other, c("CU", 32 * k, 32 * k + 32))
+            vg = c("VG", 512 * k, 512 * k + 512)
+            a2 = A("A2", slice(4 * (k % 4) + k // 4, 4 * (k % 4) + k // 4 + 3, 2))
+            if k in va:
+                tt(vg, src, c("XB", 512 * k, 512 * k + 512), OP.subtract)
+                act(a2, vg, AF.Abs)
+            elif k in ga:
+                vw = c("VW", 512 * ga.index(k), 512 * ga.index(k) + 512)
+                tt(vw, src, c("XB", 512 * k, 512 * k + 512), OP.add)
+                act(a2, vw, AF.Abs, -255.0)
+            else:
+                if plan[k] == "S":
+                    act(vg, src, AF.Copy)
+                else:
+                    cp(vg, src)
+                d = "pD%d" % (t0 % 5)
+                if not Y_FIRST:
+                    mm(A(d), c("ID"), vg, True, False)
+                for t in range(8):
+                    mm(A(d, ALL, slice(2 * t, 2 * t + 2)), c("ID"), c("Y2", 64 * k, 64 * k + 64), Y_FIRST and t == 0, t == 7 and not Y_FIRST)
+                if Y_FIRST:
+                    mm(A(d), c("ID"), vg, False, True)
+                act(a2, A(d), AF.Abs, -255.0)
+            if t0 == PATH_AT:
+                on_path()
+            if k >= 4:
+                q = k - 4
+                for ll in range(16):
+                    mm(c("pE", 64 * q, 64 * q + 64), sel("W16", ll), A("A2", slice(4 * q, 4 * q + 4), ll),
+                       False, q == 3 and ll == 15)
+        scan(c("RUN"), c("RSTB"), E, OP.add, OP.min)
+        tt(c("NE1"), E, c("RUN"), OP.not_equal)
+        scan(c("UF"), c("NE1"), c("DC"), OP.mult, OP.add)
+
+    best = c("UF", 15, 256, 16)
+
+    def gate():
+        ts(s("lt14"), s("n"), 14.0, OP.is_lt, 65536.0, OP.mult)
+        tt(s("fd2"), s("fd"), s("lt14"), OP.is_lt)
+        act(s("g1"), s("fd2"), AF.Identity, 0.0, 65536.0)
+        tt(c("MK"), bc("n"), c("KC"), OP.is_equal)
+
+    def append():
+        tt(s("hv"), s("h1"), s("go"), OP.mult)
+        tt(s("fv"), s("f1"), s("go"), OP.mult)
+        act(s("go2"), s("go"), AF.Identity, 0.0, 2.0)
+        tt(c("UP"), ind(s("hv", 2), c("APL")), c("MK"), OP.mult)
+        tt(P1, P1, c("UP"), OP.add)
+        tt(s("n"), s("n"), s("go2"), OP.add)
+
+    def pair(again, plan, merges, beside, beside2):
+        hop(True, plan, merges, beside)
+        to_list("FU", "UF", 15, 16)
+        act(s("f1"), best)
+        act(s("fd"), c("RUN", 15, 256, 16))
+        hop(False, PLAN_HOP, None, beside2)
+        tt(s("go"), c("RUN", 15, 256, 16), s("g1"), OP.is_lt)
+        if again:
+            tt(s("de"), best, s("e1"), OP.subtract)
+            tt(s("df"), s("de"), s("go"), OP.mult)
+            tt(s("e1"), s("e1"), s("df"), OP.add)
+            to_list("EU", "SM", SL["e1"], 1)
+        act(s("h1"), best)
+
+    def both(*fs):
+        def run():
+            for f in fs:
+                f()
+        return run
+
+    def points_out():
+        ts(c("XO"), HOME, 255.0, OP.min)
+        dma(T.yx[:], c("XO"), 256 * NV)
+
+    penalty()
+    last_point()
+    rows()
+    cnts["main"] = True
+    for r in range(ROUNDS):
+        edges()
+        if r:
+            cut()
+        propose(r)
+        pair(True, PLAN_CUT if r else PLAN_FIRST, r, both(shift, rows) if r else None,
+             both(gate, count if r + 1 < ROUNDS else points_out))
+        pair(False, PLAN_APP, None, both(append, rows), gate)
+        append()
+
+    ts(A("C16"), P1, -1.0, OP.add, 0.0, OP.max)
+    cp(A("N16", ALL, ALL, 0), s("n"))
+    turn("C16", 0, "ZM", 0)
+    turn("N16", 0, "ZM", 1)
+    tr(c("WL"), A("pZ"))
+    dma(T.yw[:], c("WL", 0, 256), 131072)
+    dma(T.yn[:], (T.WL[0:128:16, 256:512], c("WL", 256, 512)[1]), 8192)
+
+    if "plan" not in PLAN:
+        PLAN["plan"] = order_calls(ops)
+    order, waits, sig = PLAN["plan"]
+    count_of = {}
+    total = {}
+    for i in order:
+        o = ops[i]
+        if o["sem"]:
+            count_of[i] = total[o["sem"][0]] = o["sem"][1]
+        elif i in sig:
+            k = ESEM[o["q"]]
+            total[k] = total.get(k, 0) + 1
+            count_of[i] = total[k]
+    Q = {"V": g.vector, "S": g.scalar, "P": g.tensor, "G": g, "Y": g.sync}
+    waited = {}
+    for i in order:
+        o = ops[i]
+        if o["q"] == "R":
+            continue
+        for (key, j) in waits[i]:
+            Q[o["q"]].wait_ge(T.sem[key], count_of[j])
+            waited[key] = max(waited.get(key, 0), count_of[j])
+        ins = o["fn"]()
+        if i in sig and not o["sem"]:
+            ins.then_inc(T.sem[ESEM[o["q"]]], 1)
+    for key in sorted(total):
+        if waited.get(key, 0) < total[key]:
+            g.wait_ge(T.sem[key], total[key])

@@ -5,14 +5,13 @@ NV, NL, ROUNDS = 1760, 256, 3
 B17 = 131072.0
 BIGH, BIGP = 8192.0, -4096.0
 MAGIC = 12582912.0
-TURN_AT, BESIDE_AT, PATH_AT = 2, 2, 7
-CF_FROM_CU = True
-Y_FIRST = True
+TURN_AT, BESIDE_AT, PATH_AT, BOOST = 0, 0, 3, 50
 RLAT = 2500.0
-PLAN_HOP, PLAN_APP, PLAN_FIRST, PLAN_CUT = "SSSVVVVV", "SSSSVVVV", "SSSVVVVV", "SSSSVVVV"
-EDGE_S = (0, 2, 5)
+PLAN_HOP, PLAN_APP, PLAN_CUT = ("SSVV", "SSVV"), ("SSVV", "SSVV"), ("SSVV", "SSVV")
+EDGE_S = (0, 4, 5)
+LATE = 40
 SAMEQ = False
-GA, SC, PEC, LAT, SLACK = 1.5, 3.5, 0.42, 60.0, 120.0
+GA, SC, PEC, LAT, SLACK = 1.5, 3.5, 0.5, 120.0, 40.0
 
 SLOTS = ["n", "nm1", "th16", "bound", "SB", "NE", "j", "nd0", "jp", "t1", "back", "mx", "H2", "S2", "C2", "mB", "none",
          "dl", "dm", "as1", "bs1", "prop", "z1", "z2", "w1", "win", "e1", "g1", "fd", "fd2", "go", "go2", "de", "df", "hv", "fv", "f1", "h1",
@@ -33,8 +32,8 @@ SB = {
     "P1": ([272], F32), "PU": ([256], U16), "VAL": ([256], F32), "INV": ([256], F32), "PEN": ([512], F32),
     "RUN": ([256], F32), "NE1": ([256], F32), "DA": ([256], F32), "DB": ([256], F32), "UAB": ([512], F32),
     "ABU": ([32], U16), "ROW": ([512], F16), "EQ": ([8704], BF), "ACCS": ([256], BF), "WINB": ([16], BF),
-    "XA": ([256], F32), "XS": ([256], F32), "XR": ([256], F32), "NEG": ([256], BF), "YS": ([1280], F16),
-    "VG": ([4096], BF), "A1": ([4096], BF), "A2": ([16, 16, 16], BF), "XB": ([4096], BF), "VW": ([1536], F32), "Y2": ([512], BF),
+    "XA": ([256], BF), "XS": ([256], BF), "XR": ([256], F32), "NEG": ([256], BF), "YS": ([1280], F16),
+    "VG": ([4096], BF), "A1": ([4096], BF), "A2": ([16, 16, 16], BF), "Y2": ([512], BF),
     "EU": ([16], U16), "FU": ([16], U16), "CU": ([256], U16), "C16": ([8, 2, 16], F16), "N16": ([8, 2, 16], F16),
     "DC": ([256], F32), "PO": ([16, 24], F32), "PEV": ([16, 28], F32), "EQH": ([1792], BF),
     "UF": ([256], F32), "UE": ([256], F32), "MK": ([256], F32), "UP": ([256], F32),
@@ -45,10 +44,10 @@ for _r in range(ROUNDS):
     SB["LU%d" % _r] = ([64], U16)
     SB["RL%d" % _r] = ([32], U16)
 SCRATCH = {k: ("sbuf", [128] + v[0], v[1]) for k, v in SB.items()}
-SCRATCH["pZ"] = ("psum", [128, 16, 2, 16], F32)
-SCRATCH["pE"] = ("psum", [128, 512], F32)
-SCRATCH["pC"] = ("psum", [128, 512], F32)
-for _r in range(5):
+for _r in range(2):
+    SCRATCH["pZ%d" % _r] = ("psum", [128, 16, 2, 16], F32)
+    SCRATCH["pE%d" % _r] = ("psum", [128, 512], F32)
+for _r in range(4):
     SCRATCH["pD%d" % _r] = ("psum", [128, 32, 16], F32)
 SEMAPHORES = ["sV", "sS", "sP", "sG"] + ["d%d" % i for i in range(24)] + ["r%d" % i for i in range(12)]
 OP = AluOpType
@@ -96,7 +95,7 @@ def order_calls(ops):
     prio = [0.0] * n
     for i in range(n - 1, -1, -1):
         if ops[i]["inorder"]:
-            prio[i] = -10.0 * i
+            prio[i] = -10.0 * (i + ops[i].get("late", 0))
         else:
             prio[i] = max([prio[k] for k in succ[i]] + [-10.0 * n]) + 1.0e-4 * (ops[i]["cost"] + ops[i]["lat"])
     rdy = [0.0] * n
@@ -272,16 +271,11 @@ def rank_program(g, core, T, topo):
     def turn(src, b0, mat, zh):
         for h in range(2):
             for rh in range(2):
-                mm(A("pZ", slice(8 * zh, 8 * zh + 8), h), c(mat, (2 * h + rh) * 128, (2 * h + rh + 1) * 128),
-                   c(src, 128 * rh, 128 * rh + 128) if src == "CF" else A(src, slice(b0, b0 + 8), rh), rh == 0, rh == 1)
-
-    def zhalf(zh):
-        return A("pZ", slice(8 * zh, 8 * zh + 8))
+                mm(A("pZ0", slice(8 * zh, 8 * zh + 8), h), c(mat, (2 * h + rh) * 128, (2 * h + rh + 1) * 128),
+                   A(src, slice(b0, b0 + 8), rh), rh == 0, rh == 1)
 
     HOME, PART = c("X", 0, NV), c("X", NV, 2 * NV)
     K256 = c("KIO")
-    E = c("pE", 0, 256)
-    CL = c("pC", 0, 256)
     P1 = c("P1", 0, 256)
     G8 = c("SM", SL["G8"], SL["G8"] + 8)
     CF8 = c("SM", SL["CF0"], SL["CF0"] + 8)
@@ -327,7 +321,7 @@ def rank_program(g, core, T, topo):
     cp(A("WF"), (T.WI[:], c("WI")[1] + [("WI1", 1), ("WI2", 1)], 512, 4, False))
     turn("WF", 0, "ZF", 0)
     turn("WF", 8, "ZF", 1)
-    tr(c("WL"), A("pZ"))
+    tr(c("WL"), A("pZ0"))
     ts(c("ID"), c("KM"), 0.0, OP.is_equal)
     ts(c("IH"), c("KM"), 0.0, OP.is_equal)
     act(c("NI"), c("ID"), AF.Identity, 0.0, -1.0)
@@ -384,9 +378,11 @@ def rank_program(g, core, T, topo):
     def sel(w, ll):
         return c(w, 15 - ll, 143 - ll)
 
-    def to_list(lst, name, lo, st):
-        for rh in range(2):
-            ts(c(lst, 8 * rh, 8 * rh + 8), c(name, lo + st * rh, lo + st * rh + 14 * st + 1, 2 * st), -1.0, OP.add)
+    def to_list(lst, name, lo, st, half=None):
+        for hf in (0, 1) if half is None else (half,):
+            for rh in range(2):
+                a = lo + st * (8 * hf + rh)
+                ts(c(lst, 8 * hf + 4 * rh, 8 * hf + 4 * rh + 4), c(name, a, a + 6 * st + 1, 2 * st), -1.0, OP.add)
 
     def penalty():
         tt(c("PEN"), bc("SB", 2), c("IO2"), OP.subtract)
@@ -397,47 +393,72 @@ def rank_program(g, core, T, topo):
         to_list("EU", "UE", 15, 16)
         act(s("e1"), c("UE", 15, 256, 16))
 
-    def edges():
-        ts(c("PU", 0, 256, 2), c("P1", 0, 256, 2), -1.0, OP.add)
-        ts(c("PU", 1, 256, 2), c("P1", 1, 256, 2), 1.0, OP.max, NV - 1.0, OP.add)
-        tt(c("DA", 0, 256, 2), c("P1", 0, 256, 2), c("P1", 2, 258, 2), OP.subtract)
-        tt(c("DB", 1, 256, 2), c("P1", 1, 256, 2), c("P1", 3, 258, 2), OP.subtract)
-        act(c("DA", 13, 256, 16), c("P1", 14, 256, 16))
-        mm(E, c("ID"), c("KB"), True, False)
-        for k in range(8):
+    def hs(k, hf):
+        return c("SM", SL[k] + 8 * hf, SL[k] + 8 * hf + 8)
+
+    def hc(name, hf, o=0):
+        return c(name, o + 128 * hf, o + 128 * hf + 128)
+
+    def ends(name, hf):
+        return c(name, 128 * hf + 15, 128 * hf + 128, 16)
+
+    def edges(hf):
+        a, b = 128 * hf, 128 * hf + 128
+        pe = "pE%d" % hf
+        ts(c("PU", a, b, 2), c("P1", a, b, 2), -1.0, OP.add)
+        ts(c("PU", a + 1, b, 2), c("P1", a + 1, b, 2), 1.0, OP.max, NV - 1.0, OP.add)
+        mm(c(pe, 0, 128), c("ID"), c("KB", 0, 128), True, False)
+        for k in range(4 * hf, 4 * hf + 4):
             src = ind(c("X", 0, 2 * NV), c("PU", 32 * k, 32 * k + 32))
             if k in EDGE_S:
                 act(c("VG", 512 * k, 512 * k + 512), src, AF.Copy)
             else:
                 cp(c("VG", 512 * k, 512 * k + 512), src)
-            d = A("pD%d" % (k % 5), slice(0, 31))
+            d = A("pD%d" % (k % 4 if hf else k % 2), slice(0, 31))
             mm(d, c("ID"), c("VG", 512 * k, 512 * k + 496), True, False)
             mm(d, c("NI"), c("VG", 512 * k + 16, 512 * k + 512), False, True)
             act(c("A1", 512 * k, 512 * k + 496), d, AF.Abs)
             if k % 2:
                 q = k // 2
                 for ll in range(16):
-                    mm(c("pE", 64 * q, 64 * q + 64), sel("W16", ll), c("A1", 1024 * q + ll, 1024 * q + 1024, 16), False, q == 3 and ll == 15)
+                    mm(c(pe, 64 * (q % 2), 64 * (q % 2) + 64), sel("W16", ll), c("A1", 1024 * q + ll, 1024 * q + 1024, 16), False, q % 2 == 1 and ll == 15)
+                    ops[-1]["late"] = LATE
+        tt(c("DA", a, b - 2, 2), c("P1", a, b - 2, 2), c("P1", a + 2, b, 2), OP.subtract)
+        tt(c("DB", a + 1, b - 2, 2), c("P1", a + 1, b - 2, 2), c("P1", a + 3, b, 2), OP.subtract)
+        act(c("DA", a + 13, b, 16), c("P1", a + 14, b, 16))
 
-    def cut():
-        act(s("nm1"), s("n"), AF.Identity, -1.0)
-        ts(c("UP"), E, 500000.0, OP.is_lt, 99.0, OP.mult)
-        ts(s("nd0"), c("pE", 0, 256, 16), 1500000.0, OP.is_lt)
-        tt(CL, c("UP"), c("K1"), OP.max)
-        scan(c("RUN"), c("RSTB"), CL, OP.add, OP.min)
-        tt(s("j"), c("RUN", 15, 256, 16), s("nd0"), OP.mult)
-        tt(s("jp"), s("j"), s("n"), OP.min)
-        ts(c("SI", 16, 32), s("jp"), 0.5, OP.mult, -0.25, OP.add)
-        ts(s("t1"), s("jp"), 2.0, OP.mult)
-        ts(s("H2"), c("SI", 16, 32), 2.0, OP.mult)
-        ts(s("S2"), c("SI", 16, 32), 2.0 * B17, OP.mult, 2.0 * B17, OP.add)
-        tt(s("mx"), s("t1"), s("nm1"), OP.max)
-        tt(s("back"), s("nm1"), s("t1"), OP.is_gt)
-        tt(s("C2"), s("mx"), s("H2"), OP.subtract)
-        tt(s("SB"), s("back"), s("S2"), OP.mult)
-        ts(s("mB"), s("C2"), -B17, OP.mult, B17, OP.add)
-        tt(s("NE"), s("mB"), s("SB"), OP.subtract)
-        penalty()
+    def cut(hf):
+        pe = "pE%d" % hf
+        hi = c("SI", 16 + 8 * hf, 24 + 8 * hf)
+        act(hs("nm1", hf), hs("n", hf), AF.Identity, -1.0)
+        ts(c(pe, 256, 384), c(pe, 0, 128), 500000.0, OP.is_lt, 99.0, OP.mult)
+        ts(hs("nd0", hf), c(pe, 0, 128, 16), 1500000.0, OP.is_lt)
+        tt(c(pe, 256, 384), c(pe, 256, 384), c("K1", 0, 128), OP.max)
+        scan(hc("RUN", hf), c("RSTB", 0, 128), c(pe, 256, 384), OP.add, OP.min)
+        tt(hs("j", hf), ends("RUN", hf), hs("nd0", hf), OP.mult)
+        tt(hs("jp", hf), hs("j", hf), hs("n", hf), OP.min)
+        ts(hi, hs("jp", hf), 0.5, OP.mult, -0.25, OP.add)
+        ts(hs("t1", hf), hs("jp", hf), 2.0, OP.mult)
+        ts(hs("H2", hf), hi, 2.0, OP.mult)
+        ts(hs("S2", hf), hi, 2.0 * B17, OP.mult, 2.0 * B17, OP.add)
+        tt(hs("mx", hf), hs("t1", hf), hs("nm1", hf), OP.max)
+        tt(hs("back", hf), hs("nm1", hf), hs("t1", hf), OP.is_gt)
+        tt(hs("C2", hf), hs("mx", hf), hs("H2", hf), OP.subtract)
+        tt(hs("SB", hf), hs("back", hf), hs("S2", hf), OP.mult)
+        ts(hs("mB", hf), hs("C2", hf), -B17, OP.mult, B17, OP.add)
+        tt(hs("NE", hf), hs("mB", hf), hs("SB", hf), OP.subtract)
+        tt(hc("PEN", hf), ind(hs("SB", hf), c("BCL", 0, 8)), c("IO2", 0, 128), OP.subtract)
+        tt(hc("PEN", hf, 256), ind(hs("NE", hf), c("BCL", 0, 8)), c("IO2", 256, 384), OP.subtract)
+
+    def least(hf, r):
+        e = c("pE%d" % hf, 0, 128)
+        if r:
+            tt(e, e, hc("PEN", hf), OP.max)
+        tt(e, e, hc("PEN", hf, 256), OP.max)
+        scan(hc("RUN", hf), c("RSTB", 0, 128), e, OP.add, OP.min)
+        tt(hc("NE1", hf), e, hc("RUN", hf), OP.not_equal)
+        scan(hc("UAB", hf), hc("NE1", hf), hc("DA", hf), OP.mult, OP.add)
+        scan(hc("UAB", hf, 256), hc("NE1", hf), hc("DB", hf), OP.mult, OP.add)
 
     def new_end():
         act(s("none"), s("C2"), AF.Relu, 1.0, -1.0)
@@ -457,27 +478,24 @@ def rank_program(g, core, T, topo):
         for k in range(5):
             y = c("YS", 256 * k, 256 * k + 256)
             tt(y, bc("OH%d" % k), c("P1", 2 * k, 2 * k + 256), OP.mult)
-            mm(c("pC", 256, 512), c("IH"), y, k == 0, k == 4)
+            mm(A("pZ1", slice(8, 16)), c("IH"), y, k == 0, k == 4)
         tt(c("VAL"), bc("n"), K256, OP.is_gt)
-        tt(P1, c("pC", 256, 512), c("VAL"), OP.mult)
+        tt(P1, A("pZ1", slice(8, 16)), c("VAL"), OP.mult)
         tt(c("P1", 0, 256, 16), c("P1", 0, 256, 16), s("dl"), OP.add)
 
     def propose(r):
-        tt(E, E, c("PEN", 0, 256), OP.max)
-        tt(E, E, c("PEN", 256, 512), OP.max)
-        scan(c("RUN"), c("RSTB"), E, OP.add, OP.min)
-        tt(c("NE1"), E, c("RUN"), OP.not_equal)
-        tt(s("prop"), c("RUN", 15, 256, 16), s("bound"), OP.is_lt)
-        scan(c("UAB", 0, 256), c("NE1"), c("DA"), OP.mult, OP.add)
-        scan(c("UAB", 256, 512), c("NE1"), c("DB"), OP.mult, OP.add)
         AB = c("UAB", 13, 512, 16)
         ts(c("ABU"), AB, -1.0, OP.add)
+        tt(s("prop"), c("RUN", 15, 256, 16), s("bound"), OP.is_lt)
         tt(s("as1"), c("UAB", 13, 256, 16), s("prop"), OP.mult)
         tt(s("bs1"), c("UAB", 269, 512, 16), s("prop"), OP.mult)
-        act(c("XA"), ind(HOME, c("ABU", 0, 16)), AF.Identity, -0.5)
+        act(c("XA"), ind(HOME, c("ABU", 0, 16)), AF.Copy)
         cp(c("ROW"), ind(c("IOT"), c("ABU")))
-        tt(c("XS"), ind(PART, c("ABU", 16, 32)), c("XA"), OP.add)
-        act(c("XR"), c("XS"), AF.Identity, MAGIC, 0.5)
+        act(c("XS"), ind(PART, c("ABU", 16, 32)), AF.Copy)
+        mm(A("pD0", slice(0, 16)), c("ID"), c("XA"), True, False)
+        mm(A("pD0", slice(0, 16)), c("ID"), c("XS"), False, True)
+        act(c("INV"), A("pD0", slice(0, 16)), AF.Identity, -0.25, 0.5)
+        act(c("XR"), c("INV"), AF.Identity, MAGIC)
         act(c("MID%d" % r), c("XR"), AF.Identity, -MAGIC)
         send(c("RM%d" % r, 0, 256), c("MID%d" % r))
         for lh in range(16):
@@ -486,15 +504,15 @@ def rank_program(g, core, T, topo):
                 ts(c("EQ", o + 16 * lh, o + 256), c("ROW", 256 * e + 16 * lh, 256 * e + 256),
                    c("SM", SL[k] + lh, SL[k] + lh + 1), OP.is_equal)
                 if lh < 15:
-                    mm(A("pD3", slice(lh + 1, 16)), c("ID"), c("EQ", o + 16 * lh + 16, o + 256), lh == 0 and e == 0, lh == 14 and e == 1)
-        act(c("ACCS", 16, 256), A("pD3", slice(1, 16)), AF.Copy)
+                    mm(A("pD2", slice(lh + 1, 16)), c("ID"), c("EQ", o + 16 * lh + 16, o + 256), lh == 0 and e == 0, lh == 14 and e == 1)
+        act(c("ACCS", 16, 256), A("pD2", slice(1, 16)), AF.Copy)
         tt(s("D0", 2), AB, s("TD0", 2), OP.subtract)
         tt(s("D2", 2), AB, s("TD2", 2), OP.subtract)
         for ll in range(16):
-            mm(A("pD4", slice(0, 2)), c("TRI", 128 * ll, 128 * ll + 128), c("EQ", ll, 8704, 272), ll == 0, False)
+            mm(A("pD3", slice(0, 2)), c("TRI", 128 * ll, 128 * ll + 128), c("EQ", ll, 8704, 272), ll == 0, False)
         for ll in range(16):
-            mm(A("pD4", 0), sel("W1", ll), c("ACCS", ll, 256, 16), False, ll == 15)
-        ts(s("z1", 2), A("pD4", slice(0, 2)), 0.5, OP.is_lt)
+            mm(A("pD3", 0), sel("W1", ll), c("ACCS", ll, 256, 16), False, ll == 15)
+        ts(s("z1", 2), A("pD3", slice(0, 2)), 0.5, OP.is_lt)
         tt(s("w1"), s("z1"), s("prop"), OP.mult)
         tt(s("win"), s("w1"), s("z2"), OP.mult)
         tt(s("L0", 4), ind(s("win"), c("REP", 0, 4)), s("D0", 4), OP.mult)
@@ -511,131 +529,114 @@ def rank_program(g, core, T, topo):
 
     def count():
         act(c("WINB"), s("win"))
-        mm(c("pC", 256, 272), c("ONES"), c("WINB"), True, True)
-        add("V", lambda: g.vector.tensor_reduce(col("ACT")[0], T.pC[:, 256:272], AxisListType.X, OP.add), [col("ACT")], [c("pC", 256, 272)], 90.0)
+        mm(A("pZ1", 15, 1), c("ONES"), c("WINB"), True, True)
+        add("V", lambda: g.vector.tensor_reduce(col("ACT")[0], T.pZ1[:, 15, 1], AxisListType.X, OP.add), [col("ACT")], [A("pZ1", 15, 1)], 90.0)
         cp(c("SI", 8, 9), col("ACT"))
         ts(c("SI", 9, 10), c("SI", 8, 9), 31, OP.bitwise_and)
         ts(col("A128"), c("SI", 9, 10), 128.0, OP.mult)
         act(s("bound"), s("th16"), AF.Identity, col("A128"))
 
-    def rows():
-        gcp(A("P3"), P1)
+    def rows(hf):
+        lh = slice(8 * hf, 8 * hf + 8)
+        gcp(A("P3", lh), hc("P1", hf))
         for t in range(4):
             n = min(6, 21 - 6 * t)
-            gcp(A("PO", ALL, slice(6 * t, 6 * t + n)), A("P3", ALL, slice(1, 2 * n + 1, 2)))
+            gcp(A("PO", lh, slice(6 * t, 6 * t + n)), A("P3", lh, slice(1, 2 * n + 1, 2)))
         for t in range(4):
             n = min(7, 22 - 7 * t)
-            gcp(A("PEV", ALL, slice(7 * t, 7 * t + n)), A("P3", ALL, slice(0, 2 * n, 2)))
+            gcp(A("PEV", lh, slice(7 * t, 7 * t + n)), A("P3", lh, slice(0, 2 * n, 2)))
 
-    def hop(first, plan, merges=None, beside=None):
-        tab, mine, other, lst = (c("CH"), HOME, PART, c("EU")) if first else (c("CP"), PART, HOME, c("FU"))
+    def boost(since, by):
+        for o in ops[since:]:
+            o["late"] = by
 
-        def turned():
-            ts(c("CF"), c("CU") if CF_FROM_CU else ind(tab, lst), 1.0, OP.add)
-            turn("CF", 0, "ZM", 0)
-            turn("CF", 0, "DM", 1)
-
-        def on_path():
-            tr(CL, zhalf(0))
-            for k in range(6 if first else 7):
-                o = c("EQH", 256 * k, 256 * k + 256)
-                tt(o, CL, A("PO" if first else "PEV", ALL, slice(k, k + 16)), OP.is_equal)
-                mm(E, c("BI"), o, False, False)
-            tr(c("DC"), zhalf(1))
-        cp(c("CU"), ind(tab, lst))
-        mm(E, c("ID"), c("KB"), True, False)
-        if merges is not None:
-            apply_merges(merges)
-        pe = [k for k in range(8) if plan[k] in "SV"]
-        va = [k for k in range(8) if plan[k] == "A"]
-        ga = [k for k in range(8) if plan[k] == "G"]
-        act(c("Y2", 0, 512, 2), ind(mine, lst), AF.Relu, 255.0, -1.0)
-        if pe:
-            lo, hi = 64 * min(pe), 64 * max(pe) + 64
-            cp(c("Y2", lo + 1, hi, 2), c("Y2", lo, hi, 2))
-        if va:
-            a0, a1 = 32 * min(va), 32 * max(va) + 32
-            for i in range(16):
-                ts(c("XB", 16 * a0 + i, 16 * a1, 16), c("Y2", 2 * a0, 2 * a1, 2), -1.0, OP.mult, 255.0, OP.add)
-        if ga:
-            a0, a1 = 32 * min(ga), 32 * max(ga) + 32
-            for i in range(16):
-                gcp(c("XB", 16 * a0 + i, 16 * a1, 16), c("Y2", 2 * a0, 2 * a1, 2))
-        order = (0, 4, 1, 5, 2, 3, 6, 7) if ga else (0, 4, 1, 5, 2, 6, 3, 7)
-        for t0, k in enumerate(order):
+    def hop(first, hf, plan, beside):
+        tab, mine, other, lst = (c("CH"), HOME, PART, "EU") if first else (c("CP"), PART, HOME, "FU")
+        lst = c(lst, 8 * hf, 8 * hf + 8)
+        pz, pe = "pZ%d" % hf, "pE%d" % hf
+        e = c(pe, 0, 128)
+        at = len(ops)
+        cp(hc("CU", hf), ind(tab, lst))
+        act(c("Y2", 256 * hf, 256 * hf + 256, 2), ind(mine, lst), AF.Relu, 255.0, -1.0)
+        cp(c("Y2", 256 * hf + 1, 256 * hf + 256, 2), c("Y2", 256 * hf, 256 * hf + 256, 2))
+        boost(at, -BOOST)
+        mm(e, c("ID"), c("KB", 0, 128), True, False)
+        for t0, k in enumerate((0, 2, 1, 3)):
             if t0 == TURN_AT:
-                turned()
-            if t0 == BESIDE_AT and beside is not None:
-                beside()
-            src = ind(other, c("CU", 32 * k, 32 * k + 32))
-            vg = c("VG", 512 * k, 512 * k + 512)
-            a2 = A("A2", slice(4 * (k % 4) + k // 4, 4 * (k % 4) + k // 4 + 3, 2))
-            if k in va:
-                tt(vg, src, c("XB", 512 * k, 512 * k + 512), OP.subtract)
-                act(a2, vg, AF.Abs)
-            elif k in ga:
-                vw = c("VW", 512 * ga.index(k), 512 * ga.index(k) + 512)
-                tt(vw, src, c("XB", 512 * k, 512 * k + 512), OP.add)
-                act(a2, vw, AF.Abs, -255.0)
+                ts(hc("CF", hf), hc("CU", hf), 1.0, OP.add)
+                for zh, mat in enumerate(("ZM", "DM")):
+                    for h in range(2):
+                        for rh in range(2):
+                            mm(A(pz, slice(4 * zh, 4 * zh + 4), h), c(mat, (2 * h + rh) * 128, (2 * h + rh + 1) * 128),
+                               c("CF", 128 * hf + 64 * rh, 128 * hf + 64 * rh + 64), rh == 0, rh == 1)
+            if t0 == BESIDE_AT:
+                for f in beside:
+                    f()
+            kk = 4 * hf + k
+            src = ind(other, c("CU", 32 * kk, 32 * kk + 32))
+            vg = c("VG", 512 * kk, 512 * kk + 512)
+            b0 = 8 * hf + 4 * (k % 2) + k // 2
+            if plan[k] == "S":
+                act(vg, src, AF.Copy)
             else:
-                if plan[k] == "S":
-                    act(vg, src, AF.Copy)
-                else:
-                    cp(vg, src)
-                d = "pD%d" % (t0 % 5)
-                if not Y_FIRST:
-                    mm(A(d), c("ID"), vg, True, False)
-                for t in range(8):
-                    mm(A(d, ALL, slice(2 * t, 2 * t + 2)), c("ID"), c("Y2", 64 * k, 64 * k + 64), Y_FIRST and t == 0, t == 7 and not Y_FIRST)
-                if Y_FIRST:
-                    mm(A(d), c("ID"), vg, False, True)
-                act(a2, A(d), AF.Abs, -255.0)
+                cp(vg, src)
+            d = "pD%d" % (2 * hf + t0 % 2)
+            for t in range(8):
+                mm(A(d, ALL, slice(2 * t, 2 * t + 2)), c("ID"), c("Y2", 64 * kk, 64 * kk + 64), t == 0, False)
+            mm(A(d), c("ID"), vg, False, True)
+            act(A("A2", slice(b0, b0 + 3, 2)), A(d), AF.Abs, -255.0)
             if t0 == PATH_AT:
-                on_path()
-            if k >= 4:
-                q = k - 4
+                cl = A(pz, slice(8, 12))
+                tr(cl, A(pz, slice(0, 4)))
+                for j in range(6 if first else 7):
+                    o = hc("EQH", hf, 256 * j)
+                    tt(o, cl, A("PO" if first else "PEV", slice(8 * hf, 8 * hf + 8), slice(j, j + 16)), OP.is_equal)
+                    mm(e, c("BI"), o, False, False)
+                tr(hc("DC", hf), A(pz, slice(4, 8)))
+            if k >= 2:
+                q = k - 2
                 for ll in range(16):
-                    mm(c("pE", 64 * q, 64 * q + 64), sel("W16", ll), A("A2", slice(4 * q, 4 * q + 4), ll),
-                       False, q == 3 and ll == 15)
-        scan(c("RUN"), c("RSTB"), E, OP.add, OP.min)
-        tt(c("NE1"), E, c("RUN"), OP.not_equal)
-        scan(c("UF"), c("NE1"), c("DC"), OP.mult, OP.add)
+                    mm(c(pe, 64 * q, 64 * q + 64), sel("W16", ll), A("A2", slice(8 * hf + 4 * q, 8 * hf + 4 * q + 4), ll),
+                       False, q == 1 and ll == 15)
+                    ops[-1]["late"] = LATE
+        at = len(ops)
+        scan(hc("RUN", hf), c("RSTB", 0, 128), e, OP.add, OP.min)
+        tt(hc("NE1", hf), e, hc("RUN", hf), OP.not_equal)
+        scan(hc("UF", hf), hc("NE1", hf), hc("DC", hf), OP.mult, OP.add)
+        return at
 
-    best = c("UF", 15, 256, 16)
+    def gate(hf):
+        ts(hs("lt14", hf), hs("n", hf), 14.0, OP.is_lt, 65536.0, OP.mult)
+        tt(hs("fd2", hf), hs("fd", hf), hs("lt14", hf), OP.is_lt)
+        act(hs("g1", hf), hs("fd2", hf), AF.Identity, 0.0, 65536.0)
+        tt(hc("MK", hf), ind(hs("n", hf), c("BCL", 0, 8)), c("KC", 0, 128), OP.is_equal)
 
-    def gate():
-        ts(s("lt14"), s("n"), 14.0, OP.is_lt, 65536.0, OP.mult)
-        tt(s("fd2"), s("fd"), s("lt14"), OP.is_lt)
-        act(s("g1"), s("fd2"), AF.Identity, 0.0, 65536.0)
-        tt(c("MK"), bc("n"), c("KC"), OP.is_equal)
+    def append(hf):
+        tt(hs("hv", hf), hs("h1", hf), hs("go", hf), OP.mult)
+        tt(hs("fv", hf), hs("f1", hf), hs("go", hf), OP.mult)
+        act(hs("go2", hf), hs("go", hf), AF.Identity, 0.0, 2.0)
+        win = (T.SM[:, SL["hv"] + 8 * hf:SL["hv"] + 8 * hf + 24], hs("hv", hf)[1] + hs("fv", hf)[1], 24, 4, False)
+        tt(hc("UP", hf), ind(win, c("APL", 0, 8)), hc("MK", hf), OP.mult)
+        tt(hc("P1", hf), hc("P1", hf), hc("UP", hf), OP.add)
+        tt(hs("n", hf), hs("n", hf), hs("go2", hf), OP.add)
 
-    def append():
-        tt(s("hv"), s("h1"), s("go"), OP.mult)
-        tt(s("fv"), s("f1"), s("go"), OP.mult)
-        act(s("go2"), s("go"), AF.Identity, 0.0, 2.0)
-        tt(c("UP"), ind(s("hv", 2), c("APL")), c("MK"), OP.mult)
-        tt(P1, P1, c("UP"), OP.add)
-        tt(s("n"), s("n"), s("go2"), OP.add)
-
-    def pair(again, plan, merges, beside, beside2):
-        hop(True, plan, merges, beside)
-        to_list("FU", "UF", 15, 16)
-        act(s("f1"), best)
-        act(s("fd"), c("RUN", 15, 256, 16))
-        hop(False, PLAN_HOP, None, beside2)
-        tt(s("go"), c("RUN", 15, 256, 16), s("g1"), OP.is_lt)
-        if again:
-            tt(s("de"), best, s("e1"), OP.subtract)
-            tt(s("df"), s("de"), s("go"), OP.mult)
-            tt(s("e1"), s("e1"), s("df"), OP.add)
-            to_list("EU", "SM", SL["e1"], 1)
-        act(s("h1"), best)
-
-    def both(*fs):
-        def run():
-            for f in fs:
-                f()
-        return run
+    def pair(again, plan, beside, beside2):
+        for hf in range(2):
+            at = hop(True, hf, plan[hf], beside[hf])
+            to_list("FU", "UF", 15, 16, hf)
+            boost(at, -BOOST)
+            act(hs("f1", hf), ends("UF", hf))
+            act(hs("fd", hf), ends("RUN", hf))
+        for hf in range(2):
+            at = hop(False, hf, PLAN_HOP[hf], beside2[hf])
+            tt(hs("go", hf), ends("RUN", hf), hs("g1", hf), OP.is_lt)
+            if again:
+                tt(hs("de", hf), ends("UF", hf), hs("e1", hf), OP.subtract)
+                tt(hs("df", hf), hs("de", hf), hs("go", hf), OP.mult)
+                tt(hs("e1", hf), hs("e1", hf), hs("df", hf), OP.add)
+                to_list("EU", "SM", SL["e1"], 1, hf)
+            boost(at, -BOOST)
+            act(hs("h1", hf), ends("UF", hf))
 
     def points_out():
         ts(c("XO"), HOME, 255.0, OP.min)
@@ -643,23 +644,32 @@ def rank_program(g, core, T, topo):
 
     penalty()
     last_point()
-    rows()
+    rows(0)
+    rows(1)
     cnts["main"] = True
     for r in range(ROUNDS):
-        edges()
-        if r:
-            cut()
+        for hf in range(2):
+            if r:
+                append(hf)
+            edges(hf)
+        for hf in range(2):
+            if r:
+                cut(hf)
+            least(hf, r)
         propose(r)
-        pair(True, PLAN_CUT if r else PLAN_FIRST, r, both(shift, rows) if r else None,
-             both(gate, count if r + 1 < ROUNDS else points_out))
-        pair(False, PLAN_APP, None, both(append, rows), gate)
-        append()
+        apply_merges(r)
+        pair(True, PLAN_CUT if r else PLAN_HOP, [[shift, lambda: rows(0), lambda: rows(1)] if r else [], []],
+             [[lambda: gate(0)], [lambda: gate(1), count if r + 1 < ROUNDS else points_out]])
+        pair(False, PLAN_APP, [[lambda: append(0), lambda: rows(0)], [lambda: append(1), lambda: rows(1)]],
+             [[lambda: gate(0)], [lambda: gate(1)]])
+    append(0)
+    append(1)
 
     ts(A("C16"), P1, -1.0, OP.add, 0.0, OP.max)
     cp(A("N16", ALL, ALL, 0), s("n"))
     turn("C16", 0, "ZM", 0)
     turn("N16", 0, "ZM", 1)
-    tr(c("WL"), A("pZ"))
+    tr(c("WL"), A("pZ0"))
     dma(T.yw[:], c("WL", 0, 256), 131072)
     dma(T.yn[:], (T.WL[0:128:16, 256:512], c("WL", 256, 512)[1]), 8192)
 

@@ -2,54 +2,76 @@ import numpy as np
 from concourse.mybir import AluOpType, AxisListType, ActivationFunctionType
 
 NV, NL, ROUNDS = 1760, 256, 3
+OFF, TRASH, WIN = 16, 1776, 2032
 B17 = 131072.0
-BIGH, BIGP = 8192.0, -4096.0
+BIGH, BIGP = 262144.0, -131072.0
 MAGIC = 12582912.0
-TURN_AT, BESIDE_AT, PATH_AT, BOOST = 0, 0, 3, 50
-RLAT = 2500.0
-PLAN_HOP, PLAN_APP, PLAN_CUT = ("SSVV", "SSVV"), ("SSVV", "SSVV"), ("SSVV", "SSVV")
-EDGE_S = (0, 4, 5)
-LATE = 40
-SAMEQ = False
-GA, SC, PEC, LAT, SLACK = 1.5, 3.5, 0.5, 120.0, 40.0
+U18 = 2.0 ** -18
+FAR = 2.0 ** 99
+LI, NN = 408, 424
+PLAN_HOP = ("VSSv", "VSSv")
+PLAN_EDGE = ("VSSv", "VSSv")
+Y2_ON = "VV"
+SUMS = 1
+PIECES, GAP = (0, 12, 22, 32), 350
+HALF = 3300.0
+T_GATHER, T_ABS = (680, 680, 1340, 1460), (2020, 2445, 2870, 3295)
+T_DUP, T_PATH, T_PICK = 660, 2490, 4645
+T_SHIFT, T_OWN = (9000, 17200), 17000
+RLAT, GA, SC, PEC, LAT, VF, PASSES = 2500.0, 1.45, 3.5, 0.43, 240.0, 0.0, 6
 
-SLOTS = ["n", "nm1", "th16", "bound", "SB", "NE", "j", "nd0", "jp", "t1", "back", "mx", "H2", "S2", "C2", "mB", "none",
-         "dl", "dm", "as1", "bs1", "prop", "z1", "z2", "w1", "win", "e1", "g1", "fd", "fd2", "go", "go2", "de", "df", "hv", "fv", "f1", "h1",
-         "lt14", "TRL", "LT", "CF0", "CF1", "col", "OH0", "OH1", "OH2", "OH3", "OH4", "SC0", "SC1", "SC2", "SC3", "SC4",
-         "D0", "D1", "D2", "D3", "TD0", "TD1", "TD2", "TD3", "TR0", "TR1", "TR2", "TR3", "L0", "L1", "L2", "L3", "G8"]
+SLOTS = ["N2", "N3", "th", "bnd", "mx", "back", "none", "dm", "dm2", "AS0", "AS1", "CF0", "CF1", "col", "G8", "P4", "W8", "E16", "R16"]
 SL = {k: 16 * i for i, k in enumerate(SLOTS)}
-COLS = {"PM": 0, "PAR0": 1, "PAR1": 2, "GRP": 3, "NZ": 4, "PN0": 5, "PN1": 6, "ODD": 7, "ACT": 8, "A128": 9}
+COLS = {k: i for i, k in enumerate(("PM", "GRP", "PM4", "P3", "P7", "EVN", "ODD", "T0", "T1", "ACT", "A8", "THR", "WC", "C17", "C16", "P"))}
 
 F32, BF, F16, I32, U16 = "float32", "bfloat16", "float16", "int32", "uint16"
 SB = {
-    "X": ([4032], BF), "CH": ([NV], I32), "CP": ([NV], I32), "XO": ([NV], BF), "IOT": ([NV], F32),
-    "SM": ([16 * len(SLOTS)], F32), "SI": ([64], I32), "WI": ([512], I32), "WF": ([16, 2, 16], F32), "WL": ([512], F32),
-    "KM": ([128], F32), "KIO": ([256], F32), "TM1": ([512], F16), "P3": ([16, 16], F32), "CF": ([256], F16),
-    "ID": ([128], BF), "NI": ([128], BF), "BI": ([128], BF), "IH": ([128], F16), "ONES": ([128], BF),
-    "W16": ([144], BF), "W1": ([144], BF), "TRI": ([2048], BF), "ZM": ([512], F16), "DM": ([512], F16), "ZF": ([512], F32),
-    "KB": ([256], BF), "RSTB": ([256], F32), "K1": ([256], F32), "IO2": ([512], F32), "KC": ([256], F32),
-    "BCL": ([32], U16), "REP": ([8], U16), "APL": ([16], U16),
-    "P1": ([272], F32), "PU": ([256], U16), "VAL": ([256], F32), "INV": ([256], F32), "PEN": ([512], F32),
-    "RUN": ([256], F32), "NE1": ([256], F32), "DA": ([256], F32), "DB": ([256], F32), "UAB": ([512], F32),
-    "ABU": ([32], U16), "ROW": ([512], F16), "EQ": ([8704], BF), "ACCS": ([256], BF), "WINB": ([16], BF),
-    "XA": ([256], BF), "XS": ([256], BF), "XR": ([256], F32), "NEG": ([256], BF), "YS": ([1280], F16),
-    "VG": ([4096], BF), "A1": ([4096], BF), "A2": ([16, 16, 16], BF), "Y2": ([512], BF),
-    "EU": ([16], U16), "FU": ([16], U16), "CU": ([256], U16), "C16": ([8, 2, 16], F16), "N16": ([8, 2, 16], F16),
-    "DC": ([256], F32), "PO": ([16, 24], F32), "PEV": ([16, 28], F32), "EQH": ([1792], BF),
-    "UF": ([256], F32), "UE": ([256], F32), "MK": ([256], F32), "UP": ([256], F32),
+    "X": ([2 * WIN], BF), "CH": ([TRASH], I32), "CP": ([TRASH], I32), "XO": ([NV], BF), "IOT": ([TRASH], F32),
+    "SM": ([16 * len(SLOTS)], F32), "SI": ([16], I32), "WI": ([256], I32), "WH": ([256], F16), "NT": ([512], I32),
+    "NF": ([512], F32), "WL": ([256], F32), "WN": ([256], F32),
+    "KM": ([128], F32), "T17": ([272], F32), "V1": ([136], F32), "K16": ([128], F32), "H4": ([64], F32), "GI": ([64], F32),
+    "TRF": ([32], F32), "SCN": ([48], F32), "RR": ([128], F32), "TA": ([136], F32), "TB": ([136], F32),
+    "ID": ([128], BF), "NI": ([128], BF), "BI": ([128], BF), "CI": ([128], BF), "VI": ([128], BF), "ONES": ([128], BF),
+    "IH": ([128], F16), "NH": ([128], F16), "IF": ([128], F32), "HALF": ([128], BF), "ZERO": ([272], BF),
+    "W16": ([32], BF), "DM": ([272], F16), "KB": ([656], BF), "RSTB": ([136], F32), "RST1": ([257], BF), "RSM": ([128], BF),
+    "K2": ([256], F32), "ZM": ([64], F32), "ZN": ([32], F32), "R4": ([32], F16), "G64": ([64], F32), "GW": ([576], BF),
+    "RS2": ([256], F32), "TRA": ([32], F16), "NEG": ([256], BF), "BIG": ([256], BF),
+    "LZ": ([2], U16), "LE": ([2], U16), "LA": ([4], U16), "LR": ([4], U16), "L8": ([2], U16), "REP": ([4], U16), "BCL": ([8], U16),
+    "APL": ([16], U16), "EQ": ([128 * 48], BF), "ROW": ([512], F16), "ABU": ([32], U16),
+    "PU": ([256], U16), "VG": ([8 * 520], BF), "A2": ([4096], BF), "Y2": ([512], BF), "CU": ([256], U16), "CF": ([256], F16),
+    "LST": ([16], U16), "EQH": ([14 * 136], BF), "XA": ([256], BF), "XS": ([256], BF), "XR": ([256], F32),
+    "CAP": ([32], BF), "TOP": ([32], BF), "GO": ([32], BF), "NB": ([16], BF), "DL": ([16], F16), "WM": ([128], BF),
+    "BM": ([128], F32), "PR": ([128], F32), "TP": ([128], F32), "RSD": ([256], F32), "DAB": ([128], F32),
+    "RUN": ([272], F32), "NE1": ([272], F32), "MX": ([512], F32), "UE": ([256], F32), "OH": ([96], F32),
 }
+for _h in range(2):
+    for _k, _v in (("P", ([144], F16)), ("U1", ([128], F16)), ("U2", ([130], F16)), ("UF", ([544], F32)), ("UAB", ([256], F32)),
+                   ("RI", ([400], BF)), ("RO", ([400], BF)), ("INV", ([128], BF)), ("MK", ([128], BF)), ("M", ([256], F32)),
+                   ("PO", ([8, 26], F16)), ("PEV", ([8, 30], F16)), ("YS", ([640], F16)), ("Z", ([260], F16)), ("ZL", ([260], F16))):
+        SB[_k + str(_h)] = _v
 for _r in range(ROUNDS):
     SB["MID%d" % _r] = ([256], BF)
-    SB["RM%d" % _r] = ([512], BF)
-    SB["LU%d" % _r] = ([64], U16)
-    SB["RL%d" % _r] = ([32], U16)
-SCRATCH = {k: ("sbuf", [128] + v[0], v[1]) for k, v in SB.items()}
+    SB["RM%d" % _r] = ([256], BF)
+    SB["LU%d" % _r] = ([2, 16], U16)
+    SB["RL%d" % _r] = ([2, 16], U16)
+POOL = {}
+for _k in ("KM", "T17", "V1", "K16", "H4", "GI", "TRF", "SCN", "RR", "TA", "TB", "IF", "RSTB", "ZM", "ZN", "G64", "K2", "RS2", "ID", "NI",
+           "BI", "CI", "VI", "ONES", "HALF", "ZERO", "W16", "KB", "RST1", "RSM", "GW", "NEG", "BIG", "IH", "NH", "DM", "R4", "TRA",
+           "LZ", "LE", "LA", "LR", "L8", "REP", "BCL", "APL"):
+    _n = "K" + SB[_k][1]
+    _at = SB.get(_n, ([0], 0))[0][0]
+    POOL[_k] = (_n, _at)
+    SB[_n] = ([_at + (SB[_k][0][0] + 15) // 16 * 16], SB[_k][1])
+SCRATCH = {k: ("sbuf", [128] + v[0], v[1]) for k, v in SB.items() if k not in POOL}
+SHAPE = {k: v for k, v in SB.items()}
 for _r in range(2):
-    SCRATCH["pZ%d" % _r] = ("psum", [128, 16, 2, 16], F32)
+    SCRATCH["pZ%d" % _r] = ("psum", [128, 512], F32)
     SCRATCH["pE%d" % _r] = ("psum", [128, 512], F32)
 for _r in range(4):
     SCRATCH["pD%d" % _r] = ("psum", [128, 32, 16], F32)
-SEMAPHORES = ["sV", "sS", "sP", "sG"] + ["d%d" % i for i in range(24)] + ["r%d" % i for i in range(12)]
+for _k, _v in SCRATCH.items():
+    SHAPE[_k] = (_v[1][1:], _v[2])
+SEMAPHORES = ["sV", "sS", "sP", "sG"] + ["d%d" % i for i in range(24)] + ["r%d" % i for i in range(16)]
 OP = AluOpType
 AF = ActivationFunctionType
 ALL = slice(None)
@@ -58,8 +80,7 @@ EXT = {}
 PLAN = {}
 
 
-def order_calls(ops):
-    n = len(ops)
+def find_waits(ops):
     acc = {}
     hard = [set() for _ in ops]
     soft = [set() for _ in ops]
@@ -77,54 +98,78 @@ def order_calls(ops):
                     if kind != "acc" or k2 != "acc":
                         soft[i].add(j)
                 elif (m & m2) and (kind != "rd" or k2 != "rd"):
-                    if same and k2 == "rd" and not SAMEQ:
-                        soft[i].add(j)
-                    else:
-                        hard[i].add(j)
+                    hard[i].add(j)
         for (nm, kind, m) in mine:
             lst = acc.setdefault(nm, [])
             if kind == "wr" and nm[0] != "p":
                 lst[:] = [e for e in lst if e[2] & ~m]
+            if nm[0] == "p" and lst and ops[lst[-1][0]]["q"] != o["q"]:
+                last = ops[lst[-1][0]]["q"]
+                k = len(lst)
+                while k and ops[lst[k - 1][0]]["q"] == last:
+                    k -= 1
+                del lst[:k]
             lst.append((i, kind, m))
-    succ = [[] for _ in ops]
-    left = [0] * n
+    return hard, soft
+
+
+def place(ops, before, key, head):
+    n = len(ops)
+    after = [[] for _ in ops]
+    left = [len(b) for b in before]
     for i in range(n):
-        for j in hard[i] | soft[i]:
-            succ[j].append(i)
-            left[i] += 1
-    prio = [0.0] * n
+        for j in before[i]:
+            after[j].append(i)
+    rdy = list(head)
+    start = [0.0] * n
+    busy = {}
+    ready = sorted((key[i], i) for i in range(n) if not left[i])
+    while ready:
+        i = ready.pop(0)[1]
+        cost = ops[i]["cost"]
+        line = busy.setdefault(ops[i]["q"], [])
+        t = rdy[i]
+        k = len(line)
+        while k and line[k - 1][1] > t:
+            k -= 1
+        while k < len(line) and line[k][0] < t + cost:
+            t = max(t, line[k][1])
+            k += 1
+        line.insert(k, (t, t + cost))
+        start[i] = t
+        fresh = False
+        for m in after[i]:
+            rdy[m] = max(rdy[m], t + cost + before[m][i])
+            left[m] -= 1
+            if not left[m]:
+                ready.append((key[m], m))
+                fresh = True
+        if fresh:
+            ready.sort()
+    return start
+
+
+def order_calls(ops):
+    n = len(ops)
+    hard, soft = find_waits(ops)
+    fore = [{j: (ops[j]["lat"] + LAT if j in hard[i] else 0.0) for j in hard[i] | soft[i]} for i in range(n)]
+    back = [{} for _ in ops]
+    for i in range(n):
+        for j, d in fore[i].items():
+            back[j][i] = d
+    key = [o["t"] for o in ops]
     for i in range(n - 1, -1, -1):
-        if ops[i]["inorder"]:
-            prio[i] = -10.0 * (i + ops[i].get("late", 0))
-        else:
-            prio[i] = max([prio[k] for k in succ[i]] + [-10.0 * n]) + 1.0e-4 * (ops[i]["cost"] + ops[i]["lat"])
-    rdy = [0.0] * n
-    ready = {}
-    for i in range(n):
-        if not left[i]:
-            ready.setdefault(ops[i]["q"], []).append(i)
-    free = {}
-    order = []
-    while len(order) < n:
-        best = None
-        for q in sorted(ready):
-            if ready[q]:
-                f = free.get(q, 0.0)
-                s0 = max(f, min(rdy[i] for i in ready[q]))
-                i = max((i for i in ready[q] if rdy[i] <= s0 + SLACK), key=lambda k: (prio[k], -k))
-                st = max(f, rdy[i])
-                if best is None or st < best[0]:
-                    best = (st, i)
-        st, i = best
-        o = ops[i]
-        ready[o["q"]].remove(i)
-        free[o["q"]] = st + o["cost"]
-        order.append(i)
-        for k in succ[i]:
-            rdy[k] = max(rdy[k], st + o["cost"] + (o["lat"] + LAT if i in hard[k] else 0.0))
-            left[k] -= 1
-            if not left[k]:
-                ready.setdefault(ops[k]["q"], []).append(k)
+        if not ops[i]["inorder"]:
+            key[i] = min([key[k] - ops[i]["cost"] - d for k, d in back[i].items()] + [1.0e9])
+    best = None
+    for _ in range(PASSES):
+        start = place(ops, fore, key, [0.0] * n)
+        end = max(start[i] + ops[i]["cost"] + ops[i]["lat"] for i in range(n))
+        if best is None or end < best[0]:
+            best = (end, start)
+        late = place(ops, back, [-start[i] - ops[i]["cost"] for i in range(n)], [o["lat"] for o in ops])
+        key = [-late[i] - ops[i]["cost"] for i in range(n)]
+    order = sorted(range(n), key=lambda i: (best[1][i], i))
     pos = {i: t for t, i in enumerate(order)}
     seen = {}
     waits = {}
@@ -132,7 +177,7 @@ def order_calls(ops):
     for i in order:
         o = ops[i]
         waits[i] = []
-        if o["q"] == "R":
+        if o["q"][0] == "R":
             continue
         need = {}
         for j in hard[i]:
@@ -156,30 +201,43 @@ def rank_program(g, core, T, topo):
     rid, pid = topo.addr(mate, core)
     engs = topo.engines(core, mate)
     ops = []
-    cnts = {"d": 0, "r": 0, "main": False}
+    cnts = {"d": 0, "r": 0, "main": False, "t": 0.0, "base": 0.0}
 
-    def A(name, *idx):
+    def A(name, *idx, parts=ALL):
         key = (name, str(idx))
         if key not in EXT:
-            shp = SCRATCH[name][1][1:]
+            shp = SHAPE[name][0]
             ext = np.arange(int(np.prod(shp))).reshape(shp)[tuple(idx)].reshape(-1)
             m = 0
             for e in ext.tolist():
                 m |= 1 << e
             EXT[key] = (m, len(ext))
-        ap = T[name][(ALL,) + tuple(idx)] if idx else T[name][:]
-        return (ap, [(name, EXT[key][0])], EXT[key][1], 4 if SCRATCH[name][2] in (F32, I32) else 2, False)
+        if name in POOL:
+            buf, a0 = POOL[name]
+            ap = T[buf][parts, a0 + idx[0].start:a0 + idx[0].stop:idx[0].step]
+        else:
+            ap = T[name][(parts,) + tuple(idx)]
+        return (ap, [(name, EXT[key][0])], EXT[key][1], 4 if SHAPE[name][1] in (F32, I32) else 2, False)
 
     def c(name, lo=0, hi=None, st=None):
         if hi is None:
-            hi = SCRATCH[name][1][1]
+            hi = SHAPE[name][0][0]
         return A(name, slice(lo, hi, st))
 
-    def s(k, n=1):
-        return c("SM", SL[k], SL[k] + 16 * n)
+    def sl(a, b, st=None):
+        return slice(a, b, st)
+
+    def s(k, n=16):
+        return c("SM", SL[k], SL[k] + n)
+
+    def hs(k, hf):
+        return c("SM", SL[k] + 8 * hf, SL[k] + 8 * hf + 8)
 
     def col(k):
         return c("SM", SL["col"] + COLS[k], SL["col"] + COLS[k] + 1)
+
+    def hc(name, hf, n=128):
+        return c(name, n * hf, n * hf + n)
 
     def ind(win, off):
         return (win[0].indirect(off[0]), win[1] + off[1], 16 * off[2], win[3], True)
@@ -193,7 +251,11 @@ def rank_program(g, core, T, topo):
         for a in outs:
             wr += a[1]
         ops.append({"q": q, "fn": fn, "rd": rd, "wr": wr, "sem": sem, "cost": cost, "lat": lat, "wk": wk, "after": list(after),
-                    "inorder": cnts["main"]})
+                    "inorder": cnts["main"], "t": cnts["t"]})
+        cnts["t"] += 1.0
+
+    def at(t):
+        cnts["t"] = cnts["base"] + t
 
     def p(a):
         return a[0] if isinstance(a, tuple) else a
@@ -201,7 +263,7 @@ def rank_program(g, core, T, topo):
     def vc(o, a, k=1.0):
         if a[4]:
             return 50 + 0.83 * GA * o[2]
-        return 30 + 0.83 * max(64, o[2] * k * (0.5 if o[3] == 2 and a[3] == 2 else 1.0))
+        return VF + 0.83 * max(64, o[2] * k * (0.5 if o[3] == 2 and a[3] == 2 else 1.0))
 
     def cp(o, i):
         add("V", lambda: g.vector.tensor_copy(o[0], i[0]), [o], [i], vc(o, i))
@@ -219,25 +281,30 @@ def rank_program(g, core, T, topo):
         else:
             add("V", lambda: g.vector.tensor_scalar(o[0], a[0], p(s1), p(s2), op0, op1), [o], [a, s1, s2], vc(o, a))
 
-    def scan(o, d0, d1, op0, op1):
-        add("V", lambda: g.vector.tensor_tensor_scan(o[0], d0[0], d1[0], 0.0, op0, op1), [o], [d0, d1], vc(o, d0))
+    def scan(o, d0, d1, op0, op1, init=0.0):
+        add("V", lambda: g.vector.tensor_tensor_scan(o[0], d0[0], d1[0], p(init), op0, op1), [o], [d0, d1, init],
+            VF + 0.83 * max(64, o[2] * (0.5 if o[3] == d0[3] == d1[3] == 2 else 1.0)))
 
-    def tr(o, i):
-        add("V", lambda: g.vector.transpose(o[0], i[0]), [o], [i], vc(o, i))
+    def rsum(o, i):
+        add("V", lambda: g.vector.tensor_reduce(o[0], i[0], AxisListType.X, OP.add), [o], [i], vc(i, o))
 
     def ms(o, v):
         add("V", lambda: g.vector.memset(o[0], v), [o], [], vc(o, o))
 
     def act(o, i, f=AF.Identity, bias=0.0, scale=1.0):
         add("S", lambda: g.scalar.activation(o[0], i[0], f, bias=p(bias), scale=p(scale)), [o], [i, bias, scale],
-            65 + 0.83 * GA * o[2] if i[4] else 40 + 0.83 * max(64, o[2]))
+            65 + 0.83 * GA * o[2] if i[4] else VF + 0.83 * max(64, o[2]))
 
     def sfill(o, v):
-        act(o, c("KIO", 0, o[2]) if o[2] <= 256 else c("X", 0, o[2]), AF.Identity, v, 0.0)
+        act(o, c("T17", 0, o[2]), AF.Identity, v, 0.0)
 
     def mm(o, l, r, st, sp):
-        add("P", lambda: g.tensor.matmul(o[0], l[0], r[0], st, sp), [o], [l, r], PEC * max(64, o[2]) * (4 if l[3] == 4 else 1),
-            wk="wr" if st or sp else "acc")
+        add("P", lambda: g.tensor.matmul(o[0], l[0], r[0], st, sp), [o], [l, r],
+            PEC * max(min(64, l[2]), o[2]) * (4 if l[3] == 4 else 1), wk="wr" if st or sp else "acc")
+
+    def group(terms):
+        for k, (o, l, r) in enumerate(terms):
+            mm(o, l, r, k == 0, k == len(terms) - 1)
 
     def iota(o, pat, base, cm, fl=True):
         if fl:
@@ -248,11 +315,11 @@ def rank_program(g, core, T, topo):
     def gcp(o, i):
         add("G", lambda: g.affine_select(o[0], i[0], [[0, o[2]]], OP.is_ge, 0.0, 0, 0), [o], [i], 170 + 1.66 * o[2])
 
-    def dma(o, i, nbytes, after=()):
+    def dma(o, i, nbytes):
         k = "d%d" % cnts["d"]
         cnts["d"] += 1
         add("Y", lambda: g.sync.dma_start(p(o), p(i)).then_inc(T.sem[k], 16), [o] if isinstance(o, tuple) else [], [i], 60.0,
-            (k, 16), 2000 + nbytes / 200.0, after=after)
+            (k, 16), 2000 + nbytes / 200.0)
 
     def send(dst, src, use=engs[:len(engs) // 2]):
         neng = len(use)
@@ -261,417 +328,506 @@ def rank_program(g, core, T, topo):
         r = "r%d" % cnts["r"]
         cnts["d"] += 1
         cnts["r"] += 1
-        t = 128 * src[2] * src[3] / 80.0
-        add("G", lambda: g.remote_dma(dst[0], src[0], T.sem[r], T.sem[k], pid, rid, emask), [], [src], 300.0, (k, neng), RLAT)
-        add("R", None, [dst], [], t, (r, neng), 0.0, after=[len(ops) - 1])
+        t = 128 * src[2] * src[3] / (12.0 * neng)
+        add("G", lambda: g.remote_dma(dst[0], src[0], T.sem[r], T.sem[k], pid, rid, emask), [], [src], 300.0, (k, neng), RLAT - LAT)
+        add("R%d" % emask, None, [dst], [], t, (r, neng), 0.0, after=[len(ops) - 1])
 
-    def bc(k, n=1):
-        return ind(s(k, n), c("BCL", 0, 16 * n))
-
-    def turn(src, b0, mat, zh):
-        for h in range(2):
-            for rh in range(2):
-                mm(A("pZ0", slice(8 * zh, 8 * zh + 8), h), c(mat, (2 * h + rh) * 128, (2 * h + rh + 1) * 128),
-                   A(src, slice(b0, b0 + 8), rh), rh == 0, rh == 1)
-
-    HOME, PART = c("X", 0, NV), c("X", NV, 2 * NV)
-    K256 = c("KIO")
-    P1 = c("P1", 0, 256)
-    G8 = c("SM", SL["G8"], SL["G8"] + 8)
-    CF8 = c("SM", SL["CF0"], SL["CF0"] + 8)
+    HOME, PART = c("X", 0, WIN), c("X", WIN, 2 * WIN)
+    ID, IH, NH = c("ID"), c("IH"), c("NH")
+    G8, CF8 = s("G8", 8), s("CF0", 8)
+    P8 = sl(0, 8)
 
     H = NV // 2
     for k in range(2):
-        dma(c("X", k * H, k * H + H), T.pts[:, k * H:k * H + H], 256 * H)
-    ms(c("WI", 256, 512), 0)
-    zero = len(ops) - 1
-    dma(c("WI", 0, 256), T.way[:], 131072)
-    dma((T.WI[0:128:16, 256:512], [("WI1", 1)]), T.cnt[:], 8192, [zero])
-    dma((T.WI[1:128:16, 256:512], [("WI2", 1)]), T.th[:], 8192, [zero])
-    dma(c("CH"), T.cand[:], 512 * NV)
+        dma(c("X", OFF + k * H, OFF + k * H + H), T.pts[:, k * H:k * H + H], 256 * H)
+    dma(c("WI"), T.way[:], 131072)
+    dma(A("NT", sl(0, 256), parts=P8), T.cnt[:], 8192)
+    dma(A("NT", sl(256, 512), parts=P8), T.th[:], 8192)
+    dma(c("CH", OFF), T.cand[:], 512 * NV)
+    iota(c("T17"), [[0, 16], [1, 17]], 0, 0)
     iota(c("KM"), [[-1, 128]], 0, 1)
     iota(c("SI", 0, 2), [[0, 2]], 0, 1, False)
-    iota(s("CF0", 2), [[1, 32]], 0, 0)
-    iota(K256, [[0, 16], [1, 16]], 0, 0)
+    iota(s("CF0", 32), [[1, 32]], 0, 0)
+    iota(c("K16"), [[0, 8], [1, 16]], 0, 0)
+    iota(c("V1"), [[-16, 8], [-1, 17]], 0, 1)
+    iota(c("H4"), [[0, 16], [1, 4]], 0, 0)
     for k in range(2):
-        send(c("X", NV + k * H, NV + k * H + H), c("X", k * H, k * H + H), engs)
-    send(c("CP"), c("CH"), engs[len(engs) // 2:])
-    iota(c("IOT"), [[1, NV]], 1, 0)
-    ops[-1]["after"] = [len(ops) - 5]
+        send(c("X", WIN + OFF + k * H, WIN + OFF + k * H + H), c("X", OFF + k * H, OFF + k * H + H), engs)
+    send(c("CP", OFF), c("CH", OFF), engs[len(engs) // 2:])
+    sent = len(ops) - 4
+    ops[-2]["after"] = [sent + 1]
+    for o, pat, base in ((c("GI"), [[0, 2], [1, 8], [0, 4]], 0), (c("TRF"), [[128, 2], [0, 2], [16, 8]], TRASH),
+                         (c("IOT"), [[1, TRASH]], 0), (c("SCN"), [[1, 6], [0, 8]], 0)):
+        iota(o, pat, base, 0)
 
     PI = c("SI", 0, 1)
-    ts(c("SI", 2, 3), PI, 15, OP.bitwise_and)
-    ts(c("SI", 3, 4), PI, 4, OP.logical_shift_right, 1, OP.bitwise_and)
-    ts(c("SI", 4, 5), PI, 4, OP.logical_shift_right)
-    ts(c("SI", 5, 6), PI, 1, OP.bitwise_and)
-    cp(col("PM"), c("SI", 2, 3))
-    cp(col("PAR1"), c("SI", 3, 4))
-    cp(col("GRP"), c("SI", 4, 5))
-    ts(col("ODD"), c("SI", 5, 6), 16.0, OP.mult)
-    ts(col("PAR0"), col("PAR1"), -1.0, OP.mult, 1.0, OP.add)
-    ts(col("NZ"), col("PM"), 0.0, OP.is_gt)
-    cp(c("BCL"), s("CF0", 2))
-    act(col("PN0"), col("PAR0"), AF.Identity, 0.0, col("NZ"))
-    act(col("PN1"), col("PAR1"), AF.Identity, 0.0, col("NZ"))
-    for h in range(2):
-        for rh in range(2):
-            k = 2 * h + rh
-            ts(c("ZF", 128 * k, 128 * k + 128), c("KM"), 16.0 * (h - rh), OP.is_equal, col("PAR%d" % h), OP.mult)
-            ts(c("TM1", 128 * k, 128 * k + 128), c("KM"), 16.0 * (h - rh) + 1.0, OP.is_equal, col("PN%d" % h), OP.mult)
-    cp(A("WF"), (T.WI[:], c("WI")[1] + [("WI1", 1), ("WI2", 1)], 512, 4, False))
-    turn("WF", 0, "ZF", 0)
-    turn("WF", 8, "ZF", 1)
-    tr(c("WL"), A("pZ0"))
-    ts(c("ID"), c("KM"), 0.0, OP.is_equal)
-    ts(c("IH"), c("KM"), 0.0, OP.is_equal)
-    act(c("NI"), c("ID"), AF.Identity, 0.0, -1.0)
-    act(c("BI"), c("ID"), AF.Identity, 0.0, B17)
-    sfill(c("W16"), 0.0)
-    sfill(c("W1"), 0.0)
-    sfill(c("P1", 256, 272), 0.0)
+    for k, (a, b) in enumerate(((0, 15), (4, 7), (2, 3), (0, 3), (0, 7), (0, 1))):
+        ts(c("SI", 2 + k, 3 + k), PI, a, OP.logical_shift_right, b, OP.bitwise_and)
+    cp(c("SM", SL["col"], SL["col"] + 6), c("SI", 2, 8))
+    cp(col("P"), PI)
+    act(col("ODD"), col("EVN"), AF.Identity, 0.0, float(WIN))
+    act(col("C17"), col("PM4"), AF.Identity, 16.0, 17.0)
+    act(col("C16"), col("PM4"), AF.Identity, 15.0, 16.0)
+    for hf in range(2):
+        act(col("T%d" % hf), col("P"), AF.Identity, TRASH + 128.0 * hf)
+    ts(c("PU"), c("WI"), col("ODD"), OP.add, float(OFF), OP.add)
+    ts(c("WH"), c("WI"), float(OFF), OP.add)
+    cp(A("NF", ALL, parts=P8), A("NT", ALL, parts=P8))
+    ts(c("IF"), c("KM"), 0.0, OP.is_equal)
+    for name, v in (("ID", 1.0), ("NI", -1.0), ("BI", B17), ("CI", 65536.0), ("VI", -4096.0)):
+        act(c(name), c("IF"), AF.Identity, 0.0, v)
+    cp(IH, c("IF"))
+    ts(NH, c("IF"), -1.0, OP.mult)
     ts(G8, CF8, col("GRP"), OP.is_equal)
-    act(c("KB"), K256)
-    act(c("W16", 15, 128, 16), G8, AF.Identity, 0.0, 16.0)
-    act(c("W1", 15, 128, 16), G8)
-    cp(s("n"), c("WL", 256, 512, 16))
-    act(s("bound"), c("WL", 257, 512, 16), AF.Identity, 0.0, 16.0)
-    act(s("th16"), c("WL", 257, 512, 16), AF.Identity, 0.0, 16.0)
-    act(c("UP"), c("WL", 0, 256), AF.Identity, 1.0)
-    tt(c("VAL"), bc("n"), K256, OP.is_gt)
-    act(s("NE"), s("n"), AF.Identity, 0.0, -B17)
-    sfill(s("SB"), 0.0)
-    tt(P1, c("UP"), c("VAL"), OP.mult)
-    act(c("IO2", 0, 256), K256, AF.Identity, 0.0, B17)
-    act(c("IO2", 256, 512), K256, AF.Identity, -2.0 * B17, -B17)
+    act(c("W16", 0, 8), G8, AF.Identity, 0.0, 16.0)
+    for k in range(3):
+        act(c("W16", 8 + 8 * k, 16 + 8 * k), G8, AF.Identity, 0.0, (-16.0 if k else 16.0) * U18)
+    sfill(c("X", 0, OFF), BIGH)
+    sfill(c("X", WIN, WIN + OFF), BIGP)
+    sfill(c("X", TRASH, WIN), 0.0)
+    sfill(c("X", WIN + TRASH), 0.0)
+    ms(c("CH", 0, OFF), -OFF)
+    ms(c("CP", 0, OFF), -OFF)
+    sfill(c("VG", 512, 8 * 520, 520), 0.0)
+    act(c("KB", 0, 272), c("T17"))
+    sfill(c("KB", 136, 272, 17), 65536.0)
+    act(c("KB", 272, 400), c("K16"), AF.Identity, 0.0, U18)
+    sfill(c("KB", 286, 400, 16), 1.0)
+    sfill(c("KB", 400, 656), 129.0)
+    sfill(c("KB", 415, 656, 16), 0.0)
+    ts(c("RSTB"), c("T17", 0, 136), 0.0, OP.is_equal, 1.0e9, OP.mult)
+    for k in range(2):
+        ts(hc("RS2", k), c("K16"), 0.0, OP.is_equal, 1.0e9, OP.mult)
+    act(c("RSD"), c("RS2"))
+    act(c("RSM"), c("K16"), AF.Sign)
+    sfill(c("RST1"), 1.0)
+    sfill(c("RST1", 1, 128, 16), -1.0)
+    sfill(c("RST1", 0, 256, 16), 0.0)
+    act(c("K2", 0, 128), c("K16"), AF.Identity, 0.5)
+    act(c("K2", 128, 256, 2), c("K16", 0, 128, 2), AF.Identity, 1.0, 0.5)
+    act(c("K2", 129, 256, 2), c("K16", 1, 128, 2), AF.Identity, 1.5, 0.5)
+    sfill(c("K2", 0, 128, 16), -0.5)
+    sfill(c("K2", 15, 256, 16), -99.0)
+    for name, v in (("NEG", BIGP), ("BIG", BIGH), ("ONES", 1.0), ("HALF", -0.5), ("ZERO", 0.0)):
+        sfill(c(name), v)
+    ts(c("TA"), c("V1"), -1.0, OP.is_equal)
+    ts(c("TB"), c("V1"), 0.0, OP.is_equal)
+    sfill(c("TA", 0, 136, 17), 0.0)
+    sfill(c("TB", 16, 136, 17), 0.0)
+    cp(c("DM", 0, 136), c("TA"))
+    tt(c("DM", 136, 272), c("TA"), c("TB"), OP.subtract)
+    ts(c("ZM"), c("H4"), col("PM4"), OP.is_equal)
+    act(c("ZN"), c("ZM", 0, 32), AF.Identity, -1.0)
+    ts(s("P4", 4), s("CF0", 4), col("P3"), OP.is_equal)
     for k in range(4):
-        sfill(c("TRI", 512 * k, 512 * k + 512), 0.0)
-    for k in range(8):
-        sfill(c("A1", 512 * k + 496, 512 * k + 512), 0.0)
-    sfill(c("DA"), 0.0)
-    sfill(c("DB"), 0.0)
-    sfill(c("ACCS", 0, 16), 0.0)
-    sfill(c("NEG"), BIGP)
-    sfill(c("ONES"), 1.0)
-    sfill(c("X", 2 * NV, 4032), 0.0)
-    for r in range(ROUNDS):
-        sfill(c("RM%d" % r, 256, 512), BIGH)
-    for k in range(5):
-        sfill(s("SC%d" % k), 2.0 * k * B17)
-    ts(c("RSTB"), K256, 0.0, OP.is_equal, 1.0e9, OP.mult)
-    cp(c("ZM"), c("ZF"))
-    tt(c("DM"), c("ZM"), c("TM1"), OP.subtract)
-    ts(s("LT"), s("CF0"), col("PM"), OP.is_gt)
-    act(s("TRL"), s("CF0"), AF.Identity, col("PM"), 16.0)
-    ts(c("REP"), CF8, 0.0, OP.mult, col("PM"), OP.add)
-    ts(c("APL"), s("CF0"), col("ODD"), OP.add)
-    for ll in range(16):
-        act(c("TRI", 129 * ll, 128 * ll + 128, 16), G8, AF.Identity, 0.0, c("SM", SL["LT"] + ll, SL["LT"] + ll + 1))
-    t1, t2 = 2.0 * NV, 2.0 * NV + 256
-    for k, (trash, off) in enumerate(((t1, NV), (t2, 0), (t1, 0), (t1, NV))):
-        act(s("TR%d" % k), s("TRL"), AF.Identity, trash)
-        act(s("TD%d" % k), s("TRL"), AF.Identity, trash - off + 1.0)
-    act(c("K1"), K256, AF.Identity, 1.0)
-    act(c("KC", 0, 256, 2), c("KIO", 0, 256, 2), AF.Identity, -1.0)
-    act(c("KC", 1, 256, 2), c("KIO", 1, 256, 2))
-    ms(A("N16"), 0.0)
+        ts(c("R4", 8 * k, 8 * k + 8), G8, c("SM", SL["P4"] + k, SL["P4"] + k + 1), OP.mult)
+    ts(c("LZ"), s("CF0", 2), 68.0, OP.mult, col("C17"), OP.add)
+    ts(c("LE"), s("CF0", 2), 64.0, OP.mult, col("C16"), OP.add)
+    ts(c("LA"), s("CF0", 4), 64.0, OP.mult, col("C16"), OP.add)
+    ts(c("LA"), c("LA"), -1.0, OP.add)
+    for k in range(2):
+        cp(hc("LR", k, 2), c("LA", 0, 2))
+    cp(c("BCL"), CF8)
+    ts(c("L8"), s("CF0", 2), 4.0, OP.mult, col("PM4"), OP.add)
+    act(col("P7"), col("P7"), AF.Identity, 15.0, 16.0)
+    ts(c("REP"), s("CF0", 4), 0.0, OP.mult, col("P7"), OP.add)
+    act(col("EVN"), col("EVN"), AF.Identity, 152.0, -136.0)
+    ts(c("APL", 0, 8), CF8, 17.0, OP.mult, col("EVN"), OP.add)
+    for hf in range(2):
+        h = str(hf)
+        ms(c("P" + h, 128), 0.0)
+        ms(c("U2" + h, 0, 2), 0.0)
+        ms(c("Z" + h), 0.0)
+        ms(c("ZL" + h), 0.0)
+        sfill(c("RI" + h, 0, 144), 0.5)
+        sfill(c("RI" + h, 144, 272), -0.5)
+        sfill(c("RI" + h, 272, 400), 0.5)
+        sfill(c("RI" + h, 144, 272, 16), 0.0)
+    sfill(c("TA", 0, 128), 1.0 / 3.0)
+    scan(c("RR"), c("TA", 0, 128), c("ZERO", 0, 128), OP.mult, OP.add, 3.0 ** 61)
+    tt(c("TB", 0, 128), c("RR"), c("IF"), OP.mult)
+    rsum(col("THR"), c("TB", 0, 128))
+    ts(s("E16"), s("CF0"), col("PM"), OP.is_equal, 3.0 ** 16, OP.mult)
+    tt(s("R16"), s("E16"), c("RR", 0, 16), OP.mult)
+    rsum(col("WC"), s("R16"))
+    sfill(s("E16", 8), 3.0 ** -16)
+    scan(s("W8", 8), s("E16", 8), c("ZERO", 0, 8), OP.mult, OP.add, col("WC"))
+    ts(c("G64"), c("GI"), col("GRP"), OP.is_equal)
+    for lh in range(8):
+        act(c("GW", 64 * lh, 64 * lh + 64), c("G64"), AF.Identity, 0.0, c("SM", SL["W8"] + lh, SL["W8"] + lh + 1))
+    act(c("GW", 512, 576), c("G64"), AF.Identity, 0.0, FAR)
+    ts(c("TRA"), c("TRF"), col("PM"), OP.add)
 
-    def sel(w, ll):
-        return c(w, 15 - ll, 143 - ll)
+    def path(hf, lo=0):
+        return c("P%d" % hf, lo, lo + 128)
 
-    def to_list(lst, name, lo, st, half=None):
-        for hf in (0, 1) if half is None else (half,):
-            for rh in range(2):
-                a = lo + st * (8 * hf + rh)
-                ts(c(lst, 8 * hf + 4 * rh, 8 * hf + 4 * rh + 4), c(name, a, a + 6 * st + 1, 2 * st), -1.0, OP.add)
+    def spread(z, n, win, lst, mask):
+        tt(c(z, 3, 128 * n, 4), ind(win, c(lst, 0, 2 * n)), mask, OP.mult)
 
-    def penalty():
-        tt(c("PEN"), bc("SB", 2), c("IO2"), OP.subtract)
+    def turn(pz, z, n, more=()):
+        group([(c(pz, LI + 8 * e, LI + 8 * e + 8), c(z, 128 * e + 3 - k, 128 * e + 131 - k), c("R4", 8 * k, 8 * k + 8))
+               for e in range(n) for k in range(4)] + list(more))
 
-    def last_point():
-        act(c("INV"), c("VAL"), AF.Identity, 1.0, -1.0)
-        scan(c("UE", 0, 256), c("INV"), P1, OP.mult, OP.add)
-        to_list("EU", "UE", 15, 16)
-        act(s("e1"), c("UE", 15, 256, 16))
+    def to_list(hf, win, lst, t):
+        at(t)
+        spread("Z%d" % hf, 1, win, lst, c("ZM", 0, 32))
+        at(t + 330)
+        turn("pZ%d" % hf, "Z%d" % hf, 1)
+        at(t + 680)
+        cp(hc("LST", hf, 8), c("pZ%d" % hf, LI, LI + 8))
 
-    def hs(k, hf):
-        return c("SM", SL[k] + 8 * hf, SL[k] + 8 * hf + 8)
+    def new_path(hf, terms, t):
+        h = str(hf)
+        pz = "pZ" + h
+        scan(c("RO" + h, 272), c("RSM"), c("RI" + h, 272), OP.mult, OP.add)
+        ts(c("INV" + h), c("RO" + h, 272), 0.75, OP.is_gt)
+        group(terms + [(c(pz, 0, 128), c("VI"), c("INV" + h))])
+        ts(path(hf), c(pz, 0, 128), 0.0, OP.max)
+        scan(hc("UE", hf), c("INV" + h), path(hf), OP.mult, OP.add)
+        to_list(hf, hc("UE", hf), "LE", t)
+        for k in range(2):
+            act(c("CAP", 16 * hf + 8 * k, 16 * hf + 8 * k + 8), hs("N2", hf), AF.Sign, 6.5 - k, -1.0)
+        for k in range(4):
+            gcp(A("PO" + h, ALL, sl(6 * k, 6 * k + 8)), c("P" + h, 1, 128, 2))
+        for k in range(4):
+            gcp(A("PEV" + h, ALL, sl(7 * k, 7 * k + 8)), c("P" + h, 0, 128, 2))
+        at(t + 9000)
+        act(c("MK" + h), c("RO" + h, 272), AF.Abs, -1.25)
+        ts(c("MK" + h), c("MK" + h), 0.5, OP.is_lt)
 
-    def hc(name, hf, o=0):
-        return c(name, o + 128 * hf, o + 128 * hf + 128)
+    def first_path(hf):
+        h = str(hf)
+        pz = "pZ" + h
+        group([(c(pz, NN + 8 * k, NN + 8 * k + 8), A("NF", sl(256 * k + 128 * hf, 256 * k + 128 * hf + 128), parts=P8),
+                A("IF", P8, parts=P8)) for k in range(2)])
+        act(hs("N2", hf), c(pz, NN, NN + 8), AF.Identity, -0.5, 0.5)
+        act(hs("th", hf), c(pz, NN + 8, NN + 16), AF.Identity, 0.0, 16.0 * U18)
+        act(hs("bnd", hf), hs("th", hf))
+        act(c("RI" + h, 272, 400, 16), hs("N2", hf), AF.Identity, 0.5, -1.0)
+        new_path(hf, [(c(pz, 0, 128), hc("WH", hf), IH)], 0.0)
 
-    def ends(name, hf):
-        return c(name, 128 * hf + 15, 128 * hf + 128, 16)
+    def uf_end(hf, slot):
+        return c("UF%d" % hf, 136 * slot + 16, 136 * slot + 136, 17)
 
-    def edges(hf):
-        a, b = 128 * hf, 128 * hf + 128
-        pe = "pE%d" % hf
-        ts(c("PU", a, b, 2), c("P1", a, b, 2), -1.0, OP.add)
-        ts(c("PU", a + 1, b, 2), c("P1", a + 1, b, 2), 1.0, OP.max, NV - 1.0, OP.add)
-        mm(c(pe, 0, 128), c("ID"), c("KB", 0, 128), True, False)
-        for k in range(4 * hf, 4 * hf + 4):
-            src = ind(c("X", 0, 2 * NV), c("PU", 32 * k, 32 * k + 32))
-            if k in EDGE_S:
-                act(c("VG", 512 * k, 512 * k + 512), src, AF.Copy)
-            else:
-                cp(c("VG", 512 * k, 512 * k + 512), src)
-            d = A("pD%d" % (k % 4 if hf else k % 2), slice(0, 31))
-            mm(d, c("ID"), c("VG", 512 * k, 512 * k + 496), True, False)
-            mm(d, c("NI"), c("VG", 512 * k + 16, 512 * k + 512), False, True)
-            act(c("A1", 512 * k, 512 * k + 496), d, AF.Abs)
-            if k % 2:
-                q = k // 2
-                for ll in range(16):
-                    mm(c(pe, 64 * (q % 2), 64 * (q % 2) + 64), sel("W16", ll), c("A1", 1024 * q + ll, 1024 * q + 1024, 16), False, q % 2 == 1 and ll == 15)
-                    ops[-1]["late"] = LATE
-        tt(c("DA", a, b - 2, 2), c("P1", a, b - 2, 2), c("P1", a + 2, b, 2), OP.subtract)
-        tt(c("DB", a + 1, b - 2, 2), c("P1", a + 1, b - 2, 2), c("P1", a + 3, b, 2), OP.subtract)
-        act(c("DA", a + 13, b, 16), c("P1", a + 14, b, 16))
+    def append_one(hf, k):
+        h = str(hf)
+        tt(c("U2" + h, 2) if k else c("U1" + h), ind(hc("UF" + h, k, 272), c("APL", 0, 8)), c("MK" + h), OP.mult)
 
-    def cut(hf):
-        pe = "pE%d" % hf
-        hi = c("SI", 16 + 8 * hf, 24 + 8 * hf)
-        act(hs("nm1", hf), hs("n", hf), AF.Identity, -1.0)
-        ts(c(pe, 256, 384), c(pe, 0, 128), 500000.0, OP.is_lt, 99.0, OP.mult)
-        ts(hs("nd0", hf), c(pe, 0, 128, 16), 1500000.0, OP.is_lt)
-        tt(c(pe, 256, 384), c(pe, 256, 384), c("K1", 0, 128), OP.max)
-        scan(hc("RUN", hf), c("RSTB", 0, 128), c(pe, 256, 384), OP.add, OP.min)
-        tt(hs("j", hf), ends("RUN", hf), hs("nd0", hf), OP.mult)
-        tt(hs("jp", hf), hs("j", hf), hs("n", hf), OP.min)
-        ts(hi, hs("jp", hf), 0.5, OP.mult, -0.25, OP.add)
-        ts(hs("t1", hf), hs("jp", hf), 2.0, OP.mult)
-        ts(hs("H2", hf), hi, 2.0, OP.mult)
-        ts(hs("S2", hf), hi, 2.0 * B17, OP.mult, 2.0 * B17, OP.add)
-        tt(hs("mx", hf), hs("t1", hf), hs("nm1", hf), OP.max)
-        tt(hs("back", hf), hs("nm1", hf), hs("t1", hf), OP.is_gt)
-        tt(hs("C2", hf), hs("mx", hf), hs("H2", hf), OP.subtract)
-        tt(hs("SB", hf), hs("back", hf), hs("S2", hf), OP.mult)
-        ts(hs("mB", hf), hs("C2", hf), -B17, OP.mult, B17, OP.add)
-        tt(hs("NE", hf), hs("mB", hf), hs("SB", hf), OP.subtract)
-        tt(hc("PEN", hf), ind(hs("SB", hf), c("BCL", 0, 8)), c("IO2", 0, 128), OP.subtract)
-        tt(hc("PEN", hf, 256), ind(hs("NE", hf), c("BCL", 0, 8)), c("IO2", 256, 384), OP.subtract)
+    def went(hf, k):
+        act(c("GO", 16 * hf + 8 * k, 16 * hf + 8 * k + 8), uf_end(hf, 2 * k + 1), AF.Sign)
 
-    def least(hf, r):
-        e = c("pE%d" % hf, 0, 128)
-        if r:
-            tt(e, e, hc("PEN", hf), OP.max)
-        tt(e, e, hc("PEN", hf, 256), OP.max)
-        scan(hc("RUN", hf), c("RSTB", 0, 128), e, OP.add, OP.min)
-        tt(hc("NE1", hf), e, hc("RUN", hf), OP.not_equal)
-        scan(hc("UAB", hf), hc("NE1", hf), hc("DA", hf), OP.mult, OP.add)
-        scan(hc("UAB", hf, 256), hc("NE1", hf), hc("DB", hf), OP.mult, OP.add)
+    def new_length(hf):
+        act(hc("NB", hf, 8), hs("N2", hf))
+        group([(c("pZ%d" % hf, NN, NN + 8), ID, x) for x in
+               (hc("NB", hf, 8), c("GO", 16 * hf, 16 * hf + 8), c("GO", 16 * hf + 8, 16 * hf + 16))])
 
-    def new_end():
-        act(s("none"), s("C2"), AF.Relu, 1.0, -1.0)
-        ts(s("dl"), c("P1", 0, 256, 16), NV - 96.0, OP.is_lt, float(NV), OP.mult)
-        act(s("dm"), s("dl"), AF.Identity, 97.0 - NV)
-        ts(s("n"), s("C2"), -1.0, OP.add, 1.0, OP.max)
-        ts(c("INV"), c("PEN", 256, 512), B17, OP.is_gt)
-        tt(c("UP"), P1, c("P1", 1, 257), OP.subtract)
-        act(c("INV", 0, 256, 16), s("CF0"), AF.Identity, 0.0, 0.0)
-        tt(s("dl"), s("dm"), s("none"), OP.mult)
-        scan(c("UE"), c("INV"), c("UP"), OP.mult, OP.add)
-        tt(s("e1"), c("UE", 14, 256, 16), s("dl"), OP.add)
-        to_list("EU", "SM", SL["e1"], 1)
-
-    def shift():
-        tt(s("OH0", 5), ind(s("SB"), c("REP", 0, 5)), s("SC0", 5), OP.is_equal)
-        for k in range(5):
-            y = c("YS", 256 * k, 256 * k + 256)
-            tt(y, bc("OH%d" % k), c("P1", 2 * k, 2 * k + 256), OP.mult)
-            mm(A("pZ1", slice(8, 16)), c("IH"), y, k == 0, k == 4)
-        tt(c("VAL"), bc("n"), K256, OP.is_gt)
-        tt(P1, A("pZ1", slice(8, 16)), c("VAL"), OP.mult)
-        tt(c("P1", 0, 256, 16), c("P1", 0, 256, 16), s("dl"), OP.add)
-
-    def propose(r):
-        AB = c("UAB", 13, 512, 16)
-        ts(c("ABU"), AB, -1.0, OP.add)
-        tt(s("prop"), c("RUN", 15, 256, 16), s("bound"), OP.is_lt)
-        tt(s("as1"), c("UAB", 13, 256, 16), s("prop"), OP.mult)
-        tt(s("bs1"), c("UAB", 269, 512, 16), s("prop"), OP.mult)
-        act(c("XA"), ind(HOME, c("ABU", 0, 16)), AF.Copy)
-        cp(c("ROW"), ind(c("IOT"), c("ABU")))
-        act(c("XS"), ind(PART, c("ABU", 16, 32)), AF.Copy)
-        mm(A("pD0", slice(0, 16)), c("ID"), c("XA"), True, False)
-        mm(A("pD0", slice(0, 16)), c("ID"), c("XS"), False, True)
-        act(c("INV"), A("pD0", slice(0, 16)), AF.Identity, -0.25, 0.5)
-        act(c("XR"), c("INV"), AF.Identity, MAGIC)
-        act(c("MID%d" % r), c("XR"), AF.Identity, -MAGIC)
-        send(c("RM%d" % r, 0, 256), c("MID%d" % r))
-        for lh in range(16):
-            for e, k in enumerate(("as1", "bs1")):
-                o = 4352 * e + 256 * lh
-                ts(c("EQ", o + 16 * lh, o + 256), c("ROW", 256 * e + 16 * lh, 256 * e + 256),
-                   c("SM", SL[k] + lh, SL[k] + lh + 1), OP.is_equal)
-                if lh < 15:
-                    mm(A("pD2", slice(lh + 1, 16)), c("ID"), c("EQ", o + 16 * lh + 16, o + 256), lh == 0 and e == 0, lh == 14 and e == 1)
-        act(c("ACCS", 16, 256), A("pD2", slice(1, 16)), AF.Copy)
-        tt(s("D0", 2), AB, s("TD0", 2), OP.subtract)
-        tt(s("D2", 2), AB, s("TD2", 2), OP.subtract)
-        for ll in range(16):
-            mm(A("pD3", slice(0, 2)), c("TRI", 128 * ll, 128 * ll + 128), c("EQ", ll, 8704, 272), ll == 0, False)
-        for ll in range(16):
-            mm(A("pD3", 0), sel("W1", ll), c("ACCS", ll, 256, 16), False, ll == 15)
-        ts(s("z1", 2), A("pD3", slice(0, 2)), 0.5, OP.is_lt)
-        tt(s("w1"), s("z1"), s("prop"), OP.mult)
-        tt(s("win"), s("w1"), s("z2"), OP.mult)
-        tt(s("L0", 4), ind(s("win"), c("REP", 0, 4)), s("D0", 4), OP.mult)
-        tt(s("D0", 4), s("L0", 4), s("TR0", 4), OP.add)
-        cp(c("LU%d" % r), s("D0", 4))
-        send(c("RL%d" % r), c("LU%d" % r, 0, 32))
-        if r:
-            new_end()
-        scat(c("X"), c("LU%d" % r, 32, 48), c("MID%d" % r))
-
-    def apply_merges(r):
-        scat(c("X"), c("RL%d" % r), c("RM%d" % r))
-        scat(c("X"), c("LU%d" % r, 48, 64), c("NEG"))
-
-    def count():
-        act(c("WINB"), s("win"))
-        mm(A("pZ1", 15, 1), c("ONES"), c("WINB"), True, True)
-        add("V", lambda: g.vector.tensor_reduce(col("ACT")[0], T.pZ1[:, 15, 1], AxisListType.X, OP.add), [col("ACT")], [A("pZ1", 15, 1)], 90.0)
-        cp(c("SI", 8, 9), col("ACT"))
-        ts(c("SI", 9, 10), c("SI", 8, 9), 31, OP.bitwise_and)
-        ts(col("A128"), c("SI", 9, 10), 128.0, OP.mult)
-        act(s("bound"), s("th16"), AF.Identity, col("A128"))
-
-    def rows(hf):
-        lh = slice(8 * hf, 8 * hf + 8)
-        gcp(A("P3", lh), hc("P1", hf))
-        for t in range(4):
-            n = min(6, 21 - 6 * t)
-            gcp(A("PO", lh, slice(6 * t, 6 * t + n)), A("P3", lh, slice(1, 2 * n + 1, 2)))
-        for t in range(4):
-            n = min(7, 22 - 7 * t)
-            gcp(A("PEV", lh, slice(7 * t, 7 * t + n)), A("P3", lh, slice(0, 2 * n, 2)))
-
-    def boost(since, by):
-        for o in ops[since:]:
-            o["late"] = by
-
-    def hop(first, hf, plan, beside):
-        tab, mine, other, lst = (c("CH"), HOME, PART, "EU") if first else (c("CP"), PART, HOME, "FU")
-        lst = c(lst, 8 * hf, 8 * hf + 8)
-        pz, pe = "pZ%d" % hf, "pE%d" % hf
-        e = c(pe, 0, 128)
-        at = len(ops)
-        cp(hc("CU", hf), ind(tab, lst))
-        act(c("Y2", 256 * hf, 256 * hf + 256, 2), ind(mine, lst), AF.Relu, 255.0, -1.0)
-        cp(c("Y2", 256 * hf + 1, 256 * hf + 256, 2), c("Y2", 256 * hf, 256 * hf + 256, 2))
-        boost(at, -BOOST)
-        mm(e, c("ID"), c("KB", 0, 128), True, False)
-        for t0, k in enumerate((0, 2, 1, 3)):
-            if t0 == TURN_AT:
-                ts(hc("CF", hf), hc("CU", hf), 1.0, OP.add)
-                for zh, mat in enumerate(("ZM", "DM")):
-                    for h in range(2):
-                        for rh in range(2):
-                            mm(A(pz, slice(4 * zh, 4 * zh + 4), h), c(mat, (2 * h + rh) * 128, (2 * h + rh + 1) * 128),
-                               c("CF", 128 * hf + 64 * rh, 128 * hf + 64 * rh + 64), rh == 0, rh == 1)
-            if t0 == BESIDE_AT:
-                for f in beside:
-                    f()
-            kk = 4 * hf + k
-            src = ind(other, c("CU", 32 * kk, 32 * kk + 32))
-            vg = c("VG", 512 * kk, 512 * kk + 512)
-            b0 = 8 * hf + 4 * (k % 2) + k // 2
-            if plan[k] == "S":
-                act(vg, src, AF.Copy)
-            else:
-                cp(vg, src)
-            d = "pD%d" % (2 * hf + t0 % 2)
-            for t in range(8):
-                mm(A(d, ALL, slice(2 * t, 2 * t + 2)), c("ID"), c("Y2", 64 * kk, 64 * kk + 64), t == 0, False)
-            mm(A(d), c("ID"), vg, False, True)
-            act(A("A2", slice(b0, b0 + 3, 2)), A(d), AF.Abs, -255.0)
-            if t0 == PATH_AT:
-                cl = A(pz, slice(8, 12))
-                tr(cl, A(pz, slice(0, 4)))
-                for j in range(6 if first else 7):
-                    o = hc("EQH", hf, 256 * j)
-                    tt(o, cl, A("PO" if first else "PEV", slice(8 * hf, 8 * hf + 8), slice(j, j + 16)), OP.is_equal)
-                    mm(e, c("BI"), o, False, False)
-                tr(hc("DC", hf), A(pz, slice(4, 8)))
-            if k >= 2:
-                q = k - 2
-                for ll in range(16):
-                    mm(c(pe, 64 * q, 64 * q + 64), sel("W16", ll), A("A2", slice(8 * hf + 4 * q, 8 * hf + 4 * q + 4), ll),
-                       False, q == 1 and ll == 15)
-                    ops[-1]["late"] = LATE
-        at = len(ops)
-        scan(hc("RUN", hf), c("RSTB", 0, 128), e, OP.add, OP.min)
-        tt(hc("NE1", hf), e, hc("RUN", hf), OP.not_equal)
-        scan(hc("UF", hf), hc("NE1", hf), hc("DC", hf), OP.mult, OP.add)
-        return at
-
-    def gate(hf):
-        ts(hs("lt14", hf), hs("n", hf), 14.0, OP.is_lt, 65536.0, OP.mult)
-        tt(hs("fd2", hf), hs("fd", hf), hs("lt14", hf), OP.is_lt)
-        act(hs("g1", hf), hs("fd2", hf), AF.Identity, 0.0, 65536.0)
-        tt(hc("MK", hf), ind(hs("n", hf), c("BCL", 0, 8)), c("KC", 0, 128), OP.is_equal)
+    def parts_of(hf):
+        h = str(hf)
+        return (path(hf), c("U1" + h), c("U2" + h, 0, 128))
 
     def append(hf):
-        tt(hs("hv", hf), hs("h1", hf), hs("go", hf), OP.mult)
-        tt(hs("fv", hf), hs("f1", hf), hs("go", hf), OP.mult)
-        act(hs("go2", hf), hs("go", hf), AF.Identity, 0.0, 2.0)
-        win = (T.SM[:, SL["hv"] + 8 * hf:SL["hv"] + 8 * hf + 24], hs("hv", hf)[1] + hs("fv", hf)[1], 24, 4, False)
-        tt(hc("UP", hf), ind(win, c("APL", 0, 8)), hc("MK", hf), OP.mult)
-        tt(hc("P1", hf), hc("P1", hf), hc("UP", hf), OP.add)
-        tt(hs("n", hf), hs("n", hf), hs("go2", hf), OP.add)
+        h = str(hf)
+        pz = "pZ" + h
+        at(-900)
+        append_one(hf, 1)
+        at(-450)
+        group([(c(pz, 0, 128), x, IH) for x in parts_of(hf)])
+        at(-50)
+        ts(hc("PU", hf), c(pz, 0, 128), col("ODD"), OP.add)
+        at(400)
+        went(hf, 1)
+        group([(c(pz, 272, 400), IH, x) for x in parts_of(hf)])
+        cp(path(hf), c(pz, 272, 400))
+        new_length(hf)
+        act(hs("N3", hf), c(pz, NN, NN + 8), AF.Identity, -0.5)
+        act(c("TOP", 16 * hf, 16 * hf + 8), c(pz, NN, NN + 8), AF.Identity, 1.0, 2.0)
+        act(c("TOP", 16 * hf + 8, 16 * hf + 16), c(pz, NN, NN + 8), AF.Identity, 1.0)
 
-    def pair(again, plan, beside, beside2):
-        for hf in range(2):
-            at = hop(True, hf, plan[hf], beside[hf])
-            to_list("FU", "UF", 15, 16, hf)
-            boost(at, -BOOST)
-            act(hs("f1", hf), ends("UF", hf))
-            act(hs("fd", hf), ends("RUN", hf))
-        for hf in range(2):
-            at = hop(False, hf, PLAN_HOP[hf], beside2[hf])
-            tt(hs("go", hf), ends("RUN", hf), hs("g1", hf), OP.is_lt)
-            if again:
-                tt(hs("de", hf), ends("UF", hf), hs("e1", hf), OP.subtract)
-                tt(hs("df", hf), hs("de", hf), hs("go", hf), OP.mult)
-                tt(hs("e1", hf), hs("e1", hf), hs("df", hf), OP.add)
-                to_list("EU", "SM", SL["e1"], 1, hf)
-            boost(at, -BOOST)
-            act(hs("h1", hf), ends("UF", hf))
+    def ends_table(hf):
+        pz, P = "pZ%d" % hf, "P%d" % hf
+        group([(c(pz, 136, 408), ID, c("ZERO")),
+               (c(pz, 136, 264, 2), IH, c(P, 0, 128, 2)), (c(pz, 136, 264, 2), NH, c(P, 2, 130, 2)),
+               (c(pz, 150, 264, 16), IH, c(P, 16, 144, 16)),
+               (c(pz, 273, 400, 2), IH, c(P, 1, 128, 2)), (c(pz, 273, 400, 2), NH, c(P, 3, 130, 2))])
+
+    def gather(who, kk, win, lst, t):
+        cuts = PIECES if who == "v" else (0, 32)
+        for n, (a, b) in enumerate(zip(cuts, cuts[1:])):
+            at(t + GAP * n)
+            o, src = c("VG", 520 * kk + 16 * a, 520 * kk + 16 * b), ind(win, c(lst, 32 * kk + a, 32 * kk + b))
+            if who == "S":
+                act(o, src, AF.Copy)
+            else:
+                cp(o, src)
+
+    def sums(hf, k, w, stop, m, width, first):
+        pe = "pE%d" % hf
+        n = 4 // SUMS
+        if (k + 1) % n == 0:
+            lo = k + 1 - n
+            a = 2048 * hf + 512 * lo
+            for i in range(m):
+                mm(A(pe, sl(first + i, w[2] * width, width), parts=sl(32 * lo, 32 * lo + 32 * n)),
+                   c("A2", a + i, a + 512 * n, 16), w, False, stop and i == m - 1)
+
+    def edges(hf, r):
+        pe = "pE%d" % hf
+        n = 3 if r else 1
+        at(1500)
+        mm(c(pe, 0, 128 * n), ID, c("KB", 272, 272 + 128 * n), True, False)
+        if r:
+            mm(c(pe, 143, 384, 16), ID, hc("TOP", hf, 16), False, False)
+            mm(c(pe, 128, 256), ID, c("HALF"), False, False)
+        for k in range(4):
+            kk = 4 * hf + k
+            gather(PLAN_EDGE[hf][k], kk, c("X"), "PU", T_GATHER[k] - 400)
+            d = A("pD%d" % k)
+            at(T_ABS[k] - 1100)
+            group([(d, ID, c("VG", 520 * kk, 520 * kk + 512)), (d, c("NI"), c("VG", 520 * kk + 1, 520 * kk + 513))])
+            at(T_ABS[k] - 400)
+            act(c("A2", 512 * kk, 512 * kk + 512), d, AF.Abs)
+            at(T_ABS[k] + 260)
+            sums(hf, k, c("W16", 8, 8 + 8 * n), k == 3, 14, 16, 0)
+            if k == 1:
+                ends_table(hf)
+        at(2500)
+        for e in range(2):
+            tt(c("BM", 64 * hf + 32 * e, 64 * hf + 32 * e + 32), ind(hs("bnd", hf), c("L8")), c("ZN"), OP.add)
+
+    def cut(hf):
+        h = str(hf)
+        ji, h1 = (c("MX", 256 * hf + 128 * k + 15, 256 * hf + 128 * k + 128, 16) for k in range(2))
+        at(4250)
+        tt(c("M" + h), c("pE" + h, 128, 384), c("K2"), OP.max)
+        at(4700)
+        scan(hc("MX", hf, 256), c("RS2"), c("M" + h), OP.add, OP.min)
+        at(5150)
+        tt(hs("mx", hf), ji, hs("N3", hf), OP.max)
+        tt(hs("back", hf), hs("N3", hf), ji, OP.is_gt)
+        at(5450)
+        tt(c("RI" + h, 16, 144, 16), h1, hs("mx", hf), OP.subtract)
+        for k in range(2):
+            tt(c("RI" + h, 15 + 128 * k, 143 + 128 * k, 16), hs("back", hf), h1, OP.mult)
+        at(5850)
+        scan(c("RO" + h, 15, 272), c("RST1"), c("RI" + h, 15, 272), OP.mult, OP.add)
+        at(6200)
+        ts(hc("RSD", hf), c("RO" + h, 144, 272), 0.0, OP.is_equal, 1.0e9, OP.mult)
+
+    def pick(hf, outs, n, t, rst, beside=None):
+        e = c("pE%d" % hf, 0, n)
+        run, ne = c("RUN", 136 * hf, 136 * hf + n), c("NE1", 136 * hf, 136 * hf + n)
+        at(t)
+        scan(run, rst, e, OP.add, OP.min)
+        at(t + 350)
+        tt(ne, e, run, OP.not_equal)
+        if beside:
+            beside(run)
+        at(t + 700)
+        for k, o in enumerate(outs):
+            scan(o, ne, c("pZ%d" % hf, 136 * k + 136, 136 * k + 136 + n), OP.mult, OP.add)
+
+    def least(hf, r):
+        h = str(hf)
+        e = c("pE" + h, 0, 128)
+        t = 6200 if r else 4250
+        at(t)
+        tt(e, e, c("RO" + h, 16, 144) if r else c("RO" + h, 272), OP.max)
+        pick(hf, [hc("UAB" + h, 0), hc("UAB" + h, 1)], 128, t + 350, hc("RSD", hf),
+             lambda run: tt(hc("PR", hf, 64), ind(run, c("LR")), hc("BM", hf, 64), OP.is_lt))
+        return t + 1500
+
+    def shift(hf, t):
+        h = str(hf)
+        pz = "pZ" + h
+        q = c("RI" + h, 16, 144, 16)
+        at(t)
+        ts(c("RI" + h, 272, 400, 16), q, 0.5, OP.min)
+        act(hs("N2", hf), c("RI" + h, 272, 400, 16), AF.Identity, 0.5, -1.0)
+        act(hs("none", hf), q, AF.Relu, -0.5)
+        ts(hs("dm", hf), c("P" + h, 0, 128, 16), float(TRASH - 97), OP.is_ge, -float(NV), OP.mult)
+        act(hs("dm2", hf), hs("dm", hf), AF.Identity, 97.0)
+        tt(hc("DL", hf, 8), hs("dm2", hf), hs("none", hf), OP.mult)
+        tt(hc("OH", hf, 48), ind(c("RI" + h), c("REP", 0, 3)), c("SCN"), OP.is_equal)
+        terms = []
+        for k in range(5):
+            y = c("YS" + h, 128 * k, 128 * k + 128)
+            tt(y, ind(c("OH", 48 * hf + 8 * k, 48 * hf + 8 * k + 8), c("BCL")), path(hf, 2 * k), OP.mult)
+            terms.append((c(pz, 0, 128), IH, y))
+        new_path(hf, terms + [(c(pz, 0, 128, 16), IH, hc("DL", hf, 8))], t + 2200)
+
+    def propose(hf, r, t):
+        h = str(hf)
+        pz, pe = "pZ" + h, "pE" + h
+        ab = hc("ABU", hf, 16)
+        both = c(pz, LI, LI + 16)
+        at(t)
+        spread("Z" + h, 2, c("UAB" + h), "LA", hc("PR", hf, 64))
+        at(t + 370)
+        turn(pz, "Z" + h, 2)
+        at(t + 830)
+        cp(ab, both)
+        at(t + 1120)
+        act(s("AS" + h), both)
+        cp(hc("ROW", hf, 256), ind(c("IOT"), ab))
+        act(hc("XA", hf), ind(HOME, c("ABU", 16 * hf, 16 * hf + 8)), AF.Copy)
+        act(hc("XS", hf), ind(PART, c("ABU", 16 * hf + 8, 16 * hf + 16)), AF.Copy)
+        d = A("pD%d" % (3 * hf), P8)
+        group([(d, ID, x) for x in (c("HALF"), hc("XA", hf), hc("XS", hf))])
+        act(hc("XR", hf), d, AF.Identity, MAGIC, 0.5)
+        act(hc("MID%d" % r, hf), hc("XR", hf), AF.Identity, -MAGIC)
+        if hf:
+            send(c("RM%d" % r), c("MID%d" % r))
+        at(t + 200)
+        ts(hc("DAB", hf, 64), ind(c("UAB" + h), c("LA")), col("T" + h), OP.subtract)
+        ts(hc("TP", hf, 64), hc("PR", hf, 64), col("THR"), OP.mult, 4.0, OP.mult)
+        at(t + 1700)
+        todo = [(e, c("SM", SL["AS%d" % sh] + 8 * e + lh, SL["AS%d" % sh] + 8 * e + lh + 1), lh if sh == hf else 8)
+                for sh in range(hf + 1) for lh in range(8) for e in range(2)]
+        votes = c(pe, 384, 448)
+        for k, (e, val, w) in enumerate(todo):
+            eq = hc("EQ", 16 * hf + k)
+            ts(eq, c("ROW", 256 * hf + 128 * e, 256 * hf + 128 * e + 128), val, OP.is_equal)
+            mm(votes, eq, c("GW", 64 * w, 64 * w + 64), k == 0, k == len(todo) - 1)
+        tt(hc("WM", hf, 64), votes, hc("TP", hf, 64), OP.is_lt)
+        tt(c("ZL" + h, 3, 256, 4), hc("DAB", hf, 64), hc("WM", hf, 64), OP.mult)
+        turn(pz, "ZL" + h, 2, [(both, IH, hc("TRA", hf, 16))])
+        cp(A("LU%d" % r, ALL, sl(8 * hf, 8 * hf + 8)), both)
+        if hf:
+            send(A("RL%d" % r), A("LU%d" % r))
+
+    def apply_merges(r):
+        scat(PART, A("RL%d" % r, 0), c("RM%d" % r))
+        scat(PART, A("LU%d" % r, 1), c("NEG"))
+        scat(HOME, A("RL%d" % r, 1), c("BIG"))
+
+    def count():
+        a = c("pZ1", NN + 16, NN + 32)
+        group([(a, c("ONES"), c("WM", k, k + 16)) for k in (0, 16, 64, 80)])
+        rsum(col("ACT"), a)
+        cp(c("SI", 8, 9), col("ACT"))
+        ts(c("SI", 9, 10), c("SI", 8, 9), 31, OP.bitwise_and)
+        ts(col("A8"), c("SI", 9, 10), 128.0 * U18, OP.mult)
+        act(s("bnd"), s("th"), AF.Identity, col("A8"))
+
+    def hop(slot, hf, beside):
+        h = str(hf)
+        first = slot % 2 == 0
+        tab, mine, other = (c("CH"), HOME, PART) if first else (c("CP"), PART, HOME)
+        lst = hc("LST", hf, 8)
+        pz, pe = "pZ" + h, "pE" + h
+        at(240)
+        ts(hc("CU", hf), ind(tab, lst), float(OFF), OP.add)
+        if Y2_ON[hf] == "S":
+            act(c("Y2", 256 * hf, 256 * hf + 256, 2), ind(mine, lst), AF.Relu, 255.0, -1.0)
+        else:
+            ts(c("Y2", 256 * hf, 256 * hf + 256, 2), ind(mine, lst), 255.0, OP.subtract, 0.0, OP.min)
+        at(670)
+        cp(hc("CF", hf), hc("CU", hf))
+        at(T_DUP)
+        cp(c("Y2", 256 * hf + 1, 256 * hf + 256, 2), c("Y2", 256 * hf, 256 * hf + 256, 2))
+        at(900)
+        mm(c(pe, 0, 136), ID, c("KB", 0, 136) if first else c("KB", 136, 272), True, False)
+        if first:
+            mm(c(pe, 0, 136, 17), c("CI"), c("CAP", 16 * hf + 4 * slot, 16 * hf + 4 * slot + 8), False, False)
+        group([(c(pz, 0, 272), hc("CF", hf), c("DM")), (c(pz, 0, 136, 17), ID, c("NEG", 0, 8))])
+        at(T_PATH + 400)
+        for f in beside:
+            f()
+        for k in range(4):
+            kk = 4 * hf + k
+            gather(PLAN_HOP[hf][k], kk, other, "CU", T_GATHER[k])
+            d = "pD%d" % k
+            at(T_ABS[k] - 900)
+            for t in range(8):
+                mm(A(d, ALL, sl(2 * t, 2 * t + 2)), ID if Y2_ON[hf] == "S" else c("NI"), c("Y2", 64 * kk, 64 * kk + 64), t == 0, False)
+            at(T_ABS[k] - 460)
+            mm(A(d), ID, c("VG", 520 * kk, 520 * kk + 512), False, True)
+            at(T_ABS[k])
+            act(c("A2", 512 * kk, 512 * kk + 512), A(d), AF.Abs, -255.0)
+            if k == 2:
+                for j in range(6 if first else 7):
+                    o = hc("EQH", 2 * j + hf, 136)
+                    at(T_PATH + j)
+                    tt(o, c(pz, 0, 136), A(("PO" if first else "PEV") + h, ALL, sl(j, j + 17)), OP.is_equal)
+                    at(T_PATH + 1200 + j)
+                    mm(c(pe, 0, 136), c("BI"), o, False, False)
+            at(T_ABS[k] + 660)
+            sums(hf, k, c("W16", 0, 8), k == 3, 16, 17, 1)
+        pick(hf, [c("UF" + h, 136 * slot, 136 * slot + 136)], 136, T_PICK, c("RSTB"))
+        if slot < 3:
+            to_list(hf, c("UF" + h, 136 * slot, 136 * slot + 136), "LZ", T_PICK + 1050)
+
+    def bar(hf, slot):
+        name, n = (("PO", 6), ("PEV", 7))[slot]
+        for t in range(3):
+            gcp(A(name + str(hf), ALL, n * t + n - 1), uf_end(hf, slot))
 
     def points_out():
-        ts(c("XO"), HOME, 255.0, OP.min)
+        ts(c("XO"), c("X", OFF, TRASH), 255.0, OP.min)
         dma(T.yx[:], c("XO"), 256 * NV)
 
-    penalty()
-    last_point()
-    rows(0)
-    rows(1)
+    def result(hf):
+        h = str(hf)
+        pz = "pZ" + h
+        went(hf, 1)
+        tt(uf_end(hf, 2), uf_end(hf, 2), c("GO", 16 * hf + 8, 16 * hf + 16), OP.mult)
+        append_one(hf, 1)
+        group([(c(pz, 0, 128), x, IH) for x in parts_of(hf)])
+        act(hc("WL", hf), c(pz, 0, 128), AF.Relu, -float(OFF))
+        dma(T.yw[:, 128 * hf:128 * hf + 128], hc("WL", hf), 65536)
+        new_length(hf)
+        act(hc("NB", hf, 8), c(pz, NN, NN + 8), AF.Identity, 1.0, 2.0)
+        mm(A(pz, sl(136, 264), parts=P8), hc("NB", hf, 8), ID, True, True)
+        act(A("WN", sl(128 * hf, 128 * hf + 128), parts=P8), A(pz, sl(136, 264), parts=P8))
+        if hf:
+            dma(T.yn[:], A("WN", ALL, parts=P8), 8192)
+
+    def after_pair(hf, last):
+        went(hf, 0)
+        if last:
+            tt(uf_end(hf, 0), uf_end(hf, 0), c("GO", 16 * hf, 16 * hf + 8), OP.mult)
+        append_one(hf, 0)
+
+    first_path(0)
+    first_path(1)
     cnts["main"] = True
     for r in range(ROUNDS):
+        last = r + 1 == ROUNDS
+        base = 100000.0 * r
         for hf in range(2):
+            cnts["base"] = base + HALF * hf
             if r:
                 append(hf)
-            edges(hf)
+            edges(hf, r)
         for hf in range(2):
+            cnts["base"] = base + HALF * hf
             if r:
                 cut(hf)
-            least(hf, r)
-        propose(r)
+            propose(hf, r, least(hf, r))
+        cnts["base"] = base
+        if r:
+            shift(0, T_SHIFT[0])
+        at(T_OWN)
+        scat(HOME, A("LU%d" % r, 0), c("MID%d" % r))
+        if r:
+            shift(1, T_SHIFT[1])
+        at(T_OWN + 2500)
         apply_merges(r)
-        pair(True, PLAN_CUT if r else PLAN_HOP, [[shift, lambda: rows(0), lambda: rows(1)] if r else [], []],
-             [[lambda: gate(0)], [lambda: gate(1), count if r + 1 < ROUNDS else points_out]])
-        pair(False, PLAN_APP, [[lambda: append(0), lambda: rows(0)], [lambda: append(1), lambda: rows(1)]],
-             [[lambda: gate(0)], [lambda: gate(1)]])
-    append(0)
-    append(1)
-
-    ts(A("C16"), P1, -1.0, OP.add, 0.0, OP.max)
-    cp(A("N16", ALL, ALL, 0), s("n"))
-    turn("C16", 0, "ZM", 0)
-    turn("N16", 0, "ZM", 1)
-    tr(c("WL"), A("pZ0"))
-    dma(T.yw[:], c("WL", 0, 256), 131072)
-    dma(T.yn[:], (T.WL[0:128:16, 256:512], c("WL", 256, 512)[1]), 8192)
+        for slot in range(4):
+            for hf in range(2):
+                cnts["base"] = base + 100000.0 - 2 * HALF * (4 - slot) + HALF * hf
+                beside = []
+                if slot in (1, 2):
+                    beside.append(lambda: bar(hf, slot - 1))
+                if slot == 3:
+                    beside.append(lambda: after_pair(hf, last))
+                if slot == 1 and hf:
+                    beside.append(points_out if last else count)
+                hop(slot, hf, beside)
+    for hf in range(2):
+        cnts["base"] = 100000.0 * ROUNDS + HALF * hf
+        at(-900)
+        result(hf)
 
     if "plan" not in PLAN:
         PLAN["plan"] = order_calls(ops)
@@ -690,7 +846,7 @@ def rank_program(g, core, T, topo):
     waited = {}
     for i in order:
         o = ops[i]
-        if o["q"] == "R":
+        if o["q"][0] == "R":
             continue
         for (key, j) in waits[i]:
             Q[o["q"]].wait_ge(T.sem[key], count_of[j])

@@ -9,61 +9,75 @@ MAGIC = 12582912.0
 U18 = 2.0 ** -18
 FAR = 2.0 ** 99
 LI, NN = 408, 424
-PLAN_HOP = ("VSSv", "VSSv")
-PLAN_EDGE = ("VSSv", "VSSv")
-Y2_ON = "VV"
-SUMS = 1
+PLAN_HOP = [("VSSv", "VSSv")] * 4
+PLAN_END = [("SVSv", "SVSv")] * 4
+PLAN_EDGE = (("SV", "VS", "SV", "VV"), ("SV", "VV", "SV", "VV"))
+EQ_S = 3
+PLAN_OLD = ("SvSv", "vSvv")
+OLD_AT = ((0, 1, 2, 2), (0, 1, 2, 2))
+Y2_ON = ("SV", "VV", "VV", "VV")
+S16 = True
+NP = 4
 PIECES, GAP = (0, 12, 22, 32), 350
 HALF = 3300.0
 T_GATHER, T_ABS = (680, 680, 1340, 1460), (2020, 2445, 2870, 3295)
 T_DUP, T_PATH, T_PICK = 660, 2490, 4645
-T_SHIFT, T_OWN = (9000, 17200), 17000
-RLAT, GA, SC, PEC, LAT, VF, PASSES = 2500.0, 1.45, 3.5, 0.43, 240.0, 0.0, 6
+T_OLD = (2100, 3800)
+T_SHIFT, T_OWN = 2000, 17000
+RCALL, RLAT, GA, SC, PEC, LAT, VF = 800.0, 2500.0, 1.4, 3.5, 0.43, 250.0, 0.0
+REARLY = 3000.0
+PASSES, SHAKE = 24, 100.0
 
-SLOTS = ["N2", "N3", "th", "bnd", "mx", "back", "none", "dm", "dm2", "AS0", "AS1", "CF0", "CF1", "col", "G8", "P4", "W8", "E16", "R16"]
+SLOTS = ["N2", "N30", "N31", "mx0", "mx1", "bk0", "bk1", "dq0", "dq1", "gd0", "gd1", "go0", "go1", "N3b", "yd", "th", "bnd", "none",
+         "dm", "dm2", "AS0", "AS1", "CF0", "CF1", "col", "col2", "G8", "P4", "W8", "E16", "R16"]
 SL = {k: 16 * i for i, k in enumerate(SLOTS)}
-COLS = {k: i for i, k in enumerate(("PM", "GRP", "PM4", "P3", "P7", "EVN", "ODD", "T0", "T1", "ACT", "A8", "THR", "WC", "C17", "C16", "P"))}
+COLS = {k: i for i, k in enumerate(("PM", "GRP", "PM4", "P3", "P7", "EVN", "ODD", "T0", "T1", "ACT", "A8", "THR", "WC", "C17", "C16",
+                                    "P", "C19"))}
 
 F32, BF, F16, I32, U16 = "float32", "bfloat16", "float16", "int32", "uint16"
 SB = {
-    "X": ([2 * WIN], BF), "CH": ([TRASH], I32), "CP": ([TRASH], I32), "XO": ([NV], BF), "IOT": ([TRASH], F32),
+    "X": ([2 * WIN], BF), "CH": ([TRASH], I32), "CP": ([TRASH], F32), "CS": ([NV], F16), "CR": ([NV], F16), "XO": ([NV], BF), "IOT": ([TRASH], F32),
     "SM": ([16 * len(SLOTS)], F32), "SI": ([16], I32), "WI": ([256], I32), "WH": ([256], F16), "NT": ([512], I32),
     "NF": ([512], F32), "WL": ([256], F32), "WN": ([256], F32),
-    "KM": ([128], F32), "T17": ([272], F32), "V1": ([136], F32), "K16": ([128], F32), "H4": ([64], F32), "GI": ([64], F32),
-    "TRF": ([32], F32), "SCN": ([48], F32), "RR": ([128], F32), "TA": ([136], F32), "TB": ([136], F32),
-    "ID": ([128], BF), "NI": ([128], BF), "BI": ([128], BF), "CI": ([128], BF), "VI": ([128], BF), "ONES": ([128], BF),
-    "IH": ([128], F16), "NH": ([128], F16), "IF": ([128], F32), "HALF": ([128], BF), "ZERO": ([272], BF),
-    "W16": ([32], BF), "DM": ([272], F16), "KB": ([656], BF), "RSTB": ([136], F32), "RST1": ([257], BF), "RSM": ([128], BF),
-    "K2": ([256], F32), "ZM": ([64], F32), "ZN": ([32], F32), "R4": ([32], F16), "G64": ([64], F32), "GW": ([576], BF),
-    "RS2": ([256], F32), "TRA": ([32], F16), "NEG": ([256], BF), "BIG": ([256], BF),
-    "LZ": ([2], U16), "LE": ([2], U16), "LA": ([4], U16), "LR": ([4], U16), "L8": ([2], U16), "REP": ([4], U16), "BCL": ([8], U16),
-    "APL": ([16], U16), "EQ": ([128 * 48], BF), "ROW": ([512], F16), "ABU": ([32], U16),
-    "PU": ([256], U16), "VG": ([8 * 520], BF), "A2": ([4096], BF), "Y2": ([512], BF), "CU": ([256], U16), "CF": ([256], F16),
-    "LST": ([16], U16), "EQH": ([14 * 136], BF), "XA": ([256], BF), "XS": ([256], BF), "XR": ([256], F32),
-    "CAP": ([32], BF), "TOP": ([32], BF), "GO": ([32], BF), "NB": ([16], BF), "DL": ([16], F16), "WM": ([128], BF),
-    "BM": ([128], F32), "PR": ([128], F32), "TP": ([128], F32), "RSD": ([256], F32), "DAB": ([128], F32),
-    "RUN": ([272], F32), "NE1": ([272], F32), "MX": ([512], F32), "UE": ([256], F32), "OH": ([96], F32),
+    "EQ": ([128 * 48], BF), "ROW": ([512], F16), "ABU": ([32], U16), "PU": ([256], U16), "PH": ([256], U16),
+    "RA": ([8], U16), "KF": ([128], BF), "MV": ([128], BF), "AB": ([128 * 8], F16),
+    "VG": ([8 * 520], BF), "A2": ([4096], BF), "VE": ([8 * 520], BF), "A1": ([4096], BF),
+    "Y2": ([512], BF), "CU": ([256], U16), "CF": ([256], F16), "LST": ([16], U16), "EQH": ([14 * 136], BF),
+    "XA": ([256], BF), "XS": ([256], BF), "XR": ([256], F32), "CAP": ([32], BF), "DK": ([64], F32), "ED": ([16], BF),
+    "GO": ([32], BF), "NB": ([16], BF), "DL": ([16], F16), "WM": ([128], BF), "BM": ([128], F32), "PR": ([128], F32),
+    "TP": ([128], F32), "RSD": ([304], F32), "DAB": ([128], F32), "RUN": ([304], F32), "NE1": ([304], F32),
+    "MX": ([512], F32), "UE": ([256], F32), "OH": ([96], BF), "OT": ([256], BF), "SEL": ([640], BF),
+}
+CONST = {
+    F32: {"KM": 128, "T17": 272, "T19": 152, "V1": 136, "K16": 128, "H4": 64, "GI": 64, "TRF": 32, "SCN": 48, "RR": 128, "TA": 136,
+          "TB": 136, "IF": 128, "RSTB": 136, "ZM": 64, "ZN": 64, "G64": 64, "K2": 256, "RS2": 256, "SEF": 640, "V2": 128},
+    BF: {"ID": 128, "NI": 128, "BI": 128, "CI": 128, "VI": 128, "MI": 128, "UI": 128, "TWO": 128, "ONES": 128, "HALF": 128, "TOPF": 128,
+         "ZERO": 304, "W16": 32, "KB": 832, "RST1": 305, "RSM": 128, "GW": 576, "NEG": 256, "BIG": 128},
+    F16: {"IH": 128, "NH": 128, "DM": 272, "R4": 32, "TRA": 32, "PK": 512},
+    U16: {"LZ": 2, "LE": 2, "LA": 4, "LR": 4, "L8": 4, "LG": 2, "REP": 4, "APL": 8},
 }
 for _h in range(2):
-    for _k, _v in (("P", ([144], F16)), ("U1", ([128], F16)), ("U2", ([130], F16)), ("UF", ([544], F32)), ("UAB", ([256], F32)),
-                   ("RI", ([400], BF)), ("RO", ([400], BF)), ("INV", ([128], BF)), ("MK", ([128], BF)), ("M", ([256], F32)),
-                   ("PO", ([8, 26], F16)), ("PEV", ([8, 30], F16)), ("YS", ([640], F16)), ("Z", ([260], F16)), ("ZL", ([260], F16))):
+    for _k, _v in (("P", ([144], F16)), ("U1", ([128], F16)), ("U2", ([130], F16)), ("UF", ([544], F32)), ("UAB", ([304], F32)),
+                   ("DT", ([304], F32)), ("RI", ([464], BF)), ("RO", ([464], BF)), ("INV", ([130], BF)), ("MK", ([128], BF)),
+                   ("M", ([256], F32)), ("PO", ([8, 26], F16)), ("PEV", ([8, 30], F16)), ("YS", ([640], F16 if S16 else F32)),
+                   ("Z", ([260], F16)), ("ZL", ([260], F16)), ("ZE", ([132], F16)),
+                   ("TOP", ([2, 16], F32)), ("JH", ([2, 16], F32)), ("QS", ([2, 16], F32))):
         SB[_k + str(_h)] = _v
 for _r in range(ROUNDS):
-    SB["MID%d" % _r] = ([256], BF)
-    SB["RM%d" % _r] = ([256], BF)
-    SB["LU%d" % _r] = ([2, 16], U16)
-    SB["RL%d" % _r] = ([2, 16], U16)
+    SB["MID%d" % _r] = ([2, 144], F16)
+    SB["RM%d" % _r] = ([2, 144], F16)
+    for _k in ("LU", "LS", "RL"):
+        SB[_k + str(_r)] = ([2, 16], U16)
+SHAPE = dict(SB)
 POOL = {}
-for _k in ("KM", "T17", "V1", "K16", "H4", "GI", "TRF", "SCN", "RR", "TA", "TB", "IF", "RSTB", "ZM", "ZN", "G64", "K2", "RS2", "ID", "NI",
-           "BI", "CI", "VI", "ONES", "HALF", "ZERO", "W16", "KB", "RST1", "RSM", "GW", "NEG", "BIG", "IH", "NH", "DM", "R4", "TRA",
-           "LZ", "LE", "LA", "LR", "L8", "REP", "BCL", "APL"):
-    _n = "K" + SB[_k][1]
-    _at = SB.get(_n, ([0], 0))[0][0]
-    POOL[_k] = (_n, _at)
-    SB[_n] = ([_at + (SB[_k][0][0] + 15) // 16 * 16], SB[_k][1])
-SCRATCH = {k: ("sbuf", [128] + v[0], v[1]) for k, v in SB.items() if k not in POOL}
-SHAPE = {k: v for k, v in SB.items()}
+for _t, _names in CONST.items():
+    _at = 0
+    for _k, _n in _names.items():
+        POOL[_k] = ("K" + _t, _at)
+        SHAPE[_k] = ([_n], _t)
+        _at += (_n + 15) // 16 * 16
+    SB["K" + _t] = ([_at], _t)
+SCRATCH = {k: ("sbuf", [128] + v[0], v[1]) for k, v in SB.items()}
 for _r in range(2):
     SCRATCH["pZ%d" % _r] = ("psum", [128, 512], F32)
     SCRATCH["pE%d" % _r] = ("psum", [128, 512], F32)
@@ -71,7 +85,7 @@ for _r in range(4):
     SCRATCH["pD%d" % _r] = ("psum", [128, 32, 16], F32)
 for _k, _v in SCRATCH.items():
     SHAPE[_k] = (_v[1][1:], _v[2])
-SEMAPHORES = ["sV", "sS", "sP", "sG"] + ["d%d" % i for i in range(24)] + ["r%d" % i for i in range(16)]
+SEMAPHORES = ["sV", "sS", "sP", "sG"] + ["d%d" % i for i in range(40)] + ["r%d" % i for i in range(24)]
 OP = AluOpType
 AF = ActivationFunctionType
 ALL = slice(None)
@@ -152,6 +166,10 @@ def place(ops, before, key, head):
 def order_calls(ops):
     n = len(ops)
     hard, soft = find_waits(ops)
+    for i in range(n):
+        if "lead" in ops[i]:
+            hard[i].discard(ops[i]["lead"])
+            soft[i].add(ops[i]["lead"])
     fore = [{j: (ops[j]["lat"] + LAT if j in hard[i] else 0.0) for j in hard[i] | soft[i]} for i in range(n)]
     back = [{} for _ in ops]
     for i in range(n):
@@ -162,13 +180,15 @@ def order_calls(ops):
         if not ops[i]["inorder"]:
             key[i] = min([key[k] - ops[i]["cost"] - d for k, d in back[i].items()] + [1.0e9])
     best = None
-    for _ in range(PASSES):
+    for turn in range(PASSES):
         start = place(ops, fore, key, [0.0] * n)
         end = max(start[i] + ops[i]["cost"] + ops[i]["lat"] for i in range(n))
         if best is None or end < best[0]:
             best = (end, start)
         late = place(ops, back, [-start[i] - ops[i]["cost"] for i in range(n)], [o["lat"] for o in ops])
         key = [-late[i] - ops[i]["cost"] for i in range(n)]
+        if turn % 3 == 2:
+            key = [best[1][i] + SHAKE * (((i * 7919 + turn * 104729) * 2654435761 % 4096) / 4096.0 - 0.5) for i in range(n)]
     order = sorted(range(n), key=lambda i: (best[1][i], i))
     pos = {i: t for t, i in enumerate(order)}
     seen = {}
@@ -200,8 +220,9 @@ def rank_program(g, core, T, topo):
     mate = T.cores[(rank + len(T.cores) // 2) % len(T.cores)]
     rid, pid = topo.addr(mate, core)
     engs = topo.engines(core, mate)
+    low = engs[:len(engs) // 2]
     ops = []
-    cnts = {"d": 0, "r": 0, "main": False, "t": 0.0, "base": 0.0}
+    cnts = {"d": 0, "r": 0, "main": False, "t": 0.0, "base": 0.0, "bank": -1}
 
     def A(name, *idx, parts=ALL):
         key = (name, str(idx))
@@ -256,6 +277,10 @@ def rank_program(g, core, T, topo):
 
     def at(t):
         cnts["t"] = cnts["base"] + t
+
+    def behind(j, i=-1):
+        ops[i]["after"].append(j)
+        ops[i]["lead"] = j
 
     def p(a):
         return a[0] if isinstance(a, tuple) else a
@@ -321,45 +346,55 @@ def rank_program(g, core, T, topo):
         add("Y", lambda: g.sync.dma_start(p(o), p(i)).then_inc(T.sem[k], 16), [o] if isinstance(o, tuple) else [], [i], 60.0,
             (k, 16), 2000 + nbytes / 200.0)
 
-    def send(dst, src, use=engs[:len(engs) // 2]):
-        neng = len(use)
-        emask = sum(1 << e for e in use)
+    def send(dst, src, use, lat=RLAT):
         k = "d%d" % cnts["d"]
         r = "r%d" % cnts["r"]
         cnts["d"] += 1
         cnts["r"] += 1
-        t = 128 * src[2] * src[3] / (12.0 * neng)
-        add("G", lambda: g.remote_dma(dst[0], src[0], T.sem[r], T.sem[k], pid, rid, emask), [], [src], 300.0, (k, neng), RLAT - LAT)
-        add("R%d" % emask, None, [dst], [], t, (r, neng), 0.0, after=[len(ops) - 1])
+        mask = sum(1 << e for e in use)
+        t = 128 * src[2] * src[3] / (12.0 * len(use))
+        add("G", lambda: g.remote_dma(dst[0], src[0], T.sem[r], T.sem[k], pid, rid, mask), [], [src], RCALL, (k, len(use)),
+            lat - LAT - RCALL)
+        add("R%d" % mask, None, [dst], [], t, (r, len(use)), 0.0, after=[len(ops) - 1])
 
     HOME, PART = c("X", 0, WIN), c("X", WIN, 2 * WIN)
     ID, IH, NH = c("ID"), c("IH"), c("NH")
     G8, CF8 = s("G8", 8), s("CF0", 8)
     P8 = sl(0, 8)
 
-    H = NV // 2
-    for k in range(2):
+    H = NV // NP
+    for k in range(NP):
         dma(c("X", OFF + k * H, OFF + k * H + H), T.pts[:, k * H:k * H + H], 256 * H)
     dma(c("WI"), T.way[:], 131072)
     dma(A("NT", sl(0, 256), parts=P8), T.cnt[:], 8192)
     dma(A("NT", sl(256, 512), parts=P8), T.th[:], 8192)
     dma(c("CH", OFF), T.cand[:], 512 * NV)
+    for k in range(1, len(ops)):
+        behind(k - 1, k)
+    ops[-1]["lat"] += 3000.0
     iota(c("T17"), [[0, 16], [1, 17]], 0, 0)
+    iota(c("T19"), [[0, 8], [1, 19]], 0, 0)
     iota(c("KM"), [[-1, 128]], 0, 1)
     iota(c("SI", 0, 2), [[0, 2]], 0, 1, False)
     iota(s("CF0", 32), [[1, 32]], 0, 0)
     iota(c("K16"), [[0, 8], [1, 16]], 0, 0)
     iota(c("V1"), [[-16, 8], [-1, 17]], 0, 1)
+    iota(c("V2"), [[-16, 8], [1000, 2], [-2, 8]], 0, 1)
     iota(c("H4"), [[0, 16], [1, 4]], 0, 0)
-    for k in range(2):
+    for k in range(NP):
         send(c("X", WIN + OFF + k * H, WIN + OFF + k * H + H), c("X", OFF + k * H, OFF + k * H + H), engs)
-    send(c("CP", OFF), c("CH", OFF), engs[len(engs) // 2:])
-    sent = len(ops) - 4
-    ops[-2]["after"] = [sent + 1]
-    for o, pat, base in ((c("GI"), [[0, 2], [1, 8], [0, 4]], 0), (c("TRF"), [[128, 2], [0, 2], [16, 8]], TRASH),
-                         (c("IOT"), [[1, TRASH]], 0), (c("SCN"), [[1, 6], [0, 8]], 0)):
-        iota(o, pat, base, 0)
+    gcp(c("CS"), c("CH", OFF))
+    send(c("CR"), c("CS"), engs[len(engs) // 2:], 2 * REARLY)
+    ops[-1]["after"].append(len(ops) - 4)
+    iota(c("GI"), [[0, 2], [1, 8], [0, 4]], 0, 0)
+    iota(c("TRF"), [[128, 2], [0, 2], [16, 8]], TRASH, 0)
+    iota(c("IOT", 0, 296), [[1, 296]], 0, 0)
+    iota(c("SCN"), [[1, 6], [0, 8]], 0, 0)
+    iota(c("SEF"), [[-8, 5], [-1, 8], [0, 16]], 0, 1)
 
+    for k in range(296, TRASH, 296):
+        act(c("IOT", k, k + 296), c("IOT", 0, 296), AF.Identity, float(k))
+    ts(c("SEL"), c("SEF"), 0.0, OP.is_equal, 4096.0, OP.mult)
     PI = c("SI", 0, 1)
     for k, (a, b) in enumerate(((0, 15), (4, 7), (2, 3), (0, 3), (0, 7), (0, 1))):
         ts(c("SI", 2 + k, 3 + k), PI, a, OP.logical_shift_right, b, OP.bitwise_and)
@@ -368,85 +403,92 @@ def rank_program(g, core, T, topo):
     act(col("ODD"), col("EVN"), AF.Identity, 0.0, float(WIN))
     act(col("C17"), col("PM4"), AF.Identity, 16.0, 17.0)
     act(col("C16"), col("PM4"), AF.Identity, 15.0, 16.0)
+    act(col("C19"), col("PM4"), AF.Identity, 17.0, 19.0)
     for hf in range(2):
-        act(col("T%d" % hf), col("P"), AF.Identity, TRASH + 128.0 * hf)
-    ts(c("PU"), c("WI"), col("ODD"), OP.add, float(OFF), OP.add)
+        act(col("T%d" % hf), col("P"), AF.Identity, -TRASH - 128.0 * hf, -1.0)
     ts(c("WH"), c("WI"), float(OFF), OP.add)
+    for e in range(2):
+        for b in range(2):
+            ts(hc("PK", 2 * e + b), c("V2"), e + 1000.0 * b, OP.is_equal)
+        group([(hc("pE0", e), hc("PK", 2 * e + b), c("WH", b, 256, 2)) for b in range(2)])
+    cp(c("PH"), c("pE0", 0, 256))
     cp(A("NF", ALL, parts=P8), A("NT", ALL, parts=P8))
     ts(c("IF"), c("KM"), 0.0, OP.is_equal)
-    for name, v in (("ID", 1.0), ("NI", -1.0), ("BI", B17), ("CI", 65536.0), ("VI", -4096.0)):
+    for name, v in (("ID", 1.0), ("NI", -1.0), ("BI", B17), ("CI", 65536.0), ("VI", -4096.0), ("MI", 192.0), ("UI", 2 * U18), ("TWO", 2.0)):
         act(c(name), c("IF"), AF.Identity, 0.0, v)
     cp(IH, c("IF"))
     ts(NH, c("IF"), -1.0, OP.mult)
     ts(G8, CF8, col("GRP"), OP.is_equal)
-    act(c("W16", 0, 8), G8, AF.Identity, 0.0, 16.0)
-    for k in range(3):
-        act(c("W16", 8 + 8 * k, 16 + 8 * k), G8, AF.Identity, 0.0, (-16.0 if k else 16.0) * U18)
+    for k, v in enumerate((16.0, 16.0 * U18, -16.0 * U18, -16.0 * U18)):
+        act(hc("W16", k, 8), G8, AF.Identity, 0.0, v)
     sfill(c("X", 0, OFF), BIGH)
     sfill(c("X", WIN, WIN + OFF), BIGP)
     sfill(c("X", TRASH, WIN), 0.0)
     sfill(c("X", WIN + TRASH), 0.0)
     ms(c("CH", 0, OFF), -OFF)
-    ms(c("CP", 0, OFF), -OFF)
-    sfill(c("VG", 512, 8 * 520, 520), 0.0)
-    act(c("KB", 0, 272), c("T17"))
-    sfill(c("KB", 136, 272, 17), 65536.0)
-    act(c("KB", 272, 400), c("K16"), AF.Identity, 0.0, U18)
-    sfill(c("KB", 286, 400, 16), 1.0)
-    sfill(c("KB", 400, 656), 129.0)
-    sfill(c("KB", 415, 656, 16), 0.0)
-    ts(c("RSTB"), c("T17", 0, 136), 0.0, OP.is_equal, 1.0e9, OP.mult)
+    ms(c("CP", 0, OFF), -float(OFF))
+    sfill(c("VE", 512, 8 * 520, 520), 0.0)
+    sfill(c("KB", 272, 528), 129.0)
+    for k in range(2):
+        act(c("KB", 528 + 152 * k, 680 + 152 * k), c("T19"), AF.Identity, 0.0, U18)
+    for k in range(14, 19):
+        sfill(c("KB", 528 + k, 680, 19), 1.0)
+        sfill(c("KB", 680 + k, 832, 19), (k - 14) * U18 if k < 18 else 1.0)
+    sfill(c("RSTB"), -0.5)
+    sfill(c("RSTB", 0, 136, 17), 1.0e9)
     for k in range(2):
         ts(hc("RS2", k), c("K16"), 0.0, OP.is_equal, 1.0e9, OP.mult)
-    act(c("RSD"), c("RS2"))
     act(c("RSM"), c("K16"), AF.Sign)
-    sfill(c("RST1"), 1.0)
-    sfill(c("RST1", 1, 128, 16), -1.0)
-    sfill(c("RST1", 0, 256, 16), 0.0)
+    ms(c("RST1"), 1.0)
+    sfill(c("RST1", 1, 152, 19), -1.0)
+    sfill(c("RST1", 0, 304, 19), 0.0)
     act(c("K2", 0, 128), c("K16"), AF.Identity, 0.5)
     act(c("K2", 128, 256, 2), c("K16", 0, 128, 2), AF.Identity, 1.0, 0.5)
     act(c("K2", 129, 256, 2), c("K16", 1, 128, 2), AF.Identity, 1.5, 0.5)
     sfill(c("K2", 0, 128, 16), -0.5)
-    sfill(c("K2", 15, 256, 16), -99.0)
-    for name, v in (("NEG", BIGP), ("BIG", BIGH), ("ONES", 1.0), ("HALF", -0.5), ("ZERO", 0.0)):
+    for name, v in (("NEG", BIGP), ("BIG", BIGH), ("ONES", 1.0), ("HALF", -0.5), ("TOPF", 255.0)):
         sfill(c(name), v)
+    ms(c("ZERO"), 0.0)
     ts(c("TA"), c("V1"), -1.0, OP.is_equal)
     ts(c("TB"), c("V1"), 0.0, OP.is_equal)
     sfill(c("TA", 0, 136, 17), 0.0)
     sfill(c("TB", 16, 136, 17), 0.0)
     cp(c("DM", 0, 136), c("TA"))
+    ts(c("DM", 0, 136, 17), c("TB", 0, 136, 17), -1.0 / 4096.0, OP.mult)
     tt(c("DM", 136, 272), c("TA"), c("TB"), OP.subtract)
     ts(c("ZM"), c("H4"), col("PM4"), OP.is_equal)
-    act(c("ZN"), c("ZM", 0, 32), AF.Identity, -1.0)
+    act(c("ZN"), c("ZM"), AF.Identity, -1.0)
     ts(s("P4", 4), s("CF0", 4), col("P3"), OP.is_equal)
     for k in range(4):
-        ts(c("R4", 8 * k, 8 * k + 8), G8, c("SM", SL["P4"] + k, SL["P4"] + k + 1), OP.mult)
+        ts(hc("R4", k, 8), G8, c("SM", SL["P4"] + k, SL["P4"] + k + 1), OP.mult)
     ts(c("LZ"), s("CF0", 2), 68.0, OP.mult, col("C17"), OP.add)
     ts(c("LE"), s("CF0", 2), 64.0, OP.mult, col("C16"), OP.add)
-    ts(c("LA"), s("CF0", 4), 64.0, OP.mult, col("C16"), OP.add)
-    ts(c("LA"), c("LA"), -1.0, OP.add)
+    ts(c("LA"), s("CF0", 4), 76.0, OP.mult, col("C19"), OP.add)
     for k in range(2):
         cp(hc("LR", k, 2), c("LA", 0, 2))
-    cp(c("BCL"), CF8)
-    ts(c("L8"), s("CF0", 2), 4.0, OP.mult, col("PM4"), OP.add)
-    act(col("P7"), col("P7"), AF.Identity, 15.0, 16.0)
+        ts(hc("L8", k, 2), s("CF0", 2), 4.0, OP.mult, col("PM4"), OP.add)
+    ts(c("LG", 0, 1), col("P7"), 17.0, OP.mult, 16.0, OP.add)
+    act(col("P7"), col("P7"), AF.Identity, 18.0, 19.0)
     ts(c("REP"), s("CF0", 4), 0.0, OP.mult, col("P7"), OP.add)
     act(col("EVN"), col("EVN"), AF.Identity, 152.0, -136.0)
-    ts(c("APL", 0, 8), CF8, 17.0, OP.mult, col("EVN"), OP.add)
+    ts(c("APL"), CF8, 17.0, OP.mult, col("EVN"), OP.add)
     for hf in range(2):
         h = str(hf)
         ms(c("P" + h, 128), 0.0)
         ms(c("U2" + h, 0, 2), 0.0)
-        ms(c("Z" + h), 0.0)
-        ms(c("ZL" + h), 0.0)
-        sfill(c("RI" + h, 0, 144), 0.5)
-        sfill(c("RI" + h, 144, 272), -0.5)
-        sfill(c("RI" + h, 272, 400), 0.5)
-        sfill(c("RI" + h, 144, 272, 16), 0.0)
+        for z in ("Z", "ZL", "ZE"):
+            ms(c(z + h), 0.0)
+        sfill(c("INV" + h, 128), 1.0)
+        sfill(c("RI" + h, 0, 171), 0.5)
+        sfill(c("RI" + h, 171, 336), -0.5)
+        sfill(c("RI" + h, 336, 464), 0.5)
+        sfill(c("RI" + h, 171, 323, 19), 0.0)
+        sfill(c("RI" + h, 18, 322, 19), 0.0)
     sfill(c("TA", 0, 128), 1.0 / 3.0)
     scan(c("RR"), c("TA", 0, 128), c("ZERO", 0, 128), OP.mult, OP.add, 3.0 ** 61)
     tt(c("TB", 0, 128), c("RR"), c("IF"), OP.mult)
     rsum(col("THR"), c("TB", 0, 128))
+    act(col("THR"), col("THR"), AF.Identity, 0.0, 4.0)
     ts(s("E16"), s("CF0"), col("PM"), OP.is_equal, 3.0 ** 16, OP.mult)
     tt(s("R16"), s("E16"), c("RR", 0, 16), OP.mult)
     rsum(col("WC"), s("R16"))
@@ -454,9 +496,13 @@ def rank_program(g, core, T, topo):
     scan(s("W8", 8), s("E16", 8), c("ZERO", 0, 8), OP.mult, OP.add, col("WC"))
     ts(c("G64"), c("GI"), col("GRP"), OP.is_equal)
     for lh in range(8):
-        act(c("GW", 64 * lh, 64 * lh + 64), c("G64"), AF.Identity, 0.0, c("SM", SL["W8"] + lh, SL["W8"] + lh + 1))
-    act(c("GW", 512, 576), c("G64"), AF.Identity, 0.0, FAR)
+        act(hc("GW", lh, 64), c("G64"), AF.Identity, 0.0, c("SM", SL["W8"] + lh, SL["W8"] + lh + 1))
+    act(hc("GW", 8, 64), c("G64"), AF.Identity, 0.0, FAR)
     ts(c("TRA"), c("TRF"), col("PM"), OP.add)
+
+    def bank():
+        cnts["bank"] += 1
+        return "pD%d" % (cnts["bank"] % 4)
 
     def path(hf, lo=0):
         return c("P%d" % hf, lo, lo + 128)
@@ -464,36 +510,60 @@ def rank_program(g, core, T, topo):
     def spread(z, n, win, lst, mask):
         tt(c(z, 3, 128 * n, 4), ind(win, c(lst, 0, 2 * n)), mask, OP.mult)
 
-    def turn(pz, z, n, more=()):
-        group([(c(pz, LI + 8 * e, LI + 8 * e + 8), c(z, 128 * e + 3 - k, 128 * e + 131 - k), c("R4", 8 * k, 8 * k + 8))
-               for e in range(n) for k in range(4)] + list(more))
+    def turn(outs, z, more=()):
+        group([(o, c(z, 128 * e + 3 - k, 128 * e + 131 - k), hc("R4", k, 8)) for e, o in enumerate(outs) for k in range(4)] + list(more))
 
-    def to_list(hf, win, lst, t):
+    def to_list(hf, win, lst, t, o, z):
         at(t)
-        spread("Z%d" % hf, 1, win, lst, c("ZM", 0, 32))
+        spread(z, 1, win, lst, c("ZM", 0, 32))
         at(t + 330)
-        turn("pZ%d" % hf, "Z%d" % hf, 1)
+        turn([o], z)
         at(t + 680)
-        cp(hc("LST", hf, 8), c("pZ%d" % hf, LI, LI + 8))
+        cp(hc("LST", hf, 8), o)
 
-    def new_path(hf, terms, t):
+    def new_path(hf, d, terms, t, more):
         h = str(hf)
-        pz = "pZ" + h
-        scan(c("RO" + h, 272), c("RSM"), c("RI" + h, 272), OP.mult, OP.add)
-        ts(c("INV" + h), c("RO" + h, 272), 0.75, OP.is_gt)
-        group(terms + [(c(pz, 0, 128), c("VI"), c("INV" + h))])
-        ts(path(hf), c(pz, 0, 128), 0.0, OP.max)
-        scan(hc("UE", hf), c("INV" + h), path(hf), OP.mult, OP.add)
-        to_list(hf, hc("UE", hf), "LE", t)
+        scan(c("RO" + h, 336), c("RSM"), c("RI" + h, 336), OP.mult, OP.add)
+        ts(c("INV" + h, 0, 128), c("RO" + h, 336), 0.75, OP.is_gt)
+        group(terms + [(A(d, P8), c("VI"), c("INV" + h, 0, 128))])
+        if S16:
+            act(path(hf), A(d, P8), AF.Relu)
+        else:
+            ts(path(hf), A(d, P8), 0.0, OP.max)
+        scan(hc("UE", hf), c("INV" + h, 0, 128), path(hf), OP.mult, OP.add)
+        to_list(hf, hc("UE", hf), "LE", t, A(d, 16, P8), "ZE" + h)
         for k in range(2):
-            act(c("CAP", 16 * hf + 8 * k, 16 * hf + 8 * k + 8), hs("N2", hf), AF.Sign, 6.5 - k, -1.0)
+            act(hc("CAP", 2 * hf + k, 8), hs("N2", hf), AF.Sign, 6.5 - k, -1.0)
         for k in range(4):
-            gcp(A("PO" + h, ALL, sl(6 * k, 6 * k + 8)), c("P" + h, 1, 128, 2))
+            act(A("PO" + h, ALL, sl(6 * k, 6 * k + 8)), c("P" + h, 1, 128, 2))
         for k in range(4):
-            gcp(A("PEV" + h, ALL, sl(7 * k, 7 * k + 8)), c("P" + h, 0, 128, 2))
+            act(A("PEV" + h, ALL, sl(7 * k, 7 * k + 8)), c("P" + h, 0, 128, 2))
+        if more:
+            at(t + 1500)
+            mm(A(d, sl(8, 16)), path(hf), IH, True, True)
+            ts(hc("PU", hf), A(d, sl(8, 16)), col("ODD"), OP.add)
         at(t + 9000)
-        act(c("MK" + h), c("RO" + h, 272), AF.Abs, -1.25)
-        ts(c("MK" + h), c("MK" + h), 0.5, OP.is_lt)
+        act(c("MK" + h), c("RO" + h, 336), AF.Abs, -1.25)
+        act(c("MK" + h), c("MK" + h), AF.Relu, 1.5, -2.0)
+
+    def ramps(hf, t):
+        h = str(hf)
+        at(t)
+        scan(c("RO" + h, 18, 323), c("RST1"), c("RI" + h, 18, 323), OP.mult, OP.add)
+        at(t + 370)
+        ts(hc("RSD", hf, 152), c("RO" + h, 171, 323), 0.0, OP.is_equal, 1.0e9, OP.mult)
+
+    def edge_ends(hf):
+        pe, P = "pE%d" % hf, "P%d" % hf
+        terms = [(c(pe, 152, 456), ID, c("ZERO"))]
+        for k in range(14):
+            o = c(pe, 152 * (1 + k % 2) + k, 152 * (2 + k % 2), 19)
+            terms.append((o, IH, c(P, k, 128, 16)))
+            if k < 13:
+                terms.append((o, NH, c(P, k + 2, 128, 16)))
+        terms.append((c(pe, 152 + 13, 304, 19), IH, c(P, 14, 128, 16)))
+        group(terms)
+        act(c("DT%d" % hf), c(pe, 152, 456))
 
     def first_path(hf):
         h = str(hf)
@@ -503,119 +573,129 @@ def rank_program(g, core, T, topo):
         act(hs("N2", hf), c(pz, NN, NN + 8), AF.Identity, -0.5, 0.5)
         act(hs("th", hf), c(pz, NN + 8, NN + 16), AF.Identity, 0.0, 16.0 * U18)
         act(hs("bnd", hf), hs("th", hf))
-        act(c("RI" + h, 272, 400, 16), hs("N2", hf), AF.Identity, 0.5, -1.0)
-        new_path(hf, [(c(pz, 0, 128), hc("WH", hf), IH)], 0.0)
+        act(c("RI" + h, 336, 464, 16), hs("N2", hf), AF.Identity, 0.5, -1.0)
+        act(c("RI" + h, 19, 171, 19), hs("N2", hf), AF.Identity, 0.5, -1.0)
+        ramps(hf, 0.0)
+        d = bank()
+        new_path(hf, d, [(A(d, P8), hc("WH", hf), IH)], 0.0, True)
+        edge_ends(hf)
 
     def uf_end(hf, slot):
         return c("UF%d" % hf, 136 * slot + 16, 136 * slot + 136, 17)
 
+    def run_end(hf):
+        return c("RUN", 152 * hf + 16, 152 * hf + 136, 17)
+
     def append_one(hf, k):
         h = str(hf)
-        tt(c("U2" + h, 2) if k else c("U1" + h), ind(hc("UF" + h, k, 272), c("APL", 0, 8)), c("MK" + h), OP.mult)
+        tt(c("U2" + h, 2) if k else c("U1" + h), ind(hc("UF" + h, k, 272), c("APL")), c("MK" + h), OP.mult)
 
     def went(hf, k):
-        act(c("GO", 16 * hf + 8 * k, 16 * hf + 8 * k + 8), uf_end(hf, 2 * k + 1), AF.Sign)
-
-    def new_length(hf):
-        act(hc("NB", hf, 8), hs("N2", hf))
-        group([(c("pZ%d" % hf, NN, NN + 8), ID, x) for x in
-               (hc("NB", hf, 8), c("GO", 16 * hf, 16 * hf + 8), c("GO", 16 * hf + 8, 16 * hf + 16))])
+        act(hc("GO", 2 * hf + k, 8), uf_end(hf, 2 * k + 1), AF.Sign)
 
     def parts_of(hf):
         h = str(hf)
         return (path(hf), c("U1" + h), c("U2" + h, 0, 128))
 
     def append(hf):
-        h = str(hf)
-        pz = "pZ" + h
-        at(-900)
+        o = c("pZ%d" % hf, 272, 400)
+        at(1200)
         append_one(hf, 1)
-        at(-450)
-        group([(c(pz, 0, 128), x, IH) for x in parts_of(hf)])
-        at(-50)
-        ts(hc("PU", hf), c(pz, 0, 128), col("ODD"), OP.add)
-        at(400)
-        went(hf, 1)
-        group([(c(pz, 272, 400), IH, x) for x in parts_of(hf)])
-        cp(path(hf), c(pz, 272, 400))
-        new_length(hf)
-        act(hs("N3", hf), c(pz, NN, NN + 8), AF.Identity, -0.5)
-        act(c("TOP", 16 * hf, 16 * hf + 8), c(pz, NN, NN + 8), AF.Identity, 1.0, 2.0)
-        act(c("TOP", 16 * hf + 8, 16 * hf + 16), c(pz, NN, NN + 8), AF.Identity, 1.0)
+        group([(o, IH, x) for x in parts_of(hf)])
+        (act if S16 else cp)(path(hf), o)
 
-    def ends_table(hf):
-        pz, P = "pZ%d" % hf, "P%d" % hf
-        group([(c(pz, 136, 408), ID, c("ZERO")),
-               (c(pz, 136, 264, 2), IH, c(P, 0, 128, 2)), (c(pz, 136, 264, 2), NH, c(P, 2, 130, 2)),
-               (c(pz, 150, 264, 16), IH, c(P, 16, 144, 16)),
-               (c(pz, 273, 400, 2), IH, c(P, 1, 128, 2)), (c(pz, 273, 400, 2), NH, c(P, 3, 130, 2))])
-
-    def gather(who, kk, win, lst, t):
+    def gather(who, buf, kk, win, lst, t):
         cuts = PIECES if who == "v" else (0, 32)
         for n, (a, b) in enumerate(zip(cuts, cuts[1:])):
             at(t + GAP * n)
-            o, src = c("VG", 520 * kk + 16 * a, 520 * kk + 16 * b), ind(win, c(lst, 32 * kk + a, 32 * kk + b))
+            o, src = c(buf, 520 * kk + 16 * a, 520 * kk + 16 * b), ind(win, c(lst, 32 * kk + a, 32 * kk + b))
             if who == "S":
                 act(o, src, AF.Copy)
             else:
                 cp(o, src)
 
-    def sums(hf, k, w, stop, m, width, first):
-        pe = "pE%d" % hf
-        n = 4 // SUMS
-        if (k + 1) % n == 0:
-            lo = k + 1 - n
-            a = 2048 * hf + 512 * lo
-            for i in range(m):
-                mm(A(pe, sl(first + i, w[2] * width, width), parts=sl(32 * lo, 32 * lo + 32 * n)),
-                   c("A2", a + i, a + 512 * n, 16), w, False, stop and i == m - 1)
+    def sums(buf, hf, outs, w):
+        return [(o, c(buf, 2048 * hf + i, 2048 * hf + 2048, 16), w) for i, o in enumerate(outs)]
 
-    def edges(hf, r):
+    def edge_chunk(hf, k, who, t0, t1):
+        kk = 4 * hf + k
+        if len(who) == 1:
+            gather(who, "VE", kk, c("X"), "PU", t0)
+        for e in range(2 if len(who) == 2 else 0):
+            at(t0 - 9000 * (1 - e))
+            (act if who[e] == "S" else cp)(c("VE", 520 * kk + e, 520 * kk + 512, 2), ind((HOME, PART)[e], hc("PH", 8 * e + kk, 16)))
+        d = A(bank())
+        at(t1 - 700)
+        group([(d, ID, c("VE", 520 * kk, 520 * kk + 512)), (d, c("NI"), c("VE", 520 * kk + 1, 520 * kk + 513))])
+        at(t1)
+        act(hc("A1", kk, 512), d, AF.Abs)
+
+    def edge_keys(hf, r, t):
         pe = "pE%d" % hf
-        n = 3 if r else 1
-        at(1500)
-        mm(c(pe, 0, 128 * n), ID, c("KB", 272, 272 + 128 * n), True, False)
+        at(t)
+        terms = [(c(pe, 0, 152), ID, c("KB", 680, 832) if r else c("KB", 528, 680))]
+        terms += sums("A1", hf, [c(pe, i, 152, 19) for i in range(14)], hc("W16", 1, 8))
         if r:
-            mm(c(pe, 143, 384, 16), ID, hc("TOP", hf, 16), False, False)
-            mm(c(pe, 128, 256), ID, c("HALF"), False, False)
-        for k in range(4):
-            kk = 4 * hf + k
-            gather(PLAN_EDGE[hf][k], kk, c("X"), "PU", T_GATHER[k] - 400)
-            d = A("pD%d" % k)
-            at(T_ABS[k] - 1100)
-            group([(d, ID, c("VG", 520 * kk, 520 * kk + 512)), (d, c("NI"), c("VG", 520 * kk + 1, 520 * kk + 513))])
-            at(T_ABS[k] - 400)
-            act(c("A2", 512 * kk, 512 * kk + 512), d, AF.Abs)
-            at(T_ABS[k] + 260)
-            sums(hf, k, c("W16", 8, 8 + 8 * n), k == 3, 14, 16, 0)
-            if k == 1:
-                ends_table(hf)
-        at(2500)
-        for e in range(2):
-            tt(c("BM", 64 * hf + 32 * e, 64 * hf + 32 * e + 32), ind(hs("bnd", hf), c("L8")), c("ZN"), OP.add)
+            terms.append((c(pe, 14, 152, 19), ID, hc("ED", hf, 8)))
+            for k in range(4):
+                terms.append((c(pe, 14 + k, 152, 19), c("UI"), hc("NB", hf, 8)))
+                terms.append((c(pe, 14 + k, 152, 19), c("IF"), hc("DK", 4 * hf + k, 8)))
+            act(c("DT%d" % hf, 17, 152, 19), uf_end(hf, 3))
+            tt(c("DT%d" % hf, 16, 152, 19), uf_end(hf, 1), uf_end(hf, 3), OP.subtract)
+        group(terms)
+
+    def bounds(hf):
+        tt(hc("BM", hf, 64), ind(hs("bnd", hf), c("L8")), c("ZN"), OP.add)
+
+    def first_dead(hf):
+        h = str(hf)
+        pe = "pE" + h
+        at(-700)
+        terms = [(c(pe, 136, 392), ID, c("KB", 272, 528)), (c(pe, 136, 264), ID, c("HALF"))]
+        terms += [(c(pe, 136 + 128 * e, 264 + 128 * e), c("MI"), c("INV" + h, k, k + 128)) for e in range(2) for k in range(2)]
+        group(terms + sums("A1", hf, [c(pe, 136 + i, 392, 16) for i in range(14)], c("W16", 16, 32)))
+        at(700)
+        tt(c("M" + h), c(pe, 136, 392), c("K2"), OP.max)
+        dt = [[c("DT" + h, 152 * e + k, 152 * e + 152, 19) for k in range(19)] for e in range(2)]
+        last = c("UE", 128 * hf + 15, 128 * hf + 128, 16)
+        for o, a, b in ((dt[0][13], dt[0][13], last), (dt[0][14], last, uf_end(hf, 1)),
+                        (dt[1][13], dt[1][13], uf_end(hf, 0)), (dt[1][15], uf_end(hf, 0), uf_end(hf, 2))):
+            tt(o, a, b, OP.subtract)
+        act(dt[1][17], uf_end(hf, 2))
+        at(T_PATH + 500)
+        scan(hc("MX", hf, 256), c("RS2"), c("M" + h), OP.add, OP.min)
+        bounds(hf)
+        tt(hs("N3b", hf), hs("N2", hf), hc("GO", 2 * hf, 8), OP.add)
+        for v in range(2):
+            w = sl(8 * v, 8 * v + 8)
+            act(A("TOP" + h, 0, w), hs("N3b", hf), AF.Identity, 0.5 + 2 * v, 2.0)
+            act(A("TOP" + h, 1, w), hs("N3b", hf), AF.Identity, 1.0 + v)
+            act(hs("N3" + h, v), hs("N3b", hf), AF.Identity, v - 0.5)
+            tt(A("JH" + h, ALL, w), c("MX", 256 * hf + 15, 256 * hf + 256, 16), A("TOP" + h, ALL, w), OP.min)
+        tt(s("mx" + h), A("JH" + h, 0), s("N3" + h), OP.max)
+        tt(s("bk" + h), s("N3" + h), A("JH" + h, 0), OP.is_gt)
+        tt(A("QS" + h, 0), A("JH" + h, 1), s("mx" + h), OP.subtract)
+        tt(A("QS" + h, 1), A("JH" + h, 1), s("bk" + h), OP.mult)
+        tt(s("dq" + h), A("QS" + h, ALL, sl(8, 16)), A("QS" + h, ALL, P8), OP.subtract)
+        act(hc("NB", hf, 8), hs("N2", hf))
+        act(c("RI" + h, 19 + 14, 171, 19), hs("N2", hf), AF.Identity, -6.5)
+        act(c("RI" + h, 171 + 14, 323, 19), hs("N2", hf), AF.Identity, 6.5, -1.0)
 
     def cut(hf):
         h = str(hf)
-        ji, h1 = (c("MX", 256 * hf + 128 * k + 15, 256 * hf + 128 * k + 128, 16) for k in range(2))
-        at(4250)
-        tt(c("M" + h), c("pE" + h, 128, 384), c("K2"), OP.max)
-        at(4700)
-        scan(hc("MX", hf, 256), c("RS2"), c("M" + h), OP.add, OP.min)
-        at(5150)
-        tt(hs("mx", hf), ji, hs("N3", hf), OP.max)
-        tt(hs("back", hf), hs("N3", hf), ji, OP.is_gt)
-        at(5450)
-        tt(c("RI" + h, 16, 144, 16), h1, hs("mx", hf), OP.subtract)
+        at(-1600)
+        ts(s("go" + h), ind(c("RUN", 152 * hf, 152 * hf + 136), c("LG", 0, 1)), 65500.0, OP.is_lt)
+        at(-1250)
+        tt(s("gd" + h), s("go" + h), s("dq" + h), OP.mult)
+        at(-900)
+        tt(c("RI" + h, 19, 171, 19), hs("gd" + h, 0), A("QS" + h, 0, P8), OP.add)
         for k in range(2):
-            tt(c("RI" + h, 15 + 128 * k, 143 + 128 * k, 16), hs("back", hf), h1, OP.mult)
-        at(5850)
-        scan(c("RO" + h, 15, 272), c("RST1"), c("RI" + h, 15, 272), OP.mult, OP.add)
-        at(6200)
-        ts(hc("RSD", hf), c("RO" + h, 144, 272), 0.0, OP.is_equal, 1.0e9, OP.mult)
+            tt(c("RI" + h, 18 + 152 * k, 170 + 152 * k, 19), hs("gd" + h, 1), A("QS" + h, 1, P8), OP.add)
+        ramps(hf, -500)
 
     def pick(hf, outs, n, t, rst, beside=None):
         e = c("pE%d" % hf, 0, n)
-        run, ne = c("RUN", 136 * hf, 136 * hf + n), c("NE1", 136 * hf, 136 * hf + n)
+        run, ne = c("RUN", 152 * hf, 152 * hf + n), c("NE1", 152 * hf, 152 * hf + n)
         at(t)
         scan(run, rst, e, OP.add, OP.min)
         at(t + 350)
@@ -623,82 +703,114 @@ def rank_program(g, core, T, topo):
         if beside:
             beside(run)
         at(t + 700)
-        for k, o in enumerate(outs):
-            scan(o, ne, c("pZ%d" % hf, 136 * k + 136, 136 * k + 136 + n), OP.mult, OP.add)
+        for o, d in outs:
+            scan(o, ne, d, OP.mult, OP.add)
 
     def least(hf, r):
         h = str(hf)
-        e = c("pE" + h, 0, 128)
-        t = 6200 if r else 4250
+        e = c("pE" + h, 0, 152)
+        t = -100 if r else 4450
         at(t)
-        tt(e, e, c("RO" + h, 16, 144) if r else c("RO" + h, 272), OP.max)
-        pick(hf, [hc("UAB" + h, 0), hc("UAB" + h, 1)], 128, t + 350, hc("RSD", hf),
+        tt(e, e, c("RO" + h, 19, 171), OP.max)
+        pick(hf, [(hc("UAB" + h, k, 152), hc("DT" + h, k, 152)) for k in range(2)], 152, t + 370, hc("RSD", hf, 152),
              lambda run: tt(hc("PR", hf, 64), ind(run, c("LR")), hc("BM", hf, 64), OP.is_lt))
         return t + 1500
 
-    def shift(hf, t):
+    def shift(hf, t, more):
         h = str(hf)
-        pz = "pZ" + h
-        q = c("RI" + h, 16, 144, 16)
+        q = c("RI" + h, 19, 171, 19)
+        p40 = sl(0, 40)
         at(t)
-        ts(c("RI" + h, 272, 400, 16), q, 0.5, OP.min)
-        act(hs("N2", hf), c("RI" + h, 272, 400, 16), AF.Identity, 0.5, -1.0)
+        act(hs("N2", hf), q, AF.Relu, 0.5, -1.0)
+        act(c("RI" + h, 336, 464, 16), hs("N2", hf), AF.Identity, 0.5, -1.0)
         act(hs("none", hf), q, AF.Relu, -0.5)
         ts(hs("dm", hf), c("P" + h, 0, 128, 16), float(TRASH - 97), OP.is_ge, -float(NV), OP.mult)
         act(hs("dm2", hf), hs("dm", hf), AF.Identity, 97.0)
         tt(hc("DL", hf, 8), hs("dm2", hf), hs("none", hf), OP.mult)
         tt(hc("OH", hf, 48), ind(c("RI" + h), c("REP", 0, 3)), c("SCN"), OP.is_equal)
-        terms = []
-        for k in range(5):
-            y = c("YS" + h, 128 * k, 128 * k + 128)
-            tt(y, ind(c("OH", 48 * hf + 8 * k, 48 * hf + 8 * k + 8), c("BCL")), path(hf, 2 * k), OP.mult)
-            terms.append((c(pz, 0, 128), IH, y))
-        new_path(hf, terms + [(c(pz, 0, 128, 16), IH, hc("DL", hf, 8))], t + 2200)
+        d = bank()
+        hot = A("OT", sl(128 * hf, 128 * hf + 128), parts=p40)
+        mm(A(d, P8, parts=p40), c("OH", 48 * hf, 48 * hf + 40), ID, True, True)
+        act(hot, A(d, P8, parts=p40))
+        for ks in ((0, 1, 2, 3), (4,)):
+            d = bank()
+            terms = []
+            for n, k in enumerate(ks):
+                o = A(d, sl(8 * n, 8 * n + 8))
+                terms += [(o, IH, path(hf, 2 * k)), (o, hot, A("SEL", sl(128 * k, 128 * k + 128), parts=p40))]
+            group(terms)
+            act(c("YS" + h, 128 * ks[0], 128 * ks[-1] + 128), A(d, sl(0, 8 * len(ks))), AF.Relu, -4096.0)
+        d = bank()
+        terms = [(A(d, P8), IH if S16 else c("IF"), hc("YS" + h, k)) for k in range(5)]
+        new_path(hf, d, terms + [(A(d, P8, 0), IH, hc("DL", hf, 8))], t + 2200, more)
 
     def propose(hf, r, t):
         h = str(hf)
         pz, pe = "pZ" + h, "pE" + h
         ab = hc("ABU", hf, 16)
         both = c(pz, LI, LI + 16)
+        ends = [c(pz, LI + 8 * e, LI + 8 * e + 8) for e in range(2)]
         at(t)
         spread("Z" + h, 2, c("UAB" + h), "LA", hc("PR", hf, 64))
         at(t + 370)
-        turn(pz, "Z" + h, 2)
+        turn(ends, "Z" + h)
         at(t + 830)
         cp(ab, both)
         at(t + 1120)
-        act(s("AS" + h), both)
-        cp(hc("ROW", hf, 256), ind(c("IOT"), ab))
-        act(hc("XA", hf), ind(HOME, c("ABU", 16 * hf, 16 * hf + 8)), AF.Copy)
-        act(hc("XS", hf), ind(PART, c("ABU", 16 * hf + 8, 16 * hf + 16)), AF.Copy)
-        d = A("pD%d" % (3 * hf), P8)
-        group([(d, ID, x) for x in (c("HALF"), hc("XA", hf), hc("XS", hf))])
+        act(s("AS" + h), both, AF.Identity, 0.0, -1.0)
+        cp(hc("ROW", 2 * hf), ind(c("IOT"), hc("ABU", 2 * hf, 8)))
+        act(hc("ROW", 2 * hf + 1), ind(c("IOT"), hc("ABU", 2 * hf + 1, 8)))
+        act(A("MID%d" % r, hf, sl(128, 144)), s("AS" + h), AF.Identity, 0.0, -1.0)
+        act(hc("XA", hf), ind(HOME, hc("ABU", 2 * hf, 8)), AF.Relu, 255.0, -1.0)
+        act(hc("XS", hf), ind(PART, hc("ABU", 2 * hf + 1, 8)), AF.Relu)
+        d = c(pz, 0, 128)
+        group([(d, ID, c("HALF")), (d, ID, c("TOPF")), (d, c("NI"), hc("XA", hf)), (d, ID, hc("XS", hf))])
         act(hc("XR", hf), d, AF.Identity, MAGIC, 0.5)
-        act(hc("MID%d" % r, hf), hc("XR", hf), AF.Identity, -MAGIC)
-        if hf:
-            send(c("RM%d" % r), c("MID%d" % r))
+        act(A("MID%d" % r, hf, sl(0, 128)), hc("XR", hf), AF.Identity, -MAGIC)
+        send(A("RM%d" % r, hf), A("MID%d" % r, hf), low, REARLY)
         at(t + 200)
-        ts(hc("DAB", hf, 64), ind(c("UAB" + h), c("LA")), col("T" + h), OP.subtract)
-        ts(hc("TP", hf, 64), hc("PR", hf, 64), col("THR"), OP.mult, 4.0, OP.mult)
+        act(hc("DAB", hf, 64), ind(c("UAB" + h), c("LA")), AF.Identity, col("T" + h))
+        act(hc("TP", hf, 64), hc("PR", hf, 64), AF.Identity, 0.0, col("THR"))
         at(t + 1700)
         todo = [(e, c("SM", SL["AS%d" % sh] + 8 * e + lh, SL["AS%d" % sh] + 8 * e + lh + 1), lh if sh == hf else 8)
                 for sh in range(hf + 1) for lh in range(8) for e in range(2)]
-        votes = c(pe, 384, 448)
+        votes = c(pe, 0, 64)
         for k, (e, val, w) in enumerate(todo):
             eq = hc("EQ", 16 * hf + k)
-            ts(eq, c("ROW", 256 * hf + 128 * e, 256 * hf + 128 * e + 128), val, OP.is_equal)
-            mm(votes, eq, c("GW", 64 * w, 64 * w + 64), k == 0, k == len(todo) - 1)
+            if hf and len(todo) - k <= 2 * EQ_S and e:
+                gap = hc("AB", (len(todo) - k) // 2)
+                act(gap, hc("ROW", 2 * hf + e), AF.Abs, val)
+                act(eq, gap, AF.Relu, 1.0, -1.0)
+            else:
+                ts(eq, hc("ROW", 2 * hf + e), val, OP.add, 0.0, OP.is_equal)
+            mm(votes, eq, hc("GW", w, 64), k == 0, k == len(todo) - 1)
         tt(hc("WM", hf, 64), votes, hc("TP", hf, 64), OP.is_lt)
         tt(c("ZL" + h, 3, 256, 4), hc("DAB", hf, 64), hc("WM", hf, 64), OP.mult)
-        turn(pz, "ZL" + h, 2, [(both, IH, hc("TRA", hf, 16))])
+        turn(ends, "ZL" + h, [(both, IH, hc("TRA", hf, 16))])
+        cp(A("LS%d" % r, hf), both)
+        cnts["list"] = len(ops) - 1
+        send(A("RL%d" % r, hf), A("LS%d" % r, hf), low, RLAT if hf else REARLY)
+        if hf and not r:
+            sent = len(ops) - 2
+            for k in range(2):
+                gcp(c("CP", OFF + 880 * k, OFF + 880 * k + 880), hc("CR", k, 880))
+                behind(sent)
         cp(A("LU%d" % r, ALL, sl(8 * hf, 8 * hf + 8)), both)
-        if hf:
-            send(A("RL%d" % r), A("LU%d" % r))
 
     def apply_merges(r):
-        scat(PART, A("RL%d" % r, 0), c("RM%d" % r))
+        at(T_OWN)
+        scat(PART, A("RL%d" % r, 0, P8), A("RM%d" % r, 0, sl(0, 128)))
+        behind(cnts["list"])
         scat(PART, A("LU%d" % r, 1), c("NEG"))
-        scat(HOME, A("RL%d" % r, 1), c("BIG"))
+        for hf in range(2):
+            scat(HOME, A("LU%d" % r, 0, sl(8 * hf, 8 * hf + 8)), A("MID%d" % r, hf, sl(0, 128)))
+        cp(c("RA"), A("RM%d" % r, 1, sl(128, 136)))
+        act(c("KF"), ind(PART, c("RA")), AF.Relu, 0.0, -1.0)
+        tt(c("MV"), A("RM%d" % r, 1, sl(0, 128)), c("KF"), OP.subtract)
+        scat(HOME, A("RL%d" % r, 0, sl(8, 16)), c("BIG"))
+        at(T_OWN + 2500)
+        scat(PART, A("RL%d" % r, 1, P8), c("MV"))
+        scat(HOME, A("RL%d" % r, 1, sl(8, 16)), c("BIG"))
 
     def count():
         a = c("pZ1", NN + 16, NN + 32)
@@ -709,53 +821,74 @@ def rank_program(g, core, T, topo):
         ts(col("A8"), c("SI", 9, 10), 128.0 * U18, OP.mult)
         act(s("bnd"), s("th"), AF.Identity, col("A8"))
 
-    def hop(slot, hf, beside):
+    def hop(slot, hf, beside, last):
         h = str(hf)
         first = slot % 2 == 0
         tab, mine, other = (c("CH"), HOME, PART) if first else (c("CP"), PART, HOME)
         lst = hc("LST", hf, 8)
         pz, pe = "pZ" + h, "pE" + h
+        ends = c("Y2", 256 * hf, 256 * hf + 256, 2)
+        by_s = Y2_ON[slot][hf] == "S"
         at(240)
         ts(hc("CU", hf), ind(tab, lst), float(OFF), OP.add)
-        if Y2_ON[hf] == "S":
-            act(c("Y2", 256 * hf, 256 * hf + 256, 2), ind(mine, lst), AF.Relu, 255.0, -1.0)
+        if by_s:
+            act(ends, ind(mine, lst), AF.Relu, 255.0, -1.0)
         else:
-            ts(c("Y2", 256 * hf, 256 * hf + 256, 2), ind(mine, lst), 255.0, OP.subtract, 0.0, OP.min)
+            ts(ends, ind(mine, lst), 255.0, OP.subtract, 0.0, OP.min)
         at(670)
-        cp(hc("CF", hf), hc("CU", hf))
+        gcp(hc("CF", hf), hc("CU", hf))
         at(T_DUP)
-        cp(c("Y2", 256 * hf + 1, 256 * hf + 256, 2), c("Y2", 256 * hf, 256 * hf + 256, 2))
+        cp(c("Y2", 256 * hf + 1, 256 * hf + 256, 2), ends)
+        if slot == 0 and not last:
+            at(-2000)
+            edge_ends(hf)
+        if slot == 3 and not last:
+            first_dead(hf)
         at(900)
-        mm(c(pe, 0, 136), ID, c("KB", 0, 136) if first else c("KB", 136, 272), True, False)
-        if first:
-            mm(c(pe, 0, 136, 17), c("CI"), c("CAP", 16 * hf + 4 * slot, 16 * hf + 4 * slot + 8), False, False)
-        group([(c(pz, 0, 272), hc("CF", hf), c("DM")), (c(pz, 0, 136, 17), ID, c("NEG", 0, 8))])
+        mm(c(pz, 0, 272), hc("CF", hf), c("DM"), True, True)
         at(T_PATH + 400)
         for f in beside:
             f()
+        if slot == 0 and not last:
+            o = c(pz, NN, NN + 8)
+            mm(o, ends, hc("W16", 0, 8), True, True)
+            act(hc("ED", hf, 8), o, AF.Relu, 1.0, -1.0 if by_s else 1.0)
         for k in range(4):
             kk = 4 * hf + k
-            gather(PLAN_HOP[hf][k], kk, other, "CU", T_GATHER[k])
-            d = "pD%d" % k
+            gather((PLAN_END if last else PLAN_HOP)[slot][hf][k], "VG", kk, other, "CU", T_GATHER[k])
+            d = bank()
             at(T_ABS[k] - 900)
             for t in range(8):
-                mm(A(d, ALL, sl(2 * t, 2 * t + 2)), ID if Y2_ON[hf] == "S" else c("NI"), c("Y2", 64 * kk, 64 * kk + 64), t == 0, False)
+                mm(A(d, ALL, sl(2 * t, 2 * t + 2)), ID if by_s else c("NI"), hc("Y2", kk, 64), t == 0, False)
             at(T_ABS[k] - 460)
             mm(A(d), ID, c("VG", 520 * kk, 520 * kk + 512), False, True)
             at(T_ABS[k])
-            act(c("A2", 512 * kk, 512 * kk + 512), A(d), AF.Abs, -255.0)
-            if k == 2:
-                for j in range(6 if first else 7):
-                    o = hc("EQH", 2 * j + hf, 136)
-                    at(T_PATH + j)
-                    tt(o, c(pz, 0, 136), A(("PO" if first else "PEV") + h, ALL, sl(j, j + 17)), OP.is_equal)
-                    at(T_PATH + 1200 + j)
-                    mm(c(pe, 0, 136), c("BI"), o, False, False)
-            at(T_ABS[k] + 660)
-            sums(hf, k, c("W16", 0, 8), k == 3, 16, 17, 1)
-        pick(hf, [c("UF" + h, 136 * slot, 136 * slot + 136)], 136, T_PICK, c("RSTB"))
+            act(hc("A2", kk, 512), A(d), AF.Abs, -255.0)
+        for j in range(6 if first else 7):
+            o = hc("EQH", 2 * j + hf, 136)
+            at(T_PATH + j)
+            tt(o, c(pz, 0, 136), A(("PO" if first else "PEV") + h, ALL, sl(j, j + 17)), OP.is_equal)
+            at(T_PATH + 1200 + j)
+            mm(c(pe, 0, 136), c("BI"), o, j == 0, False)
+        mm(c(pe, 0, 136, 17), c("CI"), hc("CAP", 2 * hf + slot // 2, 8) if first else c("ONES", 0, 8), False, False)
+        at(T_ABS[3] + 660)
+        for i, (o, l, w) in enumerate(sums("A2", hf, [c(pe, 1 + i, 136, 17) for i in range(16)], hc("W16", 0, 8))):
+            mm(o, l, w, False, i == 15)
+        if not last:
+            for n, k in enumerate([k for k in range(4) if OLD_AT[hf][k] == slot]):
+                edge_chunk(hf, k, PLAN_OLD[hf][k], T_OLD[0] + 700 * n, T_OLD[1] + 430 * n)
+        pick(hf, [(hc("UF" + h, slot, 136), c(pz, 136, 272))], 136, T_PICK, c("RSTB"),
+             (lambda run: last_gate(hf)) if last and slot == 3 else None)
+        if not last:
+            at(T_PICK + 360)
+            act(hs("yd", hf), run_end(hf), AF.Identity, MAGIC, 1.0 / 16.0)
+            act(hc("DK", 4 * hf + slot, 8), hs("yd", hf), AF.Identity, -MAGIC * 16.0 * U18, 16.0 * U18)
         if slot < 3:
-            to_list(hf, c("UF" + h, 136 * slot, 136 * slot + 136), "LZ", T_PICK + 1050)
+            to_list(hf, hc("UF" + h, slot, 136), "LZ", T_PICK + 1050, c(pz, LI, LI + 8), "Z" + h)
+
+    def last_gate(hf):
+        ts(hc("GO", 2 * hf + 1, 8), run_end(hf), 65500.0, OP.is_lt)
+        tt(uf_end(hf, 2), uf_end(hf, 2), hc("GO", 2 * hf + 1, 8), OP.mult)
 
     def bar(hf, slot):
         name, n = (("PO", 6), ("PEV", 7))[slot]
@@ -768,24 +901,22 @@ def rank_program(g, core, T, topo):
 
     def result(hf):
         h = str(hf)
-        pz = "pZ" + h
-        went(hf, 1)
-        tt(uf_end(hf, 2), uf_end(hf, 2), c("GO", 16 * hf + 8, 16 * hf + 16), OP.mult)
+        o = c("pZ" + h, 0, 128)
         append_one(hf, 1)
-        group([(c(pz, 0, 128), x, IH) for x in parts_of(hf)])
-        act(hc("WL", hf), c(pz, 0, 128), AF.Relu, -float(OFF))
+        group([(o, x, IH) for x in parts_of(hf)])
+        act(hc("WL", hf), o, AF.Relu, -float(OFF))
         dma(T.yw[:, 128 * hf:128 * hf + 128], hc("WL", hf), 65536)
-        new_length(hf)
-        act(hc("NB", hf, 8), c(pz, NN, NN + 8), AF.Identity, 1.0, 2.0)
-        mm(A(pz, sl(136, 264), parts=P8), hc("NB", hf, 8), ID, True, True)
-        act(A("WN", sl(128 * hf, 128 * hf + 128), parts=P8), A(pz, sl(136, 264), parts=P8))
+        act(hc("NB", hf, 8), hs("N2", hf), AF.Identity, 0.5)
+        o = A("pE" + h, sl(0, 128), parts=P8)
+        group([(o, x, c("TWO")) for x in (hc("NB", hf, 8), hc("GO", 2 * hf, 8), hc("GO", 2 * hf + 1, 8))])
+        act(A("WN", sl(128 * hf, 128 * hf + 128), parts=P8), o)
         if hf:
             dma(T.yn[:], A("WN", ALL, parts=P8), 8192)
 
     def after_pair(hf, last):
         went(hf, 0)
         if last:
-            tt(uf_end(hf, 0), uf_end(hf, 0), c("GO", 16 * hf, 16 * hf + 8), OP.mult)
+            tt(uf_end(hf, 0), uf_end(hf, 0), hc("GO", 2 * hf, 8), OP.mult)
         append_one(hf, 0)
 
     first_path(0)
@@ -797,21 +928,21 @@ def rank_program(g, core, T, topo):
         for hf in range(2):
             cnts["base"] = base + HALF * hf
             if r:
+                cut(hf)
+                edge_keys(hf, r, -1200)
                 append(hf)
-            edges(hf, r)
+            else:
+                for k in range(4):
+                    edge_chunk(hf, k, PLAN_EDGE[hf][k], T_GATHER[k] - 400, T_ABS[k] - 400)
+                bounds(hf)
+                edge_keys(hf, r, 3500)
         for hf in range(2):
             cnts["base"] = base + HALF * hf
+            t = least(hf, r)
             if r:
-                cut(hf)
-            propose(hf, r, least(hf, r))
-        cnts["base"] = base
-        if r:
-            shift(0, T_SHIFT[0])
-        at(T_OWN)
-        scat(HOME, A("LU%d" % r, 0), c("MID%d" % r))
-        if r:
-            shift(1, T_SHIFT[1])
-        at(T_OWN + 2500)
+                shift(hf, T_SHIFT, not last)
+            propose(hf, r, t)
+        cnts["base"] = base - (5600 if r else 0)
         apply_merges(r)
         for slot in range(4):
             for hf in range(2):
@@ -819,11 +950,11 @@ def rank_program(g, core, T, topo):
                 beside = []
                 if slot in (1, 2):
                     beside.append(lambda: bar(hf, slot - 1))
-                if slot == 3:
+                if slot == 2:
                     beside.append(lambda: after_pair(hf, last))
-                if slot == 1 and hf:
+                if slot == (2 if last else 1) and hf:
                     beside.append(points_out if last else count)
-                hop(slot, hf, beside)
+                hop(slot, hf, beside, last)
     for hf in range(2):
         cnts["base"] = 100000.0 * ROUNDS + HALF * hf
         at(-900)

import numpy as np
from concourse.mybir import AluOpType, AxisListType, ActivationFunctionType

NV, NL, ROUNDS = 1760, 256, 3
OFF, TRASH, WIN = 16, 1776, 2032
B17 = 131072.0
BIGH, BIGP = 262144.0, -131072.0
MAGIC = 12582912.0
U18 = 2.0 ** -18
FAR = 2.0 ** 99
LI, NN = 408, 424
PLAN_HOP = [("VSSv", "VSSv")] * 4
PLAN_END = [("SVSv", "SVSv")] * 4
PLAN_EDGE = (("SV", "VS", "SV", "VV"), ("SV", "VV", "SV", "VV"))
EQ_S = 3
PLAN_OLD = ("SvSv", "vSvv")
OLD_AT = ((0, 1, 2, 2), (0, 1, 2, 2))
Y2_ON = ("SV", "VV", "VV", "VV")
S16 = True
NP = 4
PIECES, GAP = (0, 12, 22, 32), 350
HALF = 3300.0
T_GATHER, T_ABS = (680, 680, 1340, 1460), (2020, 2445, 2870, 3295)
T_DUP, T_PATH, T_PICK = 660, 2490, 4645
T_OLD = (2100, 3800)
T_SHIFT, T_OWN = 2000, 17000
RCALL, RLAT, GA, SC, PEC, LAT, VF = 800.0, 2500.0, 1.4, 3.5, 0.43, 250.0, 0.0
REARLY = 3000.0
PASSES, SHAKE = 24, 100.0

SLOTS = ["N2", "N30", "N31", "mx0", "mx1", "bk0", "bk1", "dq0", "dq1", "gd0", "gd1", "go0", "go1", "N3b", "yd", "th", "bnd", "none",
         "dm", "dm2", "AS0", "AS1", "CF0", "CF1", "col", "col2", "G8", "P4", "W8", "E16", "R16"]
SL = {k: 16 * i for i, k in enumerate(SLOTS)}
COLS = {k: i for i, k in enumerate(("PM", "GRP", "PM4", "P3", "P7", "EVN", "ODD", "T0", "T1", "ACT", "A8", "THR", "WC", "C17", "C16",
                                    "P", "C19"))}

F32, BF, F16, I32, U16 = "float32", "bfloat16", "float16", "int32", "uint16"
SB = {
    "X": ([2 * WIN], BF), "CH": ([TRASH], I32), "CP": ([TRASH], F32), "CS": ([NV], F16), "CR": ([NV], F16), "XO": ([NV], BF), "IOT": ([TRASH], F32),
    "SM": ([16 * len(SLOTS)], F32), "SI": ([16], I32), "WI": ([256], I32), "WH": ([256], F16), "NT": ([512], I32),
    "NF": ([512], F32), "WL": ([256], F32), "WN": ([256], F32),
    "EQ": ([128 * 48], BF), "ROW": ([512], F16), "ABU": ([32], U16), "PU": ([256], U16), "PH": ([256], U16),
    "RA": ([8], U16), "KF": ([128], BF), "MV": ([128], BF), "AB": ([128 * 8], F16),
    "VG": ([8 * 520], BF), "A2": ([4096], BF), "VE": ([8 * 520], BF), "A1": ([4096], BF),
    "Y2": ([512], BF), "CU": ([256], U16), "CF": ([256], F16), "LST": ([16], U16), "EQH": ([14 * 136], BF),
    "XA": ([256], BF), "XS": ([256], BF), "XR": ([256], F32), "CAP": ([32], BF), "DK": ([64], F32), "ED": ([16], BF),
    "GO": ([32], BF), "NB": ([16], BF), "DL": ([16], F16), "WM": ([128], BF), "BM": ([128], F32), "PR": ([128], F32),
    "TP": ([128], F32), "RSD": ([304], F32), "DAB": ([128], F32), "RUN": ([304], F32), "NE1": ([304], F32),
    "MX": ([512], F32), "UE": ([256], F32), "OH": ([96], BF), "OT": ([256], BF), "SEL": ([640], BF),
}
CONST = {
    F32: {"KM": 128, "T17": 272, "T19": 152, "V1": 136, "K16": 128, "H4": 64, "GI": 64, "TRF": 32, "SCN": 48, "RR": 128, "TA": 136,
          "TB": 136, "IF": 128, "RSTB": 136, "ZM": 64, "ZN": 64, "G64": 64, "K2": 256, "RS2": 256, "SEF": 640, "V2": 128},
    BF: {"ID": 128, "NI": 128, "BI": 128, "CI": 128, "VI": 128, "MI": 128, "UI": 128, "TWO": 128, "ONES": 128, "HALF": 128, "TOPF": 128,
         "ZERO": 304, "W16": 32, "KB": 832, "RST1": 305, "RSM": 128, "GW": 576, "NEG": 256, "BIG": 128},
    F16: {"IH": 128, "NH": 128, "DM": 272, "R4": 32, "TRA": 32, "PK": 512},
    U16: {"LZ": 2, "LE": 2, "LA": 4, "LR": 4, "L8": 4, "LG": 2, "REP": 4, "APL": 8},
}
for _h in range(2):
    for _k, _v in (("P", ([144], F16)), ("U1", ([128], F16)), ("U2", ([130], F16)), ("UF", ([544], F32)), ("UAB", ([304], F32)),
                   ("DT", ([304], F32)), ("RI", ([464], BF)), ("RO", ([464], BF)), ("INV", ([130], BF)), ("MK", ([128], BF)),
                   ("M", ([256], F32)), ("PO", ([8, 26], F16)), ("PEV", ([8, 30], F16)), ("YS", ([640], F16 if S16 else F32)),
                   ("Z", ([260], F16)), ("ZL", ([260], F16)), ("ZE", ([132], F16)),
                   ("TOP", ([2, 16], F32)), ("JH", ([2, 16], F32)), ("QS", ([2, 16], F32))):
        SB[_k + str(_h)] = _v
for _r in range(ROUNDS):
    SB["MID%d" % _r] = ([2, 144], F16)
    SB["RM%d" % _r] = ([2, 144], F16)
    for _k in ("LU", "LS", "RL"):
        SB[_k + str(_r)] = ([2, 16], U16)
SHAPE = dict(SB)
POOL = {}
for _t, _names in CONST.items():
    _at = 0
    for _k, _n in _names.items():
        POOL[_k] = ("K" + _t, _at)
        SHAPE[_k] = ([_n], _t)
        _at += (_n + 15) // 16 * 16
    SB["K" + _t] = ([_at], _t)
SCRATCH = {k: ("sbuf", [128] + v[0], v[1]) for k, v in SB.items()}
for _r in range(2):
    SCRATCH["pZ%d" % _r] = ("psum", [128, 512], F32)
    SCRATCH["pE%d" % _r] = ("psum", [128, 512], F32)
for _r in range(4):
    SCRATCH["pD%d" % _r] = ("psum", [128, 32, 16], F32)
for _k, _v in SCRATCH.items():
    SHAPE[_k] = (_v[1][1:], _v[2])
SEMAPHORES = ["sV", "sS", "sP", "sG"] + ["d%d" % i for i in range(40)] + ["r%d" % i for i in range(24)]
OP = AluOpType
AF = ActivationFunctionType
ALL = slice(None)
ESEM = {"V": "sV", "S": "sS", "P": "sP", "G": "sG"}
EXT = {}
PLAN = {}


def find_waits(ops):
    acc = {}
    hard = [set() for _ in ops]
    soft = [set() for _ in ops]
    for i, o in enumerate(ops):
        hard[i] |= set(o["after"])
        mine = [(nm, "rd", m) for nm, m in o["rd"]] + [(nm, o["wk"], m) for nm, m in o["wr"]]
        for (nm, kind, m) in mine:
            psum = nm[0] == "p"
            for (j, k2, m2) in acc.get(nm, []):
                oj = ops[j]
                same = oj["q"] == o["q"] and oj["sem"] is None and o["sem"] is None
                if psum and not same:
                    hard[i].add(j)
                elif psum and o["q"] == "P":
                    if kind != "acc" or k2 != "acc":
                        soft[i].add(j)
                elif (m & m2) and (kind != "rd" or k2 != "rd"):
                    hard[i].add(j)
        for (nm, kind, m) in mine:
            lst = acc.setdefault(nm, [])
            if kind == "wr" and nm[0] != "p":
                lst[:] = [e for e in lst if e[2] & ~m]
            if nm[0] == "p" and lst and ops[lst[-1][0]]["q"] != o["q"]:
                last = ops[lst[-1][0]]["q"]
                k = len(lst)
                while k and ops[lst[k - 1][0]]["q"] == last:
                    k -= 1
                del lst[:k]
            lst.append((i, kind, m))
    return hard, soft


def place(ops, before, key, head):
    n = len(ops)
    after = [[] for _ in ops]
    left = [len(b) for b in before]
    for i in range(n):
        for j in before[i]:
            after[j].append(i)
    rdy = list(head)
    start = [0.0] * n
    busy = {}
    ready = sorted((key[i], i) for i in range(n) if not left[i])
    while ready:
        i = ready.pop(0)[1]
        cost = ops[i]["cost"]
        line = busy.setdefault(ops[i]["q"], [])
        t = rdy[i]
        k = len(line)
        while k and line[k - 1][1] > t:
            k -= 1
        while k < len(line) and line[k][0] < t + cost:
            t = max(t, line[k][1])
            k += 1
        line.insert(k, (t, t + cost))
        start[i] = t
        fresh = False
        for m in after[i]:
            rdy[m] = max(rdy[m], t + cost + before[m][i])
            left[m] -= 1
            if not left[m]:
                ready.append((key[m], m))
                fresh = True
        if fresh:
            ready.sort()
    return start


def order_calls(ops):
    n = len(ops)
    hard, soft = find_waits(ops)
    for i in range(n):
        if "lead" in ops[i]:
            hard[i].discard(ops[i]["lead"])
            soft[i].add(ops[i]["lead"])
    fore = [{j: (ops[j]["lat"] + LAT if j in hard[i] else 0.0) for j in hard[i] | soft[i]} for i in range(n)]
    back = [{} for _ in ops]
    for i in range(n):
        for j, d in fore[i].items():
            back[j][i] = d
    key = [o["t"] for o in ops]
    for i in range(n - 1, -1, -1):
        if not ops[i]["inorder"]:
            key[i] = min([key[k] - ops[i]["cost"] - d for k, d in back[i].items()] + [1.0e9])
    best = None
    for turn in range(PASSES):
        start = place(ops, fore, key, [0.0] * n)
        end = max(start[i] + ops[i]["cost"] + ops[i]["lat"] for i in range(n))
        if best is None or end < best[0]:
            best = (end, start)
        late = place(ops, back, [-start[i] - ops[i]["cost"] for i in range(n)], [o["lat"] for o in ops])
        key = [-late[i] - ops[i]["cost"] for i in range(n)]
        if turn % 3 == 2:
            key = [best[1][i] + SHAKE * (((i * 7919 + turn * 104729) * 2654435761 % 4096) / 4096.0 - 0.5) for i in range(n)]
    order = sorted(range(n), key=lambda i: (best[1][i], i))
    pos = {i: t for t, i in enumerate(order)}
    seen = {}
    waits = {}
    sig = set()
    for i in order:
        o = ops[i]
        waits[i] = []
        if o["q"][0] == "R":
            continue
        need = {}
        for j in hard[i]:
            key = ops[j]["sem"][0] if ops[j]["sem"] else ESEM[ops[j]["q"]]
            if key not in need or pos[j] > pos[need[key]]:
                need[key] = j
        sq = seen.setdefault(o["q"], {})
        for key in sorted(need):
            if sq.get(key, -1) < pos[need[key]]:
                sq[key] = pos[need[key]]
                waits[i].append((key, need[key]))
                sig.add(need[key])
    return order, waits, sig


def rank_program(g, core, T, topo):
    rank = T.rank_of(core)
    if rank is None:
        return
    mate = T.cores[(rank + len(T.cores) // 2) % len(T.cores)]
    rid, pid = topo.addr(mate, core)
    engs = topo.engines(core, mate)
    low = engs[:len(engs) // 2]
    ops = []
    cnts = {"d": 0, "r": 0, "main": False, "t": 0.0, "base": 0.0, "bank": -1}

    def A(name, *idx, parts=ALL):
        key = (name, str(idx))
        if key not in EXT:
            shp = SHAPE[name][0]
            ext = np.arange(int(np.prod(shp))).reshape(shp)[tuple(idx)].reshape(-1)
            m = 0
            for e in ext.tolist():
                m |= 1 << e
            EXT[key] = (m, len(ext))
        if name in POOL:
            buf, a0 = POOL[name]
            ap = T[buf][parts, a0 + idx[0].start:a0 + idx[0].stop:idx[0].step]
        else:
            ap = T[name][(parts,) + tuple(idx)]
        return (ap, [(name, EXT[key][0])], EXT[key][1], 4 if SHAPE[name][1] in (F32, I32) else 2, False)

    def c(name, lo=0, hi=None, st=None):
        if hi is None:
            hi = SHAPE[name][0][0]
        return A(name, slice(lo, hi, st))

    def sl(a, b, st=None):
        return slice(a, b, st)

    def s(k, n=16):
        return c("SM", SL[k], SL[k] + n)

    def hs(k, hf):
        return c("SM", SL[k] + 8 * hf, SL[k] + 8 * hf + 8)

    def col(k):
        return c("SM", SL["col"] + COLS[k], SL["col"] + COLS[k] + 1)

    def hc(name, hf, n=128):
        return c(name, n * hf, n * hf + n)

    def ind(win, off):
        return (win[0].indirect(off[0]), win[1] + off[1], 16 * off[2], win[3], True)

    def add(q, fn, outs, ins, cost, sem=None, lat=0.0, wk="wr", after=()):
        rd = []
        for a in ins:
            if isinstance(a, tuple):
                rd += a[1]
        wr = []
        for a in outs:
            wr += a[1]
        ops.append({"q": q, "fn": fn, "rd": rd, "wr": wr, "sem": sem, "cost": cost, "lat": lat, "wk": wk, "after": list(after),
                    "inorder": cnts["main"], "t": cnts["t"]})
        cnts["t"] += 1.0

    def at(t):
        cnts["t"] = cnts["base"] + t

    def behind(j, i=-1):
        ops[i]["after"].append(j)
        ops[i]["lead"] = j

    def p(a):
        return a[0] if isinstance(a, tuple) else a

    def vc(o, a, k=1.0):
        if a[4]:
            return 50 + 0.83 * GA * o[2]
        return VF + 0.83 * max(64, o[2] * k * (0.5 if o[3] == 2 and a[3] == 2 else 1.0))

    def cp(o, i):
        add("V", lambda: g.vector.tensor_copy(o[0], i[0]), [o], [i], vc(o, i))

    def scat(win, off, i):
        add("V", lambda: g.vector.tensor_copy(win[0].indirect(off[0]), i[0]), [win], [off, i], 50 + 0.83 * SC * i[2])

    def tt(o, a, b, op):
        k = 1.0 if "p" in (a[1][0][0][0], b[1][0][0][0]) else 2.0
        add("V", lambda: g.vector.tensor_tensor(o[0], a[0], b[0], op), [o], [a, b], vc(o, a, k))

    def ts(o, a, s1, op0, s2=None, op1=None):
        if op1 is None:
            add("V", lambda: g.vector.tensor_scalar(o[0], a[0], p(s1), None, op0), [o], [a, s1], vc(o, a))
        else:
            add("V", lambda: g.vector.tensor_scalar(o[0], a[0], p(s1), p(s2), op0, op1), [o], [a, s1, s2], vc(o, a))

    def scan(o, d0, d1, op0, op1, init=0.0):
        add("V", lambda: g.vector.tensor_tensor_scan(o[0], d0[0], d1[0], p(init), op0, op1), [o], [d0, d1, init],
            VF + 0.83 * max(64, o[2] * (0.5 if o[3] == d0[3] == d1[3] == 2 else 1.0)))

    def rsum(o, i):
        add("V", lambda: g.vector.tensor_reduce(o[0], i[0], AxisListType.X, OP.add), [o], [i], vc(i, o))

    def ms(o, v):
        add("V", lambda: g.vector.memset(o[0], v), [o], [], vc(o, o))

    def act(o, i, f=AF.Identity, bias=0.0, scale=1.0):
        add("S", lambda: g.scalar.activation(o[0], i[0], f, bias=p(bias), scale=p(scale)), [o], [i, bias, scale],
            65 + 0.83 * GA * o[2] if i[4] else VF + 0.83 * max(64, o[2]))

    def sfill(o, v):
        act(o, c("T17", 0, o[2]), AF.Identity, v, 0.0)

    def mm(o, l, r, st, sp):
        add("P", lambda: g.tensor.matmul(o[0], l[0], r[0], st, sp), [o], [l, r],
            PEC * max(min(64, l[2]), o[2]) * (4 if l[3] == 4 else 1), wk="wr" if st or sp else "acc")

    def group(terms):
        for k, (o, l, r) in enumerate(terms):
            mm(o, l, r, k == 0, k == len(terms) - 1)

    def iota(o, pat, base, cm, fl=True):
        if fl:
            add("G", lambda: g.iota(o[0], pat, base, cm, allow_small_or_imprecise_dtypes=True), [o], [], 130 + 1.66 * o[2])
        else:
            add("G", lambda: g.iota(o[0], pat, base, cm), [o], [], 130 + 1.66 * o[2])

    def gcp(o, i):
        add("G", lambda: g.affine_select(o[0], i[0], [[0, o[2]]], OP.is_ge, 0.0, 0, 0), [o], [i], 170 + 1.66 * o[2])

    def dma(o, i, nbytes):
        k = "d%d" % cnts["d"]
        cnts["d"] += 1
        add("Y", lambda: g.sync.dma_start(p(o), p(i)).then_inc(T.sem[k], 16), [o] if isinstance(o, tuple) else [], [i], 60.0,
            (k, 16), 2000 + nbytes / 200.0)

    def send(dst, src, use, lat=RLAT):
        k = "d%d" % cnts["d"]
        r = "r%d" % cnts["r"]
        cnts["d"] += 1
        cnts["r"] += 1
        mask = sum(1 << e for e in use)
        t = 128 * src[2] * src[3] / (12.0 * len(use))
        add("G", lambda: g.remote_dma(dst[0], src[0], T.sem[r], T.sem[k], pid, rid, mask), [], [src], RCALL, (k, len(use)),
            lat - LAT - RCALL)
        add("R%d" % mask, None, [dst], [], t, (r, len(use)), 0.0, after=[len(ops) - 1])

    HOME, PART = c("X", 0, WIN), c("X", WIN, 2 * WIN)
    ID, IH, NH = c("ID"), c("IH"), c("NH")
    G8, CF8 = s("G8", 8), s("CF0", 8)
    P8 = sl(0, 8)

    H = NV // NP
    for k in range(NP):
        dma(c("X", OFF + k * H, OFF + k * H + H), T.pts[:, k * H:k * H + H], 256 * H)
    dma(c("WI"), T.way[:], 131072)
    dma(A("NT", sl(0, 256), parts=P8), T.cnt[:], 8192)
    dma(A("NT", sl(256, 512), parts=P8), T.th[:], 8192)
    dma(c("CH", OFF), T.cand[:], 512 * NV)
    for k in range(1, len(ops)):
        behind(k - 1, k)
    ops[-1]["lat"] += 3000.0
    iota(c("T17"), [[0, 16], [1, 17]], 0, 0)
    iota(c("T19"), [[0, 8], [1, 19]], 0, 0)
    iota(c("KM"), [[-1, 128]], 0, 1)
    iota(c("SI", 0, 2), [[0, 2]], 0, 1, False)
    iota(s("CF0", 32), [[1, 32]], 0, 0)
    iota(c("K16"), [[0, 8], [1, 16]], 0, 0)
    iota(c("V1"), [[-16, 8], [-1, 17]], 0, 1)
    iota(c("V2"), [[-16, 8], [1000, 2], [-2, 8]], 0, 1)
    iota(c("H4"), [[0, 16], [1, 4]], 0, 0)
    for k in range(NP):
        send(c("X", WIN + OFF + k * H, WIN + OFF + k * H + H), c("X", OFF + k * H, OFF + k * H + H), engs)
    gcp(c("CS"), c("CH", OFF))
    send(c("CR"), c("CS"), engs[len(engs) // 2:], 2 * REARLY)
    ops[-1]["after"].append(len(ops) - 4)
    iota(c("GI"), [[0, 2], [1, 8], [0, 4]], 0, 0)
    iota(c("TRF"), [[128, 2], [0, 2], [16, 8]], TRASH, 0)
    iota(c("IOT", 0, 296), [[1, 296]], 0, 0)
    iota(c("SCN"), [[1, 6], [0, 8]], 0, 0)
    iota(c("SEF"), [[-8, 5], [-1, 8], [0, 16]], 0, 1)

    for k in range(296, TRASH, 296):
        act(c("IOT", k, k + 296), c("IOT", 0, 296), AF.Identity, float(k))
    ts(c("SEL"), c("SEF"), 0.0, OP.is_equal, 4096.0, OP.mult)
    PI = c("SI", 0, 1)
    for k, (a, b) in enumerate(((0, 15), (4, 7), (2, 3), (0, 3), (0, 7), (0, 1))):
        ts(c("SI", 2 + k, 3 + k), PI, a, OP.logical_shift_right, b, OP.bitwise_and)
    cp(c("SM", SL["col"], SL["col"] + 6), c("SI", 2, 8))
    cp(col("P"), PI)
    act(col("ODD"), col("EVN"), AF.Identity, 0.0, float(WIN))
    act(col("C17"), col("PM4"), AF.Identity, 16.0, 17.0)
    act(col("C16"), col("PM4"), AF.Identity, 15.0, 16.0)
    act(col("C19"), col("PM4"), AF.Identity, 17.0, 19.0)
    for hf in range(2):
        act(col("T%d" % hf), col("P"), AF.Identity, -TRASH - 128.0 * hf, -1.0)
    ts(c("WH"), c("WI"), float(OFF), OP.add)
    for e in range(2):
        for b in range(2):
            ts(hc("PK", 2 * e + b), c("V2"), e + 1000.0 * b, OP.is_equal)
        group([(hc("pE0", e), hc("PK", 2 * e + b), c("WH", b, 256, 2)) for b in range(2)])
    cp(c("PH"), c("pE0", 0, 256))
    cp(A("NF", ALL, parts=P8), A("NT", ALL, parts=P8))
    ts(c("IF"), c("KM"), 0.0, OP.is_equal)
    for name, v in (("ID", 1.0), ("NI", -1.0), ("BI", B17), ("CI", 65536.0), ("VI", -4096.0), ("MI", 192.0), ("UI", 2 * U18), ("TWO", 2.0)):
        act(c(name), c("IF"), AF.Identity, 0.0, v)
    cp(IH, c("IF"))
    ts(NH, c("IF"), -1.0, OP.mult)
    ts(G8, CF8, col("GRP"), OP.is_equal)
    for k, v in enumerate((16.0, 16.0 * U18, -16.0 * U18, -16.0 * U18)):
        act(hc("W16", k, 8), G8, AF.Identity, 0.0, v)
    sfill(c("X", 0, OFF), BIGH)
    sfill(c("X", WIN, WIN + OFF), BIGP)
    sfill(c("X", TRASH, WIN), 0.0)
    sfill(c("X", WIN + TRASH), 0.0)
    ms(c("CH", 0, OFF), -OFF)
    ms(c("CP", 0, OFF), -float(OFF))
    sfill(c("VE", 512, 8 * 520, 520), 0.0)
    sfill(c("KB", 272, 528), 129.0)
    for k in range(2):
        act(c("KB", 528 + 152 * k, 680 + 152 * k), c("T19"), AF.Identity, 0.0, U18)
    for k in range(14, 19):
        sfill(c("KB", 528 + k, 680, 19), 1.0)
        sfill(c("KB", 680 + k, 832, 19), (k - 14) * U18 if k < 18 else 1.0)
    sfill(c("RSTB"), -0.5)
    sfill(c("RSTB", 0, 136, 17), 1.0e9)
    for k in range(2):
        ts(hc("RS2", k), c("K16"), 0.0, OP.is_equal, 1.0e9, OP.mult)
    act(c("RSM"), c("K16"), AF.Sign)
    ms(c("RST1"), 1.0)
    sfill(c("RST1", 1, 152, 19), -1.0)
    sfill(c("RST1", 0, 304, 19), 0.0)
    act(c("K2", 0, 128), c("K16"), AF.Identity, 0.5)
    act(c("K2", 128, 256, 2), c("K16", 0, 128, 2), AF.Identity, 1.0, 0.5)
    act(c("K2", 129, 256, 2), c("K16", 1, 128, 2), AF.Identity, 1.5, 0.5)
    sfill(c("K2", 0, 128, 16), -0.5)
    for name, v in (("NEG", BIGP), ("BIG", BIGH), ("ONES", 1.0), ("HALF", -0.5), ("TOPF", 255.0)):
        sfill(c(name), v)
    ms(c("ZERO"), 0.0)
    ts(c("TA"), c("V1"), -1.0, OP.is_equal)
    ts(c("TB"), c("V1"), 0.0, OP.is_equal)
    sfill(c("TA", 0, 136, 17), 0.0)
    sfill(c("TB", 16, 136, 17), 0.0)
    cp(c("DM", 0, 136), c("TA"))
    ts(c("DM", 0, 136, 17), c("TB", 0, 136, 17), -1.0 / 4096.0, OP.mult)
    tt(c("DM", 136, 272), c("TA"), c("TB"), OP.subtract)
    ts(c("ZM"), c("H4"), col("PM4"), OP.is_equal)
    act(c("ZN"), c("ZM"), AF.Identity, -1.0)
    ts(s("P4", 4), s("CF0", 4), col("P3"), OP.is_equal)
    for k in range(4):
        ts(hc("R4", k, 8), G8, c("SM", SL["P4"] + k, SL["P4"] + k + 1), OP.mult)
    ts(c("LZ"), s("CF0", 2), 68.0, OP.mult, col("C17"), OP.add)
    ts(c("LE"), s("CF0", 2), 64.0, OP.mult, col("C16"), OP.add)
    ts(c("LA"), s("CF0", 4), 76.0, OP.mult, col("C19"), OP.add)
    for k in range(2):
        cp(hc("LR", k, 2), c("LA", 0, 2))
        ts(hc("L8", k, 2), s("CF0", 2), 4.0, OP.mult, col("PM4"), OP.add)
    ts(c("LG", 0, 1), col("P7"), 17.0, OP.mult, 16.0, OP.add)
    act(col("P7"), col("P7"), AF.Identity, 18.0, 19.0)
    ts(c("REP"), s("CF0", 4), 0.0, OP.mult, col("P7"), OP.add)
    act(col("EVN"), col("EVN"), AF.Identity, 152.0, -136.0)
    ts(c("APL"), CF8, 17.0, OP.mult, col("EVN"), OP.add)
    for hf in range(2):
        h = str(hf)
        ms(c("P" + h, 128), 0.0)
        ms(c("U2" + h, 0, 2), 0.0)
        for z in ("Z", "ZL", "ZE"):
            ms(c(z + h), 0.0)
        sfill(c("INV" + h, 128), 1.0)
        sfill(c("RI" + h, 0, 171), 0.5)
        sfill(c("RI" + h, 171, 336), -0.5)
        sfill(c("RI" + h, 336, 464), 0.5)
        sfill(c("RI" + h, 171, 323, 19), 0.0)
        sfill(c("RI" + h, 18, 322, 19), 0.0)
    sfill(c("TA", 0, 128), 1.0 / 3.0)
    scan(c("RR"), c("TA", 0, 128), c("ZERO", 0, 128), OP.mult, OP.add, 3.0 ** 61)
    tt(c("TB", 0, 128), c("RR"), c("IF"), OP.mult)
    rsum(col("THR"), c("TB", 0, 128))
    act(col("THR"), col("THR"), AF.Identity, 0.0, 4.0)
    ts(s("E16"), s("CF0"), col("PM"), OP.is_equal, 3.0 ** 16, OP.mult)
    tt(s("R16"), s("E16"), c("RR", 0, 16), OP.mult)
    rsum(col("WC"), s("R16"))
    sfill(s("E16", 8), 3.0 ** -16)
    scan(s("W8", 8), s("E16", 8), c("ZERO", 0, 8), OP.mult, OP.add, col("WC"))
    ts(c("G64"), c("GI"), col("GRP"), OP.is_equal)
    for lh in range(8):
        act(hc("GW", lh, 64), c("G64"), AF.Identity, 0.0, c("SM", SL["W8"] + lh, SL["W8"] + lh + 1))
    act(hc("GW", 8, 64), c("G64"), AF.Identity, 0.0, FAR)
    ts(c("TRA"), c("TRF"), col("PM"), OP.add)

    def bank():
        cnts["bank"] += 1
        return "pD%d" % (cnts["bank"] % 4)

    def path(hf, lo=0):
        return c("P%d" % hf, lo, lo + 128)

    def spread(z, n, win, lst, mask):
        tt(c(z, 3, 128 * n, 4), ind(win, c(lst, 0, 2 * n)), mask, OP.mult)

    def turn(outs, z, more=()):
        group([(o, c(z, 128 * e + 3 - k, 128 * e + 131 - k), hc("R4", k, 8)) for e, o in enumerate(outs) for k in range(4)] + list(more))

    def to_list(hf, win, lst, t, o, z):
        at(t)
        spread(z, 1, win, lst, c("ZM", 0, 32))
        at(t + 330)
        turn([o], z)
        at(t + 680)
        cp(hc("LST", hf, 8), o)

    def new_path(hf, d, terms, t, more):
        h = str(hf)
        scan(c("RO" + h, 336), c("RSM"), c("RI" + h, 336), OP.mult, OP.add)
        ts(c("INV" + h, 0, 128), c("RO" + h, 336), 0.75, OP.is_gt)
        group(terms + [(A(d, P8), c("VI"), c("INV" + h, 0, 128))])
        if S16:
            act(path(hf), A(d, P8), AF.Relu)
        else:
            ts(path(hf), A(d, P8), 0.0, OP.max)
        scan(hc("UE", hf), c("INV" + h, 0, 128), path(hf), OP.mult, OP.add)
        to_list(hf, hc("UE", hf), "LE", t, A(d, 16, P8), "ZE" + h)
        for k in range(2):
            act(hc("CAP", 2 * hf + k, 8), hs("N2", hf), AF.Sign, 6.5 - k, -1.0)
        for k in range(4):
            act(A("PO" + h, ALL, sl(6 * k, 6 * k + 8)), c("P" + h, 1, 128, 2))
        for k in range(4):
            act(A("PEV" + h, ALL, sl(7 * k, 7 * k + 8)), c("P" + h, 0, 128, 2))
        if more:
            at(t + 1500)
            mm(A(d, sl(8, 16)), path(hf), IH, True, True)
            ts(hc("PU", hf), A(d, sl(8, 16)), col("ODD"), OP.add)
        at(t + 9000)
        act(c("MK" + h), c("RO" + h, 336), AF.Abs, -1.25)
        act(c("MK" + h), c("MK" + h), AF.Relu, 1.5, -2.0)

    def ramps(hf, t):
        h = str(hf)
        at(t)
        scan(c("RO" + h, 18, 323), c("RST1"), c("RI" + h, 18, 323), OP.mult, OP.add)
        at(t + 370)
        ts(hc("RSD", hf, 152), c("RO" + h, 171, 323), 0.0, OP.is_equal, 1.0e9, OP.mult)

    def edge_ends(hf):
        pe, P = "pE%d" % hf, "P%d" % hf
        terms = [(c(pe, 152, 456), ID, c("ZERO"))]
        for k in range(14):
            o = c(pe, 152 * (1 + k % 2) + k, 152 * (2 + k % 2), 19)
            terms.append((o, IH, c(P, k, 128, 16)))
            if k < 13:
                terms.append((o, NH, c(P, k + 2, 128, 16)))
        terms.append((c(pe, 152 + 13, 304, 19), IH, c(P, 14, 128, 16)))
        group(terms)
        act(c("DT%d" % hf), c(pe, 152, 456))

    def first_path(hf):
        h = str(hf)
        pz = "pZ" + h
        group([(c(pz, NN + 8 * k, NN + 8 * k + 8), A("NF", sl(256 * k + 128 * hf, 256 * k + 128 * hf + 128), parts=P8),
                A("IF", P8, parts=P8)) for k in range(2)])
        act(hs("N2", hf), c(pz, NN, NN + 8), AF.Identity, -0.5, 0.5)
        act(hs("th", hf), c(pz, NN + 8, NN + 16), AF.Identity, 0.0, 16.0 * U18)
        act(hs("bnd", hf), hs("th", hf))
        act(c("RI" + h, 336, 464, 16), hs("N2", hf), AF.Identity, 0.5, -1.0)
        act(c("RI" + h, 19, 171, 19), hs("N2", hf), AF.Identity, 0.5, -1.0)
        ramps(hf, 0.0)
        d = bank()
        new_path(hf, d, [(A(d, P8), hc("WH", hf), IH)], 0.0, True)
        edge_ends(hf)

    def uf_end(hf, slot):
        return c("UF%d" % hf, 136 * slot + 16, 136 * slot + 136, 17)

    def run_end(hf):
        return c("RUN", 152 * hf + 16, 152 * hf + 136, 17)

    def append_one(hf, k):
        h = str(hf)
        tt(c("U2" + h, 2) if k else c("U1" + h), ind(hc("UF" + h, k, 272), c("APL")), c("MK" + h), OP.mult)

    def went(hf, k):
        act(hc("GO", 2 * hf + k, 8), uf_end(hf, 2 * k + 1), AF.Sign)

    def parts_of(hf):
        h = str(hf)
        return (path(hf), c("U1" + h), c("U2" + h, 0, 128))

    def append(hf):
        o = c("pZ%d" % hf, 272, 400)
        at(1200)
        append_one(hf, 1)
        group([(o, IH, x) for x in parts_of(hf)])
        (act if S16 else cp)(path(hf), o)

    def gather(who, buf, kk, win, lst, t):
        cuts = PIECES if who == "v" else (0, 32)
        for n, (a, b) in enumerate(zip(cuts, cuts[1:])):
            at(t + GAP * n)
            o, src = c(buf, 520 * kk + 16 * a, 520 * kk + 16 * b), ind(win, c(lst, 32 * kk + a, 32 * kk + b))
            if who == "S":
                act(o, src, AF.Copy)
            else:
                cp(o, src)

    def sums(buf, hf, outs, w):
        return [(o, c(buf, 2048 * hf + i, 2048 * hf + 2048, 16), w) for i, o in enumerate(outs)]

    def edge_chunk(hf, k, who, t0, t1):
        kk = 4 * hf + k
        if len(who) == 1:
            gather(who, "VE", kk, c("X"), "PU", t0)
        for e in range(2 if len(who) == 2 else 0):
            at(t0 - 9000 * (1 - e))
            (act if who[e] == "S" else cp)(c("VE", 520 * kk + e, 520 * kk + 512, 2), ind((HOME, PART)[e], hc("PH", 8 * e + kk, 16)))
        d = A(bank())
        at(t1 - 700)
        group([(d, ID, c("VE", 520 * kk, 520 * kk + 512)), (d, c("NI"), c("VE", 520 * kk + 1, 520 * kk + 513))])
        at(t1)
        act(hc("A1", kk, 512), d, AF.Abs)

    def edge_keys(hf, r, t):
        pe = "pE%d" % hf
        at(t)
        terms = [(c(pe, 0, 152), ID, c("KB", 680, 832) if r else c("KB", 528, 680))]
        terms += sums("A1", hf, [c(pe, i, 152, 19) for i in range(14)], hc("W16", 1, 8))
        if r:
            terms.append((c(pe, 14, 152, 19), ID, hc("ED", hf, 8)))
            for k in range(4):
                terms.append((c(pe, 14 + k, 152, 19), c("UI"), hc("NB", hf, 8)))
                terms.append((c(pe, 14 + k, 152, 19), c("IF"), hc("DK", 4 * hf + k, 8)))
            act(c("DT%d" % hf, 17, 152, 19), uf_end(hf, 3))
            tt(c("DT%d" % hf, 16, 152, 19), uf_end(hf, 1), uf_end(hf, 3), OP.subtract)
        group(terms)

    def bounds(hf):
        tt(hc("BM", hf, 64), ind(hs("bnd", hf), c("L8")), c("ZN"), OP.add)

    def first_dead(hf):
        h = str(hf)
        pe = "pE" + h
        at(-700)
        terms = [(c(pe, 136, 392), ID, c("KB", 272, 528)), (c(pe, 136, 264), ID, c("HALF"))]
        terms += [(c(pe, 136 + 128 * e, 264 + 128 * e), c("MI"), c("INV" + h, k, k + 128)) for e in range(2) for k in range(2)]
        group(terms + sums("A1", hf, [c(pe, 136 + i, 392, 16) for i in range(14)], c("W16", 16, 32)))
        at(700)
        tt(c("M" + h), c(pe, 136, 392), c("K2"), OP.max)
        dt = [[c("DT" + h, 152 * e + k, 152 * e + 152, 19) for k in range(19)] for e in range(2)]
        last = c("UE", 128 * hf + 15, 128 * hf + 128, 16)
        for o, a, b in ((dt[0][13], dt[0][13], last), (dt[0][14], last, uf_end(hf, 1)),
                        (dt[1][13], dt[1][13], uf_end(hf, 0)), (dt[1][15], uf_end(hf, 0), uf_end(hf, 2))):
            tt(o, a, b, OP.subtract)
        act(dt[1][17], uf_end(hf, 2))
        at(T_PATH + 500)
        scan(hc("MX", hf, 256), c("RS2"), c("M" + h), OP.add, OP.min)
        bounds(hf)
        tt(hs("N3b", hf), hs("N2", hf), hc("GO", 2 * hf, 8), OP.add)
        for v in range(2):
            w = sl(8 * v, 8 * v + 8)
            act(A("TOP" + h, 0, w), hs("N3b", hf), AF.Identity, 0.5 + 2 * v, 2.0)
            act(A("TOP" + h, 1, w), hs("N3b", hf), AF.Identity, 1.0 + v)
            act(hs("N3" + h, v), hs("N3b", hf), AF.Identity, v - 0.5)
            tt(A("JH" + h, ALL, w), c("MX", 256 * hf + 15, 256 * hf + 256, 16), A("TOP" + h, ALL, w), OP.min)
        tt(s("mx" + h), A("JH" + h, 0), s("N3" + h), OP.max)
        tt(s("bk" + h), s("N3" + h), A("JH" + h, 0), OP.is_gt)
        tt(A("QS" + h, 0), A("JH" + h, 1), s("mx" + h), OP.subtract)
        tt(A("QS" + h, 1), A("JH" + h, 1), s("bk" + h), OP.mult)
        tt(s("dq" + h), A("QS" + h, ALL, sl(8, 16)), A("QS" + h, ALL, P8), OP.subtract)
        act(hc("NB", hf, 8), hs("N2", hf))
        act(c("RI" + h, 19 + 14, 171, 19), hs("N2", hf), AF.Identity, -6.5)
        act(c("RI" + h, 171 + 14, 323, 19), hs("N2", hf), AF.Identity, 6.5, -1.0)

    def cut(hf):
        h = str(hf)
        at(-1600)
        ts(s("go" + h), ind(c("RUN", 152 * hf, 152 * hf + 136), c("LG", 0, 1)), 65500.0, OP.is_lt)
        at(-1250)
        tt(s("gd" + h), s("go" + h), s("dq" + h), OP.mult)
        at(-900)
        tt(c("RI" + h, 19, 171, 19), hs("gd" + h, 0), A("QS" + h, 0, P8), OP.add)
        for k in range(2):
            tt(c("RI" + h, 18 + 152 * k, 170 + 152 * k, 19), hs("gd" + h, 1), A("QS" + h, 1, P8), OP.add)
        ramps(hf, -500)

    def pick(hf, outs, n, t, rst, beside=None):
        e = c("pE%d" % hf, 0, n)
        run, ne = c("RUN", 152 * hf, 152 * hf + n), c("NE1", 152 * hf, 152 * hf + n)
        at(t)
        scan(run, rst, e, OP.add, OP.min)
        at(t + 350)
        tt(ne, e, run, OP.not_equal)
        if beside:
            beside(run)
        at(t + 700)
        for o, d in outs:
            scan(o, ne, d, OP.mult, OP.add)

    def least(hf, r):
        h = str(hf)
        e = c("pE" + h, 0, 152)
        t = -100 if r else 4450
        at(t)
        tt(e, e, c("RO" + h, 19, 171), OP.max)
        pick(hf, [(hc("UAB" + h, k, 152), hc("DT" + h, k, 152)) for k in range(2)], 152, t + 370, hc("RSD", hf, 152),
             lambda run: tt(hc("PR", hf, 64), ind(run, c("LR")), hc("BM", hf, 64), OP.is_lt))
        return t + 1500

    def shift(hf, t, more):
        h = str(hf)
        q = c("RI" + h, 19, 171, 19)
        p40 = sl(0, 40)
        at(t)
        act(hs("N2", hf), q, AF.Relu, 0.5, -1.0)
        act(c("RI" + h, 336, 464, 16), hs("N2", hf), AF.Identity, 0.5, -1.0)
        act(hs("none", hf), q, AF.Relu, -0.5)
        ts(hs("dm", hf), c("P" + h, 0, 128, 16), float(TRASH - 97), OP.is_ge, -float(NV), OP.mult)
        act(hs("dm2", hf), hs("dm", hf), AF.Identity, 97.0)
        tt(hc("DL", hf, 8), hs("dm2", hf), hs("none", hf), OP.mult)
        tt(hc("OH", hf, 48), ind(c("RI" + h), c("REP", 0, 3)), c("SCN"), OP.is_equal)
        d = bank()
        hot = A("OT", sl(128 * hf, 128 * hf + 128), parts=p40)
        mm(A(d, P8, parts=p40), c("OH", 48 * hf, 48 * hf + 40), ID, True, True)
        act(hot, A(d, P8, parts=p40))
        for ks in ((0, 1, 2, 3), (4,)):
            d = bank()
            terms = []
            for n, k in enumerate(ks):
                o = A(d, sl(8 * n, 8 * n + 8))
                terms += [(o, IH, path(hf, 2 * k)), (o, hot, A("SEL", sl(128 * k, 128 * k + 128), parts=p40))]
            group(terms)
            act(c("YS" + h, 128 * ks[0], 128 * ks[-1] + 128), A(d, sl(0, 8 * len(ks))), AF.Relu, -4096.0)
        d = bank()
        terms = [(A(d, P8), IH if S16 else c("IF"), hc("YS" + h, k)) for k in range(5)]
        new_path(hf, d, terms + [(A(d, P8, 0), IH, hc("DL", hf, 8))], t + 2200, more)

    def propose(hf, r, t):
        h = str(hf)
        pz, pe = "pZ" + h, "pE" + h
        ab = hc("ABU", hf, 16)
        both = c(pz, LI, LI + 16)
        ends = [c(pz, LI + 8 * e, LI + 8 * e + 8) for e in range(2)]
        at(t)
        spread("Z" + h, 2, c("UAB" + h), "LA", hc("PR", hf, 64))
        at(t + 370)
        turn(ends, "Z" + h)
        at(t + 830)
        cp(ab, both)
        at(t + 1120)
        act(s("AS" + h), both, AF.Identity, 0.0, -1.0)
        cp(hc("ROW", 2 * hf), ind(c("IOT"), hc("ABU", 2 * hf, 8)))
        act(hc("ROW", 2 * hf + 1), ind(c("IOT"), hc("ABU", 2 * hf + 1, 8)))
        act(A("MID%d" % r, hf, sl(128, 144)), s("AS" + h), AF.Identity, 0.0, -1.0)
        act(hc("XA", hf), ind(HOME, hc("ABU", 2 * hf, 8)), AF.Relu, 255.0, -1.0)
        act(hc("XS", hf), ind(PART, hc("ABU", 2 * hf + 1, 8)), AF.Relu)
        d = c(pz, 0, 128)
        group([(d, ID, c("HALF")), (d, ID, c("TOPF")), (d, c("NI"), hc("XA", hf)), (d, ID, hc("XS", hf))])
        act(hc("XR", hf), d, AF.Identity, MAGIC, 0.5)
        act(A("MID%d" % r, hf, sl(0, 128)), hc("XR", hf), AF.Identity, -MAGIC)
        send(A("RM%d" % r, hf), A("MID%d" % r, hf), low, REARLY)
        at(t + 200)
        act(hc("DAB", hf, 64), ind(c("UAB" + h), c("LA")), AF.Identity, col("T" + h))
        act(hc("TP", hf, 64), hc("PR", hf, 64), AF.Identity, 0.0, col("THR"))
        at(t + 1700)
        todo = [(e, c("SM", SL["AS%d" % sh] + 8 * e + lh, SL["AS%d" % sh] + 8 * e + lh + 1), lh if sh == hf else 8)
                for sh in range(hf + 1) for lh in range(8) for e in range(2)]
        votes = c(pe, 0, 64)
        for k, (e, val, w) in enumerate(todo):
            eq = hc("EQ", 16 * hf + k)
            if hf and len(todo) - k <= 2 * EQ_S and e:
                gap = hc("AB", (len(todo) - k) // 2)
                act(gap, hc("ROW", 2 * hf + e), AF.Abs, val)
                act(eq, gap, AF.Relu, 1.0, -1.0)
            else:
                ts(eq, hc("ROW", 2 * hf + e), val, OP.add, 0.0, OP.is_equal)
            mm(votes, eq, hc("GW", w, 64), k == 0, k == len(todo) - 1)
        tt(hc("WM", hf, 64), votes, hc("TP", hf, 64), OP.is_lt)
        tt(c("ZL" + h, 3, 256, 4), hc("DAB", hf, 64), hc("WM", hf, 64), OP.mult)
        turn(ends, "ZL" + h, [(both, IH, hc("TRA", hf, 16))])
        cp(A("LS%d" % r, hf), both)
        cnts["list"] = len(ops) - 1
        send(A("RL%d" % r, hf), A("LS%d" % r, hf), low, RLAT if hf else REARLY)
        if hf and not r:
            sent = len(ops) - 2
            for k in range(2):
                gcp(c("CP", OFF + 880 * k, OFF + 880 * k + 880), hc("CR", k, 880))
                behind(sent)
        cp(A("LU%d" % r, ALL, sl(8 * hf, 8 * hf + 8)), both)

    def apply_merges(r):
        at(T_OWN)
        scat(PART, A("RL%d" % r, 0, P8), A("RM%d" % r, 0, sl(0, 128)))
        behind(cnts["list"])
        scat(PART, A("LU%d" % r, 1), c("NEG"))
        for hf in range(2):
            scat(HOME, A("LU%d" % r, 0, sl(8 * hf, 8 * hf + 8)), A("MID%d" % r, hf, sl(0, 128)))
        cp(c("RA"), A("RM%d" % r, 1, sl(128, 136)))
        act(c("KF"), ind(PART, c("RA")), AF.Relu, 0.0, -1.0)
        tt(c("MV"), A("RM%d" % r, 1, sl(0, 128)), c("KF"), OP.subtract)
        scat(HOME, A("RL%d" % r, 0, sl(8, 16)), c("BIG"))
        at(T_OWN + 2500)
        scat(PART, A("RL%d" % r, 1, P8), c("MV"))
        scat(HOME, A("RL%d" % r, 1, sl(8, 16)), c("BIG"))

    def count():
        a = c("pZ1", NN + 16, NN + 32)
        group([(a, c("ONES"), c("WM", k, k + 16)) for k in (0, 16, 64, 80)])
        rsum(col("ACT"), a)
        cp(c("SI", 8, 9), col("ACT"))
        ts(c("SI", 9, 10), c("SI", 8, 9), 31, OP.bitwise_and)
        ts(col("A8"), c("SI", 9, 10), 128.0 * U18, OP.mult)
        act(s("bnd"), s("th"), AF.Identity, col("A8"))

    def hop(slot, hf, beside, last):
        h = str(hf)
        first = slot % 2 == 0
        tab, mine, other = (c("CH"), HOME, PART) if first else (c("CP"), PART, HOME)
        lst = hc("LST", hf, 8)
        pz, pe = "pZ" + h, "pE" + h
        ends = c("Y2", 256 * hf, 256 * hf + 256, 2)
        by_s = Y2_ON[slot][hf] == "S"
        at(240)
        ts(hc("CU", hf), ind(tab, lst), float(OFF), OP.add)
        if by_s:
            act(ends, ind(mine, lst), AF.Relu, 255.0, -1.0)
        else:
            ts(ends, ind(mine, lst), 255.0, OP.subtract, 0.0, OP.min)
        at(670)
        gcp(hc("CF", hf), hc("CU", hf))
        at(T_DUP)
        cp(c("Y2", 256 * hf + 1, 256 * hf + 256, 2), ends)
        if slot == 0 and not last:
            at(-2000)
            edge_ends(hf)
        if slot == 3 and not last:
            first_dead(hf)
        at(900)
        mm(c(pz, 0, 272), hc("CF", hf), c("DM"), True, True)
        at(T_PATH + 400)
        for f in beside:
            f()
        if slot == 0 and not last:
            o = c(pz, NN, NN + 8)
            mm(o, ends, hc("W16", 0, 8), True, True)
            act(hc("ED", hf, 8), o, AF.Relu, 1.0, -1.0 if by_s else 1.0)
        for k in range(4):
            kk = 4 * hf + k
            gather((PLAN_END if last else PLAN_HOP)[slot][hf][k], "VG", kk, other, "CU", T_GATHER[k])
            d = bank()
            at(T_ABS[k] - 900)
            for t in range(8):
                mm(A(d, ALL, sl(2 * t, 2 * t + 2)), ID if by_s else c("NI"), hc("Y2", kk, 64), t == 0, False)
            at(T_ABS[k] - 460)
            mm(A(d), ID, c("VG", 520 * kk, 520 * kk + 512), False, True)
            at(T_ABS[k])
            act(hc("A2", kk, 512), A(d), AF.Abs, -255.0)
        for j in range(6 if first else 7):
            o = hc("EQH", 2 * j + hf, 136)
            at(T_PATH + j)
            tt(o, c(pz, 0, 136), A(("PO" if first else "PEV") + h, ALL, sl(j, j + 17)), OP.is_equal)
            at(T_PATH + 1200 + j)
            mm(c(pe, 0, 136), c("BI"), o, j == 0, False)
        mm(c(pe, 0, 136, 17), c("CI"), hc("CAP", 2 * hf + slot // 2, 8) if first else c("ONES", 0, 8), False, False)
        at(T_ABS[3] + 660)
        for i, (o, l, w) in enumerate(sums("A2", hf, [c(pe, 1 + i, 136, 17) for i in range(16)], hc("W16", 0, 8))):
            mm(o, l, w, False, i == 15)
        if not last:
            for n, k in enumerate([k for k in range(4) if OLD_AT[hf][k] == slot]):
                edge_chunk(hf, k, PLAN_OLD[hf][k], T_OLD[0] + 700 * n, T_OLD[1] + 430 * n)
        pick(hf, [(hc("UF" + h, slot, 136), c(pz, 136, 272))], 136, T_PICK, c("RSTB"),
             (lambda run: last_gate(hf)) if last and slot == 3 else None)
        if not last:
            at(T_PICK + 360)
            act(hs("yd", hf), run_end(hf), AF.Identity, MAGIC, 1.0 / 16.0)
            act(hc("DK", 4 * hf + slot, 8), hs("yd", hf), AF.Identity, -MAGIC * 16.0 * U18, 16.0 * U18)
        if slot < 3:
            to_list(hf, hc("UF" + h, slot, 136), "LZ", T_PICK + 1050, c(pz, LI, LI + 8), "Z" + h)

    def last_gate(hf):
        ts(hc("GO", 2 * hf + 1, 8), run_end(hf), 65500.0, OP.is_lt)
        tt(uf_end(hf, 2), uf_end(hf, 2), hc("GO", 2 * hf + 1, 8), OP.mult)

    def bar(hf, slot):
        name, n = (("PO", 6), ("PEV", 7))[slot]
        for t in range(3):
            gcp(A(name + str(hf), ALL, n * t + n - 1), uf_end(hf, slot))

    def points_out():
        ts(c("XO"), c("X", OFF, TRASH), 255.0, OP.min)
        dma(T.yx[:], c("XO"), 256 * NV)

    def result(hf):
        h = str(hf)
        o = c("pZ" + h, 0, 128)
        append_one(hf, 1)
        group([(o, x, IH) for x in parts_of(hf)])
        act(hc("WL", hf), o, AF.Relu, -float(OFF))
        dma(T.yw[:, 128 * hf:128 * hf + 128], hc("WL", hf), 65536)
        act(hc("NB", hf, 8), hs("N2", hf), AF.Identity, 0.5)
        o = A("pE" + h, sl(0, 128), parts=P8)
        group([(o, x, c("TWO")) for x in (hc("NB", hf, 8), hc("GO", 2 * hf, 8), hc("GO", 2 * hf + 1, 8))])
        act(A("WN", sl(128 * hf, 128 * hf + 128), parts=P8), o)
        if hf:
            dma(T.yn[:], A("WN", ALL, parts=P8), 8192)

    def after_pair(hf, last):
        went(hf, 0)
        if last:
            tt(uf_end(hf, 0), uf_end(hf, 0), hc("GO", 2 * hf, 8), OP.mult)
        append_one(hf, 0)

    first_path(0)
    first_path(1)
    cnts["main"] = True
    for r in range(ROUNDS):
        last = r + 1 == ROUNDS
        base = 100000.0 * r
        for hf in range(2):
            cnts["base"] = base + HALF * hf
            if r:
                cut(hf)
                edge_keys(hf, r, -1200)
                append(hf)
            else:
                for k in range(4):
                    edge_chunk(hf, k, PLAN_EDGE[hf][k], T_GATHER[k] - 400, T_ABS[k] - 400)
                bounds(hf)
                edge_keys(hf, r, 3500)
        for hf in range(2):
            cnts["base"] = base + HALF * hf
            t = least(hf, r)
            if r:
                shift(hf, T_SHIFT, not last)
            propose(hf, r, t)
        cnts["base"] = base - (5600 if r else 0)
        apply_merges(r)
        for slot in range(4):
            for hf in range(2):
                cnts["base"] = base + 100000.0 - 2 * HALF * (4 - slot) + HALF * hf
                beside = []
                if slot in (1, 2):
                    beside.append(lambda: bar(hf, slot - 1))
                if slot == 2:
                    beside.append(lambda: after_pair(hf, last))
                if slot == (2 if last else 1) and hf:
                    beside.append(points_out if last else count)
                hop(slot, hf, beside, last)
    for hf in range(2):
        cnts["base"] = 100000.0 * ROUNDS + HALF * hf
        at(-900)
        result(hf)

    if "plan" not in PLAN:
        PLAN["plan"] = order_calls(ops)
    order, waits, sig = PLAN["plan"]
    count_of = {}
    total = {}
    for i in order:
        o = ops[i]
        if o["sem"]:
            count_of[i] = total[o["sem"][0]] = o["sem"][1]
        elif i in sig:
            k = ESEM[o["q"]]
            total[k] = total.get(k, 0) + 1
            count_of[i] = total[k]
    Q = {"V": g.vector, "S": g.scalar, "P": g.tensor, "G": g, "Y": g.sync}
    waited = {}
    for i in order:
        o = ops[i]
        if o["q"][0] == "R":
            continue
        for (key, j) in waits[i]:
            Q[o["q"]].wait_ge(T.sem[key], count_of[j])
            waited[key] = max(waited.get(key, 0), count_of[j])
        ins = o["fn"]()
        if i in sig and not o["sem"]:
            ins.then_inc(T.sem[ESEM[o["q"]]], 1)
    for key in sorted(total):
        if waited.get(key, 0) < total[key]:
            g.wait_ge(T.sem[key], total[key])
